import numpy as np
import ml_dtypes


def mxq(x, axis, fmt="e4m3"):
    dtype, down = {"e4m3": (ml_dtypes.float8_e4m3fn, 7), "e5m2": (ml_dtypes.float8_e5m2, 14)}[fmt]
    v = np.moveaxis(np.asarray(x, np.float32).astype(ml_dtypes.bfloat16).astype(np.float64), axis, -1)
    blocks = v.reshape(v.shape[:-1] + (-1, 32))
    amax = np.abs(blocks).max(-1, keepdims=True)
    byte = np.maximum(np.where(amax > 0, np.frexp(amax)[1] - 1 + 127, 0) - down, 1)
    scale = np.exp2(byte - 127.0)
    codes = (blocks / scale).astype(np.float32).astype(dtype).astype(np.float64)
    return np.moveaxis((codes * scale).reshape(v.shape), -1, axis)


WIDE = False


def mx_kscale(k):
    if not WIDE:
        return np.ones(k)
    levels = np.array([10, -10, 5, -5, 0])
    if k % 512:
        return np.exp2(np.random.permutation(np.resize(levels, k // 32))).repeat(32)
    a = np.empty((k // 512, 16))
    for p in range(k // 512):
        a[p, :8] = np.random.permutation(np.resize(levels, 8))
        for g in range(8):
            far = levels[np.abs(levels - a[p, g]) >= 10]
            a[p, g + 8] = far[np.random.randint(len(far))]
    return np.exp2(a.ravel()).repeat(32)


BF16 = ml_dtypes.bfloat16


def bf(x):
    return np.asarray(x, np.float32).astype(BF16)


def f64(x):
    return np.asarray(x).astype(np.float64)


E2M1 = np.array([0.0, 0.5, 1.0, 1.5, 2.0, 3.0, 4.0, 6.0, -0.0, -0.5, -1.0, -1.5, -2.0, -3.0, -4.0, -6.0])


def pack_weight(w, fmt):
    k, n = w.shape
    w = f64(bf(w)).reshape(k // 32, 32, n)
    amax = np.abs(w).max(1)
    if fmt == "e4m3":
        byte = np.frexp(amax)[1] - 1 + 127 - 7
    else:
        mant, ex = np.frexp(amax / 6.0)
        byte = np.where(mant > 0.5, ex, ex - 1) + 127
    byte = np.clip(np.where(amax > 0, byte, 1), 1, 254)
    scaled = (w * np.exp2(127.0 - byte)[:, None, :]).reshape(k, n).astype(np.float32)
    by_word = np.ascontiguousarray(scaled.reshape(k // 512, 128, 4, n).transpose(0, 1, 3, 2))
    if fmt == "e4m3":
        words = by_word.astype(ml_dtypes.float8_e4m3fn).view(np.uint8)
    else:
        c = by_word.astype(ml_dtypes.float4_e2m1fn).view(np.uint8) & 0xF
        words = c[..., 0::2] | (c[..., 1::2] << 4)
    return np.ascontiguousarray(words), np.ascontiguousarray(byte.astype(np.uint8).reshape(k // 512, 16, n))


def unpack_weight(words, scales, fmt):
    g, p, n, _ = words.shape
    if fmt == "e4m3":
        vals = np.ascontiguousarray(words).view(ml_dtypes.float8_e4m3fn).astype(np.float64)
    else:
        nib = np.empty((g, p, n, 4), np.uint8)
        nib[..., 0::2] = words & 0xF
        nib[..., 1::2] = words >> 4
        vals = E2M1[nib]
    vals = vals * np.repeat(np.exp2(scales.astype(np.float64) - 127.0), 8, axis=1)[..., None]
    return vals.transpose(0, 1, 3, 2).reshape(g * 512, n)
def pack4(w):
    words, scales = pack_weight(w, "e2m1")
    return words.reshape(words.shape[0], 128, -1), scales


def unpack4(words, scales):
    return unpack_weight(words.reshape(words.shape[0], 128, -1, 2), scales, "e2m1")


I, J, C, K, R = 1024, 1024, 2, 1024, 512


def draw0():
    s = mx_kscale(K)
    t = mx_kscale(C * J)
    u = mx_kscale(I)
    left = np.random.standard_normal((I, K)) * s * u[:, None]
    right = np.random.standard_normal((C * J, K)) / np.sqrt(K) / s * t[:, None]
    prior = 0.5 * np.random.standard_normal((I, C * J)) * u[:, None] * t
    near = np.random.uniform(0.2, 1.8, (I, J))
    v = np.random.standard_normal((C * J, R)) / np.sqrt(C * J) / t[:, None]
    y = np.random.standard_normal((I, R)) / np.sqrt(I) / u[:, None]
    v_words, v_scales = pack4(v)
    return {"left": bf(left), "right": bf(right), "prior": bf(prior), "near": bf(near),
            "v_words": v_words, "v_scales": v_scales, "y": bf(y)}


def core(left, right, prior, near, v_words, v_scales, y):
    z = mxq(f64(left), 1, "e4m3") @ mxq(f64(right), 1, "e4m3").T
    z = np.maximum(z + f64(prior), 0.0)
    z = (z.reshape(I, C, J) * f64(near)[:, None, :]).reshape(I, C * J)
    to_ligand = mxq(z, 1, "e4m3") @ unpack4(v_words, v_scales)
    to_receptor = mxq(z, 0, "e4m3").T @ mxq(f64(y), 0, "e4m3")
    return to_ligand, to_receptor


def e4m3fn_bytes(y):
    return np.clip(np.asarray(y, np.float64), -448.0, 448.0).astype(np.float32).astype(ml_dtypes.float8_e4m3fn).view(np.uint8)


def e4m3fn_values(b):
    return np.asarray(b, np.uint8).view(ml_dtypes.float8_e4m3fn).astype(np.float64)


def setup_inputs():
    d = draw0()
    x0 = np.asarray(d['y']).astype(np.float64)
    s = (np.max(np.abs(x0), axis=(1,), keepdims=True) / 448.0).astype(np.float32)
    out = {}
    for k, v in d.items():
        if k == 'y':
            out['y_bytes'] = e4m3fn_bytes(x0 / s.astype(np.float64))
            out['y_scale'] = s
        else:
            out[k] = v
    return out


def reference(left, right, prior, near, v_words, v_scales, y_bytes, y_scale):
    return core(left, right, prior, near, v_words, v_scales, e4m3fn_values(y_bytes) * y_scale.astype(np.float64))

@@ -1,0 +1,465 @@
+from contextlib import ExitStack
+
+import concourse.mybir as mybir
+from concourse.masks import make_identity
+
+I, J, C, K, R = 1024, 1024, 2, 1024, 512
+M = C * J
+FLOPS = 2 * I * M * K + 2 * I * M * R + 2 * I * M * R
+
+F32 = mybir.dt.float32
+BF16 = mybir.dt.bfloat16
+I32 = mybir.dt.int32
+U32 = mybir.dt.uint32
+U8 = mybir.dt.uint8
+FP8 = mybir.dt.float8_e4m3fn
+FP8X4 = mybir.dt.float8_e4m3fn_x4
+FP4X4 = mybir.dt.float4_e2m1fn_x4
+ADD = mybir.AluOpType.add
+MAX = mybir.AluOpType.max
+MULT = mybir.AluOpType.mult
+COPY = mybir.ActivationFunctionType.Copy
+
+P = 128
+ORDER = [(0, 0), (1, 0), (0, 1), (1, 1), (0, 2), (0, 3), (1, 2), (1, 3)]
+N_UNITS = len(ORDER)
+
+
+def tile_pair_tensor_messages_s8_kernel(
+    tc, left, right, prior, near, v_words, v_scales, y_bytes, y_scale, to_ligand, to_receptor
+):
+    nc = tc.nc
+    left_v = left.rearrange("(g p t) d -> g p t d", p=P, t=4)
+    right_v = right.rearrange("(g s q) d -> g q s d", s=4, q=P)
+    prior_v = prior.rearrange("(g p t) m -> g p t m", p=P, t=4)
+    near_v = near.rearrange("(g p t) m -> g p t m", p=P, t=4)
+    lig_v = to_ligand.rearrange("(g p t) r -> g t p r", p=P, t=4)
+    rec_v = to_receptor.rearrange("(g s q) r -> g s q r", s=4, q=P)
+
+    with ExitStack() as ctx:
+        keep = ctx.enter_context(tc.tile_pool(name="keep", bufs=1))
+        work = ctx.enter_context(tc.tile_pool(name="work", bufs=2))
+        s1_pool = ctx.enter_context(tc.psum_pool(name="s1", bufs=1))
+        w_pool = ctx.enter_context(tc.psum_pool(name="w", bufs=4))
+        ctx.enter_context(tc.manual_schedule())
+
+        ident = keep.tile([P, P], F32, name="ident", align_bytes=64)
+        make_identity(nc, ident[:])
+        warm = keep.tile([P, 2], F32, name="warm", align_bytes=64)
+        nc.gpsimd.memset(warm[:], 0.0)
+        v_tile = keep.tile([P, 4, 2 * R], U8, name="v_tile", align_bytes=64)
+        vs_tile = keep.tile([P, 4, R], U8, name="vs_tile", align_bytes=64)
+        nc.gpsimd.memset(vs_tile[:].rearrange("p g n -> p (g n)").bitcast(I32), 0)
+        nc.scalar.activation(warm[:, 1:2], warm[:, 0:1], COPY)
+
+        lc = [keep.tile([P, 4, 2, P], U32, name=f"lc{g}", align_bytes=64) for g in range(2)]
+        ls = [keep.tile([P, 4, 2, P], U8, name=f"ls{g}", align_bytes=64) for g in range(2)]
+        rc = [keep.tile([P, 2, 4 * P], U32, name=f"rc{g}", align_bytes=64) for g in range(4)]
+        rs = [keep.tile([P, 2, 4 * P], U8, name=f"rs{g}", align_bytes=64) for g in range(4)]
+        yc = [keep.tile([P, R], U32, name=f"yc{g}", align_bytes=64) for g in range(2)]
+        ys = [keep.tile([P, R], U8, name=f"ys{g}", align_bytes=64) for g in range(2)]
+        za_c, za_s, zb_c, zb_s = {}, {}, {}, {}
+        for g, b in ORDER:
+            za_c[g, b] = keep.tile([P, 4 * P], U32, name=f"zac{g}{b}", align_bytes=64)
+            za_s[g, b] = keep.tile([P, 4 * P], U8, name=f"zas{g}{b}", align_bytes=64)
+            zb_c[g, b] = keep.tile([P, 4, P], U32, name=f"zbc{g}{b}", align_bytes=64)
+            zb_s[g, b] = keep.tile([P, 4, P], U8, name=f"zbs{g}{b}", align_bytes=64)
+
+        raws, priors, nears = {}, {}, {}
+
+        def raw_tile(key):
+            raw = work.tile([P, 4, K], BF16, name="raw", tag="raw", bufs=4, align_bytes=64)
+            raws[key] = raw
+
+        def load_raw(key, t0, t1):
+            side, g = key
+            view = left_v if side == "l" else right_v
+            nc.sync.dma_start(out=raws[key][:, t0:t1, :], in_=view[g, :, t0:t1, :])
+
+        def load_prior(g, b):
+            t = work.tile([P, 4, 4 * P], BF16, name="prior_t", tag="prior_t", bufs=5, align_bytes=64)
+            nc.sync.dma_start(out=t[:], in_=prior_v[g, :, :, 512 * b : 512 * (b + 1)])
+            priors[g, b] = t
+
+        def load_near(g, b):
+            t = keep.tile([P, 4, 4 * P], BF16, name=f"near{g}{b}", align_bytes=64)
+            nc.sync.dma_start(out=t[:], in_=near_v[g, :, :, 512 * b : 512 * (b + 1)])
+            nears[g, b] = t
+
+        def transpose_rows(key, t):
+            words = raws[key][:].rearrange("p t d -> p (t d)").bitcast(F32)
+            bank = w_pool.tile([P, 2, 2, P], F32, name="bank", tag="bank", bufs=4)
+            for h in range(2):
+                for u in range(2):
+                    lo = 512 * t + 256 * h
+                    nc.tensor.transpose(bank[:, h, u, :], words[:, lo + u : lo + 256 : 2], ident[:])
+            return bank
+
+        grouped = {}
+
+        def copy_rows(key, t, bank, on_vector):
+            side, g = key
+            src = bank[:].rearrange("x h u p -> x h p u")
+            if side == "l":
+                if t == 0:
+                    grouped[key] = work.tile([P, 4, 2, P, 4], BF16, name="rin", tag="rin", bufs=3, align_bytes=64)
+                dst = grouped[key][:, t].rearrange("x h p e -> x (h p e)").bitcast(F32)
+                dst = dst.rearrange("x (h p u) -> x h p u", h=2, u=2)
+            else:
+                if t == 0:
+                    grouped[key] = work.tile([P, 2, 4, P, 4], BF16, name="rin", tag="rin", bufs=3, align_bytes=64)
+                dst = grouped[key][:].rearrange("x h s p e -> x (h s p e)").bitcast(F32)
+                dst = dst.rearrange("x (h s p u) -> x h s p u", h=2, s=4, u=2)[:, :, t]
+            if on_vector:
+                nc.vector.tensor_copy(out=dst, in_=src)
+            else:
+                nc.scalar.copy(out=dst, in_=src)
+
+        def quantize_left(g, t0, t1):
+            nc.vector.quantize_mx(
+                out=lc[g][:, t0:t1].rearrange("x t h p -> x (t h p)").bitcast(FP8X4),
+                scales=ls[g][:, t0:t1].rearrange("x t h p -> x (t h p)"),
+                in_=grouped["l", g][:, t0:t1].rearrange("x t h p e -> x (t h p e)"),
+            )
+
+        def quantize_right(g, h, s0=0, s1=4):
+            nc.vector.quantize_mx(
+                out=rc[g][:, h, P * s0 : P * s1].bitcast(FP8X4),
+                scales=rs[g][:, h, P * s0 : P * s1],
+                in_=grouped["r", g][:, h, s0:s1].rearrange("x s p e -> x (s p e)"),
+            )
+
+        s1_banks = {}
+
+        def stage1(k, t):
+            g, b = ORDER[k]
+            bank = s1_pool.tile([P, 4 * P], F32, name="s1b", tag=f"s1b{t}", bufs=1)
+            for h in range(2):
+                nc.tensor.matmul_mx(
+                    out=bank[:],
+                    lhsT=lc[g][:, t, h, :].bitcast(FP8X4),
+                    lhsT_scale=ls[g][:, t, h, :],
+                    rhs=rc[b][:, h, :].bitcast(FP8X4),
+                    rhs_scale=rs[b][:, h, :],
+                    start=(h == 0),
+                    stop=(h == 1),
+                )
+            s1_banks[k, t] = bank
+
+        sums, zns, zis, lis, z_banks = {}, {}, {}, {}, {}
+
+        def add_prior(k, t):
+            g, b = ORDER[k]
+            if t == 0:
+                sums[k] = work.tile([P, 4, 4 * P], F32, name="sum_t", tag="sum_t", bufs=2, align_bytes=64)
+            nc.vector.tensor_tensor(
+                out=sums[k][:, t, :], in0=s1_banks[k, t][:], in1=priors[g, b][:, t, :], op=ADD
+            )
+
+        def relu_near(k, t0, t1):
+            g, b = ORDER[k]
+            if t0 == 0:
+                zns[k] = work.tile([P, 4, 4 * P], BF16, name="zn", tag="zn", bufs=3, align_bytes=64)
+            nc.vector.scalar_tensor_tensor(
+                out=zns[k][:, t0:t1].rearrange("p t m -> p (t m)"),
+                in0=sums[k][:, t0:t1].rearrange("p t m -> p (t m)"),
+                scalar=0.0,
+                in1=nears[g, b % 2][:, t0:t1].rearrange("p t m -> p (t m)"),
+                op0=MAX,
+                op1=MULT,
+            )
+
+        def group_a(k, c0, c1, engine):
+            if k not in zis:
+                zis[k] = work.tile([P, 4 * P, 4], BF16, name="zi", tag="zi", bufs=2, align_bytes=64)
+            dst = zis[k][:, P * c0 : P * c1, :].rearrange("p (c i) t -> p c t i", i=4)
+            src = zns[k][:, :, P * c0 : P * c1].rearrange("p t (c i) -> p c t i", i=4)
+            if engine == "v":
+                nc.vector.tensor_copy(out=dst, in_=src)
+            elif engine == "s":
+                nc.scalar.copy(out=dst, in_=src)
+            else:
+                nc.gpsimd.tensor_scalar(out=dst, in0=src, scalar1=1.0, scalar2=0.0, op0=MULT, op1=ADD)
+
+        def quantize_a(k, s0=0, s1=4):
+            g, b = ORDER[k]
+            nc.vector.quantize_mx(
+                out=za_c[g, b][:, P * s0 : P * s1].bitcast(FP8X4),
+                scales=za_s[g, b][:, P * s0 : P * s1],
+                in_=zis[k][:, P * s0 : P * s1].rearrange("p m t -> p (m t)"),
+            )
+
+        def transpose_z(k, half):
+            bank = w_pool.tile([P, 2, 2, P], F32, name="bank", tag="bank", bufs=4)
+            z_banks[k, half] = bank
+            for tt in range(2):
+                words = zns[k][:, 2 * half + tt, :].bitcast(F32)
+                for u in range(2):
+                    nc.tensor.transpose(bank[:, tt, u, :], words[:, u : 2 * P : 2], ident[:])
+
+        def copy_b(k, half, on_vector=False):
+            if half == 0:
+                lis[k] = work.tile([P, 4, P, 4], BF16, name="li", tag="li", bufs=2, align_bytes=64)
+            dst = lis[k][:, 2 * half : 2 * half + 2].rearrange("q t p e -> q (t p e)").bitcast(F32)
+            dst = dst.rearrange("q (t p u) -> q t p u", t=2, u=2)
+            src = z_banks[k, half][:].rearrange("q t u p -> q t p u")
+            if on_vector:
+                nc.vector.tensor_copy(out=dst, in_=src)
+            else:
+                nc.scalar.copy(out=dst, in_=src)
+
+        def quantize_b(k, h0=0, h1=2):
+            g, b = ORDER[k]
+            nc.vector.quantize_mx(
+                out=zb_c[g, b][:, 2 * h0 : 2 * h1].rearrange("q t p -> q (t p)").bitcast(FP8X4),
+                scales=zb_s[g, b][:, 2 * h0 : 2 * h1].rearrange("q t p -> q (t p)"),
+                in_=lis[k][:, 2 * h0 : 2 * h1].rearrange("q t p e -> q (t p e)"),
+            )
+
+        outs = {}
+
+        def finish(bank, kind, g, t, on_vector):
+            if (kind, g) not in outs:
+                outs[kind, g] = work.tile([P, 4, R], F32, name="raw", tag="raw", bufs=4, align_bytes=64)
+            o = outs[kind, g][:, t, :]
+            if on_vector:
+                nc.vector.tensor_copy(out=o, in_=bank[:])
+            else:
+                nc.scalar.copy(out=o, in_=bank[:])
+            nc.sync.dma_start(out=(rec_v if kind == "r" else lig_v)[g, t], in_=o)
+
+        def receptor(b, s, on_vector=False):
+            bank = w_pool.tile([P, R], F32, name="bank", tag="bank", bufs=4)
+            for g in range(2):
+                nc.tensor.matmul_mx(
+                    out=bank[:],
+                    lhsT=za_c[g, b][:, P * s : P * (s + 1)].bitcast(FP8X4),
+                    lhsT_scale=za_s[g, b][:, P * s : P * (s + 1)],
+                    rhs=yc[g][:].bitcast(FP8X4),
+                    rhs_scale=ys[g][:],
+                    start=(g == 0),
+                    stop=(g == 1),
+                )
+            finish(bank, "r", b, s, on_vector)
+
+        def ligand_passes(bank, g, t, blocks):
+            for b in blocks:
+                nc.tensor.matmul_mx(
+                    out=bank[:],
+                    lhsT=zb_c[g, b][:, t, :].bitcast(FP8X4),
+                    lhsT_scale=zb_s[g, b][:, t, :],
+                    rhs=v_tile[:, b, :].bitcast(FP4X4),
+                    rhs_scale=vs_tile[:, b, :],
+                    start=(b == 0),
+                    stop=(b == 3),
+                )
+
+        def ligand(g, t, on_vector=False):
+            bank = w_pool.tile([P, R], F32, name="bank", tag="bank", bufs=4)
+            ligand_passes(bank, g, t, range(4))
+            finish(bank, "l", g, t, on_vector)
+
+        y_codes = keep.tile([P, 2, 4, R], U8, name="y_codes", align_bytes=64)
+        y_sc = keep.tile([P, 2, 4], F32, name="y_sc", align_bytes=64)
+        y_plane, y_group = {}, {}
+
+        def load_y():
+            nc.sync.dma_start(out=y_sc[:], in_=y_scale.rearrange("(g p t) o -> p g (t o)", p=P, t=4))
+            nc.sync.dma_start(out=y_codes[:], in_=y_bytes.rearrange("(g p t) r -> p g t r", p=P, t=4))
+
+        def widen_y(g):
+            y_plane[g] = work.tile([P, 4, R], BF16, name="y_plane", tag="y_plane", bufs=2, align_bytes=64)
+            for t in range(4):
+                nc.scalar.activation(
+                    y_plane[g][:, t, :], y_codes[:, g, t, :].bitcast(FP8), COPY, scale=y_sc[:, g, t : t + 1]
+                )
+
+        def group_y(g):
+            y_group[g] = work.tile([P, R, 4], BF16, name="y_group", tag="y_group", bufs=1, align_bytes=64)
+            nc.vector.tensor_copy(
+                out=y_group[g][:].rearrange("p (c i) t -> p c t i", i=4),
+                in_=y_plane[g][:].rearrange("p t (c i) -> p c t i", i=4),
+            )
+
+        def quantize_y(g):
+            nc.vector.quantize_mx(
+                out=yc[g][:].bitcast(FP8X4), scales=ys[g][:], in_=y_group[g][:].rearrange("p r t -> p (r t)")
+            )
+
+        L0, R0, L1, R1, R2, R3 = ("l", 0), ("r", 0), ("l", 1), ("r", 1), ("r", 2), ("r", 3)
+        for key in (L0, R0, L1, R1):
+            raw_tile(key)
+        load_raw(L0, 0, 1)
+        for s in range(4):
+            load_raw(R0, s, s + 1)
+        load_raw(L0, 1, 2)
+        load_raw(L0, 2, 4)
+        load_prior(0, 0)
+        load_y()
+        load_raw(L1, 0, 2)
+        load_near(0, 0)
+        load_raw(L1, 2, 4)
+        load_prior(1, 0)
+        load_near(1, 0)
+        load_raw(R1, 0, 2)
+        load_raw(R1, 2, 4)
+        load_prior(0, 1)
+        load_near(0, 1)
+        load_prior(1, 1)
+        load_near(1, 1)
+
+        def rows(key, t, on_vector=False):
+            bank = transpose_rows(key, t)
+            copy_rows(key, t, bank, on_vector)
+
+        rows(L0, 0, True)
+        rows(R0, 0)
+        rows(R0, 1, True)
+        quantize_left(0, 0, 1)
+        quantize_right(0, 0, 0, 1)
+        quantize_right(0, 1, 0, 1)
+        rows(R0, 2)
+        rows(R0, 3, True)
+        quantize_right(0, 0, 1, 3)
+        quantize_right(0, 1, 1, 3)
+        quantize_right(0, 0, 3, 4)
+        quantize_right(0, 1, 3, 4)
+        rows(L0, 1)
+        stage1(0, 0)
+        quantize_left(0, 1, 2)
+        rows(L0, 2)
+        rows(L0, 3)
+        stage1(0, 1)
+        add_prior(0, 0)
+        quantize_left(0, 2, 4)
+        stage1(0, 2)
+        stage1(0, 3)
+        for t in range(1, 4):
+            add_prior(0, t)
+        widen_y(0)
+        for t in range(4):
+            rows(L1, t)
+        relu_near(0, 0, 2)
+        quantize_left(1, 0, 2)
+        relu_near(0, 2, 4)
+        quantize_left(1, 2, 4)
+        for t in range(4):
+            stage1(1, t)
+        group_y(0)
+        widen_y(1)
+        for t in range(4):
+            rows(R1, t)
+
+        raw_tile(R2)
+        load_raw(R2, 0, 4)
+        load_prior(0, 2)
+        raw_tile(R3)
+        load_raw(R3, 0, 4)
+
+        def load_v():
+            nc.sync.dma_start(
+                out=v_tile[:].rearrange("p g n -> p (g n)").bitcast(I32).rearrange("p (g n) -> p g n", g=4),
+                in_=v_words.bitcast(I32).rearrange("g p n -> p g n"),
+            )
+            vs_words = vs_tile[:].rearrange("p g n -> p (g n)").bitcast(I32).rearrange("p (g n) -> p g n", g=4)
+            for quad in range(4):
+                nc.sync.dma_start(
+                    out=vs_words[32 * quad : 32 * quad + 4],
+                    in_=v_scales.bitcast(I32)[:, 4 * quad : 4 * quad + 4, :].rearrange("g q n -> q g n"),
+                )
+
+        lig_banks = {}
+
+        def ligand_open(g, t, pool_tag):
+            if pool_tag:
+                lig_banks[g, t] = s1_pool.tile([P, R], F32, name="s1b", tag=f"s1b{t}", bufs=1)
+            else:
+                lig_banks[g, t] = w_pool.tile([P, R], F32, name="bank", tag="bank", bufs=4)
+            ligand_passes(lig_banks[g, t], g, t, range(2 if pool_tag else 3))
+
+        def ligand_close(g, t, on_vector=False):
+            ligand_passes(lig_banks[g, t], g, t, range(3, 4))
+            finish(lig_banks[g, t], "l", g, t, on_vector)
+
+        last = N_UNITS - 1
+        ahead = {1: R2, 2: R3}
+        fresh = {1: R1, 3: R2, 4: R3}
+        for k in range(1, N_UNITS):
+            for t in range(4):
+                add_prior(k, t)
+            group_a(k - 1, 0, 1, "g")
+            group_a(k - 1, 1, 2, "g")
+            for half in range(2):
+                transpose_z(k - 1, half)
+                copy_b(k - 1, half)
+            group_a(k - 1, 2, 4, "s")
+            if k == 1:
+                load_v()
+                load_prior(0, 3)
+                load_prior(1, 2)
+            if k == 2:
+                load_prior(1, 3)
+            key = fresh.get(k)
+            if key is not None:
+                quantize_right(key[1], 0)
+                quantize_right(key[1], 1)
+            if k < last:
+                for t in range(4):
+                    stage1(k + 1, t)
+            relu_near(k, 0, 2)
+            quantize_b(k - 1)
+            if k == 1:
+                quantize_y(0)
+                group_y(1)
+            if k == 2:
+                quantize_y(1)
+            quantize_a(k - 1)
+            key = ahead.get(k)
+            if key is not None:
+                for t in range(4):
+                    rows(key, t)
+            if k == 3:
+                for s in range(4):
+                    receptor(0, s)
+            if k == 4:
+                for s in range(4):
+                    receptor(1, s)
+            if k == 5:
+                ligand_open(0, 0, False)
+                ligand_open(0, 1, False)
+            if k == 6:
+                ligand_close(0, 0)
+                ligand_close(0, 1)
+                ligand(0, 2)
+                ligand(0, 3)
+            relu_near(k, 2, 4)
+
+        for t in range(4):
+            ligand_open(1, t, True)
+        receptor(2, 0)
+        transpose_z(last, 0)
+        copy_b(last, 0)
+        receptor(2, 1)
+        receptor(2, 2)
+        transpose_z(last, 1)
+        group_a(last, 0, 1, "v")
+        quantize_b(last, 0, 1)
+        group_a(last, 1, 2, "v")
+        quantize_a(last, 0, 1)
+        copy_b(last, 1)
+        group_a(last, 3, 4, "s")
+        for t in range(4):
+            ligand_passes(lig_banks[1, t], 1, t, [2])
+        receptor(2, 3)
+        group_a(last, 2, 3, "v")
+        quantize_a(last, 1, 2)
+        ligand_close(1, 0, True)
+        ligand_close(1, 1)
+        quantize_b(last, 1, 2)
+        receptor(3, 0, True)
+        quantize_a(last, 2, 4)
+        receptor(3, 1)
+        ligand_close(1, 2, True)
+        ligand_close(1, 3)
+        receptor(3, 2, True)
+        receptor(3, 3)

@@ -21,8 +21,9 @@ MULT = mybir.AluOpType.mult
 COPY = mybir.ActivationFunctionType.Copy
 
 P = 128
-ORDER = [(0, 0), (1, 0), (0, 1), (1, 1), (0, 2), (0, 3), (1, 2), (1, 3)]
-N_UNITS = len(ORDER)
+W = 512
+ORDER = [(0, 0), (0, 2), (0, 1), (0, 3), (1, 0), (1, 2), (1, 1), (1, 3)]
+LAST = len(ORDER) - 1
 
 
 def tile_pair_tensor_messages_s8_kernel(
@@ -33,8 +34,10 @@ def tile_pair_tensor_messages_s8_kernel(
     right_v = right.rearrange("(g s q) d -> g q s d", s=4, q=P)
     prior_v = prior.rearrange("(g p t) m -> g p t m", p=P, t=4)
     near_v = near.rearrange("(g p t) m -> g p t m", p=P, t=4)
-    lig_v = to_ligand.rearrange("(g p t) r -> g t p r", p=P, t=4)
-    rec_v = to_receptor.rearrange("(g s q) r -> g s q r", s=4, q=P)
+    out_v = {
+        "l": to_ligand.rearrange("(g p t) r -> g p t r", p=P, t=4),
+        "r": to_receptor.rearrange("(g p t) r -> g p t r", p=P, t=4),
+    }
 
     with ExitStack() as ctx:
         keep = ctx.enter_context(tc.tile_pool(name="keep", bufs=1))
@@ -45,95 +48,100 @@ def tile_pair_tensor_messages_s8_kernel(
 
         ident = keep.tile([P, P], F32, name="ident", align_bytes=64)
         make_identity(nc, ident[:])
-        warm = keep.tile([P, 2], F32, name="warm", align_bytes=64)
-        nc.gpsimd.memset(warm[:], 0.0)
         v_tile = keep.tile([P, 4, 2 * R], U8, name="v_tile", align_bytes=64)
         vs_tile = keep.tile([P, 4, R], U8, name="vs_tile", align_bytes=64)
         nc.gpsimd.memset(vs_tile[:].rearrange("p g n -> p (g n)").bitcast(I32), 0)
-        nc.scalar.activation(warm[:, 1:2], warm[:, 0:1], COPY)
 
         lc = [keep.tile([P, 4, 2, P], U32, name=f"lc{g}", align_bytes=64) for g in range(2)]
         ls = [keep.tile([P, 4, 2, P], U8, name=f"ls{g}", align_bytes=64) for g in range(2)]
-        rc = [keep.tile([P, 2, 4 * P], U32, name=f"rc{g}", align_bytes=64) for g in range(4)]
-        rs = [keep.tile([P, 2, 4 * P], U8, name=f"rs{g}", align_bytes=64) for g in range(4)]
+        rc = [keep.tile([P, 2, W], U32, name=f"rc{g}", align_bytes=64) for g in range(4)]
+        rs = [keep.tile([P, 2, W], U8, name=f"rs{g}", align_bytes=64) for g in range(4)]
         yc = [keep.tile([P, R], U32, name=f"yc{g}", align_bytes=64) for g in range(2)]
         ys = [keep.tile([P, R], U8, name=f"ys{g}", align_bytes=64) for g in range(2)]
         za_c, za_s, zb_c, zb_s = {}, {}, {}, {}
         for g, b in ORDER:
-            za_c[g, b] = keep.tile([P, 4 * P], U32, name=f"zac{g}{b}", align_bytes=64)
-            za_s[g, b] = keep.tile([P, 4 * P], U8, name=f"zas{g}{b}", align_bytes=64)
+            za_c[g, b] = keep.tile([P, 4, P], U32, name=f"zac{g}{b}", align_bytes=64)
+            za_s[g, b] = keep.tile([P, 4, P], U8, name=f"zas{g}{b}", align_bytes=64)
             zb_c[g, b] = keep.tile([P, 4, P], U32, name=f"zbc{g}{b}", align_bytes=64)
             zb_s[g, b] = keep.tile([P, 4, P], U8, name=f"zbs{g}{b}", align_bytes=64)
 
         raws, priors, nears = {}, {}, {}
 
-        def raw_tile(key):
-            raw = work.tile([P, 4, K], BF16, name="raw", tag="raw", bufs=4, align_bytes=64)
-            raws[key] = raw
-
-        def load_raw(key, t0, t1):
+        def load_rows(key, t):
             side, g = key
             view = left_v if side == "l" else right_v
-            nc.sync.dma_start(out=raws[key][:, t0:t1, :], in_=view[g, :, t0:t1, :])
+            raw = work.tile([P, K], BF16, name="raw", tag="raw", bufs=9, align_bytes=64)
+            nc.sync.dma_start(out=raw[:], in_=view[g, :, t, :])
+            raws[key, t] = raw
 
-        def load_prior(g, b):
-            t = work.tile([P, 4, 4 * P], BF16, name="prior_t", tag="prior_t", bufs=5, align_bytes=64)
-            nc.sync.dma_start(out=t[:], in_=prior_v[g, :, :, 512 * b : 512 * (b + 1)])
-            priors[g, b] = t
+        def load_prior(k, t0=0, t1=4):
+            g, b = ORDER[k]
+            if t0 == 0:
+                priors[k] = work.tile([P, 4, W], BF16, name="prior_t", tag="prior_t", bufs=5, align_bytes=64)
+            nc.sync.dma_start(out=priors[k][:, t0:t1, :], in_=prior_v[g, :, t0:t1, W * b : W * (b + 1)])
 
-        def load_near(g, b):
-            t = keep.tile([P, 4, 4 * P], BF16, name=f"near{g}{b}", align_bytes=64)
-            nc.sync.dma_start(out=t[:], in_=near_v[g, :, :, 512 * b : 512 * (b + 1)])
-            nears[g, b] = t
+        def load_near(g, c):
+            near_t = keep.tile([P, 4, W], BF16, name=f"near{g}{c}", align_bytes=64)
+            nc.sync.dma_start(out=near_t[:], in_=near_v[g, :, :, W * c : W * (c + 1)])
+            nears[g, c] = near_t
 
-        def transpose_rows(key, t):
-            words = raws[key][:].rearrange("p t d -> p (t d)").bitcast(F32)
-            bank = w_pool.tile([P, 2, 2, P], F32, name="bank", tag="bank", bufs=4)
-            for h in range(2):
-                for u in range(2):
-                    lo = 512 * t + 256 * h
-                    nc.tensor.transpose(bank[:, h, u, :], words[:, lo + u : lo + 256 : 2], ident[:])
-            return bank
+        def new_bank(shape):
+            return w_pool.tile(shape, F32, name="bank", tag="bank", bufs=4)
 
-        grouped = {}
-
-        def copy_rows(key, t, bank, on_vector):
-            side, g = key
-            src = bank[:].rearrange("x h u p -> x h p u")
-            if side == "l":
-                if t == 0:
-                    grouped[key] = work.tile([P, 4, 2, P, 4], BF16, name="rin", tag="rin", bufs=3, align_bytes=64)
-                dst = grouped[key][:, t].rearrange("x h p e -> x (h p e)").bitcast(F32)
-                dst = dst.rearrange("x (h p u) -> x h p u", h=2, u=2)
-            else:
-                if t == 0:
-                    grouped[key] = work.tile([P, 2, 4, P, 4], BF16, name="rin", tag="rin", bufs=3, align_bytes=64)
-                dst = grouped[key][:].rearrange("x h s p e -> x (h s p e)").bitcast(F32)
-                dst = dst.rearrange("x (h s p u) -> x h s p u", h=2, s=4, u=2)[:, :, t]
+        def copy(on_vector, dst, src):
             if on_vector:
                 nc.vector.tensor_copy(out=dst, in_=src)
             else:
                 nc.scalar.copy(out=dst, in_=src)
 
+        grouped = {}
+
+        def rows(key, t, on_vector=False):
+            side, g = key
+            words = raws[key, t][:].bitcast(F32)
+            bank = new_bank([P, 2, 2, P])
+            for h in range(2):
+                for u in range(2):
+                    nc.tensor.transpose(bank[:, h, u, :], words[:, 256 * h + u : 256 * (h + 1) : 2], ident[:])
+            if t == 0:
+                grouped[key] = work.tile([P, 8, 2 * P], F32, name="rin", tag="rin", bufs=3, align_bytes=64)
+            if side == "l":
+                dst = grouped[key][:, 2 * t : 2 * t + 2, :]
+            else:
+                dst = grouped[key][:, t : 8 : 4, :]
+            copy(on_vector, dst.rearrange("x h (p u) -> x h p u", u=2), bank[:].rearrange("x h u p -> x h p u"))
+
+        def quantize(codes, scales, values):
+            nc.vector.quantize_mx(out=codes.bitcast(FP8X4), scales=scales, in_=values)
+
         def quantize_left(g, t0, t1):
-            nc.vector.quantize_mx(
-                out=lc[g][:, t0:t1].rearrange("x t h p -> x (t h p)").bitcast(FP8X4),
-                scales=ls[g][:, t0:t1].rearrange("x t h p -> x (t h p)"),
-                in_=grouped["l", g][:, t0:t1].rearrange("x t h p e -> x (t h p e)"),
+            quantize(
+                lc[g][:, t0:t1].rearrange("x t h p -> x (t h p)"),
+                ls[g][:, t0:t1].rearrange("x t h p -> x (t h p)"),
+                grouped["l", g][:, 2 * t0 : 2 * t1].rearrange("x a w -> x (a w)").bitcast(BF16),
             )
 
         def quantize_right(g, h, s0=0, s1=4):
-            nc.vector.quantize_mx(
-                out=rc[g][:, h, P * s0 : P * s1].bitcast(FP8X4),
-                scales=rs[g][:, h, P * s0 : P * s1],
-                in_=grouped["r", g][:, h, s0:s1].rearrange("x s p e -> x (s p e)"),
+            quantize(
+                rc[g][:, h, P * s0 : P * s1],
+                rs[g][:, h, P * s0 : P * s1],
+                grouped["r", g][:, 4 * h + s0 : 4 * h + s1].rearrange("x a w -> x (a w)").bitcast(BF16),
             )
+
+        def quantize_rows(key, half):
+            if key[0] == "l":
+                quantize_left(key[1], 2 * half, 2 * half + 2)
+            else:
+                quantize_right(key[1], half)
 
         s1_banks = {}
 
+        def s1_bank(t):
+            return s1_pool.tile([P, W], F32, name="s1b", tag=f"s1b{t}", bufs=1)
+
         def stage1(k, t):
             g, b = ORDER[k]
-            bank = s1_pool.tile([P, 4 * P], F32, name="s1b", tag=f"s1b{t}", bufs=1)
+            bank = s1_bank(t)
             for h in range(2):
                 nc.tensor.matmul_mx(
                     out=bank[:],
@@ -146,101 +154,85 @@ def tile_pair_tensor_messages_s8_kernel(
                 )
             s1_banks[k, t] = bank
 
-        sums, zns, zis, lis, z_banks = {}, {}, {}, {}, {}
+        sums, zs, zis, lis = {}, {}, {}, {}
 
         def add_prior(k, t):
-            g, b = ORDER[k]
             if t == 0:
-                sums[k] = work.tile([P, 4, 4 * P], F32, name="sum_t", tag="sum_t", bufs=2, align_bytes=64)
-            nc.vector.tensor_tensor(
-                out=sums[k][:, t, :], in0=s1_banks[k, t][:], in1=priors[g, b][:, t, :], op=ADD
-            )
+                sums[k] = work.tile([P, 4, W], F32, name="sum_t", tag="sum_t", bufs=2, align_bytes=64)
+            nc.vector.tensor_tensor(out=sums[k][:, t, :], in0=s1_banks[k, t][:], in1=priors[k][:, t, :], op=ADD)
 
-        def relu_near(k, t0, t1):
+        def relu_near(k, u, t0=0, t1=4):
             g, b = ORDER[k]
             if t0 == 0:
-                zns[k] = work.tile([P, 4, 4 * P], BF16, name="zn", tag="zn", bufs=3, align_bytes=64)
+                zs[k, u] = work.tile([P, 4, 2 * P], BF16, name="z", tag="z", bufs=4, align_bytes=64)
+            pairs = "p t (q u e) -> p (t q) u e"
             nc.vector.scalar_tensor_tensor(
-                out=zns[k][:, t0:t1].rearrange("p t m -> p (t m)"),
-                in0=sums[k][:, t0:t1].rearrange("p t m -> p (t m)"),
+                out=zs[k, u][:, t0:t1].rearrange("p t (q e) -> p (t q) e", e=2),
+                in0=sums[k][:, t0:t1].rearrange(pairs, u=2, e=2)[:, :, u, :],
                 scalar=0.0,
-                in1=nears[g, b % 2][:, t0:t1].rearrange("p t m -> p (t m)"),
+                in1=nears[g, b % 2][:, t0:t1].rearrange(pairs, u=2, e=2)[:, :, u, :],
                 op0=MAX,
                 op1=MULT,
             )
 
-        def group_a(k, c0, c1, engine):
-            if k not in zis:
-                zis[k] = work.tile([P, 4 * P, 4], BF16, name="zi", tag="zi", bufs=2, align_bytes=64)
-            dst = zis[k][:, P * c0 : P * c1, :].rearrange("p (c i) t -> p c t i", i=4)
-            src = zns[k][:, :, P * c0 : P * c1].rearrange("p t (c i) -> p c t i", i=4)
-            if engine == "v":
-                nc.vector.tensor_copy(out=dst, in_=src)
-            elif engine == "s":
-                nc.scalar.copy(out=dst, in_=src)
-            else:
+        def group_a(k, u, engine):
+            zis[k, u] = work.tile([P, 2, P, 4], BF16, name="zi", tag="zi", bufs=4, align_bytes=64)
+            if engine == "g":
+                dst = zis[k, u][:]
+                src = zs[k, u][:].rearrange("p t (q e) -> p e q t", e=2)
                 nc.gpsimd.tensor_scalar(out=dst, in0=src, scalar1=1.0, scalar2=0.0, op0=MULT, op1=ADD)
+            else:
+                dst = zis[k, u][:].rearrange("p e (c i) t -> p c t i e", i=2)
+                src = zs[k, u][:].rearrange("p t (c i e) -> p c t i e", i=2, e=2)
+                copy(engine == "v", dst, src)
 
-        def quantize_a(k, s0=0, s1=4):
+        def quantize_a(k, u):
             g, b = ORDER[k]
-            nc.vector.quantize_mx(
-                out=za_c[g, b][:, P * s0 : P * s1].bitcast(FP8X4),
-                scales=za_s[g, b][:, P * s0 : P * s1],
-                in_=zis[k][:, P * s0 : P * s1].rearrange("p m t -> p (m t)"),
+            quantize(
+                za_c[g, b][:, 2 * u : 2 * u + 2].rearrange("p j q -> p (j q)"),
+                za_s[g, b][:, 2 * u : 2 * u + 2].rearrange("p j q -> p (j q)"),
+                zis[k, u][:].rearrange("p e q t -> p (e q t)"),
             )
 
-        def transpose_z(k, half):
-            bank = w_pool.tile([P, 2, 2, P], F32, name="bank", tag="bank", bufs=4)
-            z_banks[k, half] = bank
+        def turn_z(k, half, on_vector=False):
+            bank = new_bank([P, 2, 2, P])
             for tt in range(2):
-                words = zns[k][:, 2 * half + tt, :].bitcast(F32)
                 for u in range(2):
-                    nc.tensor.transpose(bank[:, tt, u, :], words[:, u : 2 * P : 2], ident[:])
-
-        def copy_b(k, half, on_vector=False):
+                    nc.tensor.transpose(bank[:, tt, u, :], zs[k, u][:, 2 * half + tt, :].bitcast(F32), ident[:])
             if half == 0:
-                lis[k] = work.tile([P, 4, P, 4], BF16, name="li", tag="li", bufs=2, align_bytes=64)
-            dst = lis[k][:, 2 * half : 2 * half + 2].rearrange("q t p e -> q (t p e)").bitcast(F32)
-            dst = dst.rearrange("q (t p u) -> q t p u", t=2, u=2)
-            src = z_banks[k, half][:].rearrange("q t u p -> q t p u")
-            if on_vector:
-                nc.vector.tensor_copy(out=dst, in_=src)
-            else:
-                nc.scalar.copy(out=dst, in_=src)
+                lis[k] = work.tile([P, 4, 2 * P], F32, name="li", tag="li", bufs=2, align_bytes=64)
+            dst = lis[k][:, 2 * half : 2 * half + 2].rearrange("q t (p u) -> q t p u", u=2)
+            copy(on_vector, dst, bank[:].rearrange("q t u p -> q t p u"))
 
         def quantize_b(k, h0=0, h1=2):
             g, b = ORDER[k]
-            nc.vector.quantize_mx(
-                out=zb_c[g, b][:, 2 * h0 : 2 * h1].rearrange("q t p -> q (t p)").bitcast(FP8X4),
-                scales=zb_s[g, b][:, 2 * h0 : 2 * h1].rearrange("q t p -> q (t p)"),
-                in_=lis[k][:, 2 * h0 : 2 * h1].rearrange("q t p e -> q (t p e)"),
+            quantize(
+                zb_c[g, b][:, 2 * h0 : 2 * h1].rearrange("q t p -> q (t p)"),
+                zb_s[g, b][:, 2 * h0 : 2 * h1].rearrange("q t p -> q (t p)"),
+                lis[k][:, 2 * h0 : 2 * h1].rearrange("q t w -> q (t w)").bitcast(BF16),
             )
 
-        outs = {}
+        def finish(bank, kind, g, t, on_vector=False):
+            o = work.tile([P, R], F32, name="o", tag="o", bufs=8, align_bytes=64)
+            copy(on_vector, o[:], bank[:])
+            nc.sync.dma_start(out=out_v[kind][g, :, t, :], in_=o[:])
 
-        def finish(bank, kind, g, t, on_vector):
-            if (kind, g) not in outs:
-                outs[kind, g] = work.tile([P, 4, R], F32, name="raw", tag="raw", bufs=4, align_bytes=64)
-            o = outs[kind, g][:, t, :]
-            if on_vector:
-                nc.vector.tensor_copy(out=o, in_=bank[:])
-            else:
-                nc.scalar.copy(out=o, in_=bank[:])
-            nc.sync.dma_start(out=(rec_v if kind == "r" else lig_v)[g, t], in_=o)
-
-        def receptor(b, s, on_vector=False):
-            bank = w_pool.tile([P, R], F32, name="bank", tag="bank", bufs=4)
-            for g in range(2):
+        def receptor_passes(bank, b, j, groups):
+            for g in groups:
                 nc.tensor.matmul_mx(
                     out=bank[:],
-                    lhsT=za_c[g, b][:, P * s : P * (s + 1)].bitcast(FP8X4),
-                    lhsT_scale=za_s[g, b][:, P * s : P * (s + 1)],
+                    lhsT=za_c[g, b][:, j, :].bitcast(FP8X4),
+                    lhsT_scale=za_s[g, b][:, j, :],
                     rhs=yc[g][:].bitcast(FP8X4),
                     rhs_scale=ys[g][:],
                     start=(g == 0),
                     stop=(g == 1),
                 )
-            finish(bank, "r", b, s, on_vector)
+
+        def receptor(b, j, on_vector=False):
+            bank = new_bank([P, R])
+            receptor_passes(bank, b, j, (0, 1))
+            finish(bank, "r", b, j, on_vector)
 
         def ligand_passes(bank, g, t, blocks):
             for b in blocks:
@@ -255,8 +247,8 @@ def tile_pair_tensor_messages_s8_kernel(
                 )
 
         def ligand(g, t, on_vector=False):
-            bank = w_pool.tile([P, R], F32, name="bank", tag="bank", bufs=4)
-            ligand_passes(bank, g, t, range(4))
+            bank = new_bank([P, R])
+            ligand_passes(bank, g, t, (0, 2, 1, 3))
             finish(bank, "l", g, t, on_vector)
 
         y_codes = keep.tile([P, 2, 4, R], U8, name="y_codes", align_bytes=64)
@@ -267,94 +259,24 @@ def tile_pair_tensor_messages_s8_kernel(
             nc.sync.dma_start(out=y_sc[:], in_=y_scale.rearrange("(g p t) o -> p g (t o)", p=P, t=4))
             nc.sync.dma_start(out=y_codes[:], in_=y_bytes.rearrange("(g p t) r -> p g t r", p=P, t=4))
 
-        def widen_y(g):
-            y_plane[g] = work.tile([P, 4, R], BF16, name="y_plane", tag="y_plane", bufs=2, align_bytes=64)
-            for t in range(4):
-                nc.scalar.activation(
-                    y_plane[g][:, t, :], y_codes[:, g, t, :].bitcast(FP8), COPY, scale=y_sc[:, g, t : t + 1]
-                )
+        def widen_y(g, t):
+            if t == 0:
+                y_plane[g] = work.tile([P, 4, R], BF16, name="y_plane", tag="y_plane", bufs=2, align_bytes=64)
+            nc.scalar.activation(
+                y_plane[g][:, t, :], y_codes[:, g, t, :].bitcast(FP8), COPY, scale=y_sc[:, g, t : t + 1]
+            )
 
-        def group_y(g):
-            y_group[g] = work.tile([P, R, 4], BF16, name="y_group", tag="y_group", bufs=1, align_bytes=64)
-            nc.vector.tensor_copy(
-                out=y_group[g][:].rearrange("p (c i) t -> p c t i", i=4),
-                in_=y_plane[g][:].rearrange("p t (c i) -> p c t i", i=4),
+        def group_y(g, half):
+            if half == 0:
+                y_group[g] = work.tile([P, R, 4], BF16, name="y_group", tag="y_group", bufs=1, align_bytes=64)
+            cols = slice(256 * half, 256 * (half + 1))
+            nc.scalar.copy(
+                out=y_group[g][:, cols].rearrange("p (c i) t -> p c t i", i=4),
+                in_=y_plane[g][:, :, cols].rearrange("p t (c i) -> p c t i", i=4),
             )
 
         def quantize_y(g):
-            nc.vector.quantize_mx(
-                out=yc[g][:].bitcast(FP8X4), scales=ys[g][:], in_=y_group[g][:].rearrange("p r t -> p (r t)")
-            )
-
-        L0, R0, L1, R1, R2, R3 = ("l", 0), ("r", 0), ("l", 1), ("r", 1), ("r", 2), ("r", 3)
-        for key in (L0, R0, L1, R1):
-            raw_tile(key)
-        load_raw(L0, 0, 1)
-        for s in range(4):
-            load_raw(R0, s, s + 1)
-        load_raw(L0, 1, 2)
-        load_raw(L0, 2, 4)
-        load_prior(0, 0)
-        load_y()
-        load_raw(L1, 0, 2)
-        load_near(0, 0)
-        load_raw(L1, 2, 4)
-        load_prior(1, 0)
-        load_near(1, 0)
-        load_raw(R1, 0, 2)
-        load_raw(R1, 2, 4)
-        load_prior(0, 1)
-        load_near(0, 1)
-        load_prior(1, 1)
-        load_near(1, 1)
-
-        def rows(key, t, on_vector=False):
-            bank = transpose_rows(key, t)
-            copy_rows(key, t, bank, on_vector)
-
-        rows(L0, 0, True)
-        rows(R0, 0)
-        rows(R0, 1, True)
-        quantize_left(0, 0, 1)
-        quantize_right(0, 0, 0, 1)
-        quantize_right(0, 1, 0, 1)
-        rows(R0, 2)
-        rows(R0, 3, True)
-        quantize_right(0, 0, 1, 3)
-        quantize_right(0, 1, 1, 3)
-        quantize_right(0, 0, 3, 4)
-        quantize_right(0, 1, 3, 4)
-        rows(L0, 1)
-        stage1(0, 0)
-        quantize_left(0, 1, 2)
-        rows(L0, 2)
-        rows(L0, 3)
-        stage1(0, 1)
-        add_prior(0, 0)
-        quantize_left(0, 2, 4)
-        stage1(0, 2)
-        stage1(0, 3)
-        for t in range(1, 4):
-            add_prior(0, t)
-        widen_y(0)
-        for t in range(4):
-            rows(L1, t)
-        relu_near(0, 0, 2)
-        quantize_left(1, 0, 2)
-        relu_near(0, 2, 4)
-        quantize_left(1, 2, 4)
-        for t in range(4):
-            stage1(1, t)
-        group_y(0)
-        widen_y(1)
-        for t in range(4):
-            rows(R1, t)
-
-        raw_tile(R2)
-        load_raw(R2, 0, 4)
-        load_prior(0, 2)
-        raw_tile(R3)
-        load_raw(R3, 0, 4)
+            quantize(yc[g][:], ys[g][:], y_group[g][:].rearrange("p r t -> p (r t)"))
 
         def load_v():
             nc.sync.dma_start(
@@ -368,98 +290,183 @@ def tile_pair_tensor_messages_s8_kernel(
                     in_=v_scales.bitcast(I32)[:, 4 * quad : 4 * quad + 4, :].rearrange("g q n -> q g n"),
                 )
 
-        lig_banks = {}
+        L0, L1, R0, R1, R2, R3 = ("l", 0), ("l", 1), ("r", 0), ("r", 1), ("r", 2), ("r", 3)
 
-        def ligand_open(g, t, pool_tag):
-            if pool_tag:
-                lig_banks[g, t] = s1_pool.tile([P, R], F32, name="s1b", tag=f"s1b{t}", bufs=1)
-            else:
-                lig_banks[g, t] = w_pool.tile([P, R], F32, name="bank", tag="bank", bufs=4)
-            ligand_passes(lig_banks[g, t], g, t, range(2 if pool_tag else 3))
+        def load_block(key):
+            for t in range(4):
+                load_rows(key, t)
 
-        def ligand_close(g, t, on_vector=False):
-            ligand_passes(lig_banks[g, t], g, t, range(3, 4))
-            finish(lig_banks[g, t], "l", g, t, on_vector)
+        load_rows(L0, 0)
+        load_block(R0)
+        for t in range(1, 4):
+            load_rows(L0, t)
+        load_prior(0, 0, 2)
+        load_prior(0, 2, 4)
 
-        last = N_UNITS - 1
-        ahead = {1: R2, 2: R3}
-        fresh = {1: R1, 3: R2, 4: R3}
-        for k in range(1, N_UNITS):
+        rows(L0, 0, True)
+        rows(R0, 0)
+        rows(R0, 1)
+        quantize_left(0, 0, 1)
+        rows(R0, 2)
+        load_block(R2)
+        load_near(0, 0)
+        load_prior(1)
+        for h in range(2):
+            quantize_right(0, h, 0, 2)
+        rows(R0, 3, True)
+        rows(L0, 1)
+        for h in range(2):
+            quantize_right(0, h, 2, 4)
+        rows(L0, 2)
+        quantize_left(0, 1, 2)
+        rows(L0, 3)
+        load_block(R1)
+        load_prior(2)
+        stage1(0, 0)
+        stage1(0, 1)
+        quantize_left(0, 2, 3)
+        add_prior(0, 0)
+        rows(R2, 0)
+        quantize_left(0, 3, 4)
+        add_prior(0, 1)
+        rows(R2, 1)
+        stage1(0, 2)
+        stage1(0, 3)
+        rows(R2, 2)
+        rows(R2, 3)
+        add_prior(0, 2)
+        add_prior(0, 3)
+        load_block(R3)
+        load_near(0, 1)
+        load_prior(3)
+        for h in range(2):
+            quantize_right(2, h, 0, 2)
+        for h in range(2):
+            quantize_right(2, h, 2, 4)
+        relu_near(0, 1)
+        group_a(0, 1, "s")
+        for t in range(4):
+            stage1(1, t)
+        relu_near(0, 0)
+
+        turned = {1: R3, 2: L1}
+        fresh = {2: R3, 3: L1}
+        for k in range(1, LAST):
             for t in range(4):
                 add_prior(k, t)
-            group_a(k - 1, 0, 1, "g")
-            group_a(k - 1, 1, 2, "g")
-            for half in range(2):
-                transpose_z(k - 1, half)
-                copy_b(k - 1, half)
-            group_a(k - 1, 2, 4, "s")
+            group_a(k - 1, 0, "g")
             if k == 1:
+                for s in range(4):
+                    rows(R1, s)
+            turn_z(k - 1, 0)
+            turn_z(k - 1, 1)
+            if k == 1:
+                load_y()
+                load_block(L1)
+                load_prior(4)
+                load_near(1, 0)
                 load_v()
-                load_prior(0, 3)
-                load_prior(1, 2)
+                load_prior(5)
             if k == 2:
-                load_prior(1, 3)
-            key = fresh.get(k)
-            if key is not None:
-                quantize_right(key[1], 0)
-                quantize_right(key[1], 1)
-            if k < last:
-                for t in range(4):
-                    stage1(k + 1, t)
-            relu_near(k, 0, 2)
-            quantize_b(k - 1)
-            if k == 1:
-                quantize_y(0)
-                group_y(1)
-            if k == 2:
-                quantize_y(1)
-            quantize_a(k - 1)
-            key = ahead.get(k)
-            if key is not None:
-                for t in range(4):
-                    rows(key, t)
+                load_prior(6)
+                load_near(1, 1)
             if k == 3:
-                for s in range(4):
-                    receptor(0, s)
-            if k == 4:
-                for s in range(4):
-                    receptor(1, s)
+                load_prior(7)
+            if k in fresh:
+                quantize_rows(fresh[k], 0)
+                quantize_rows(fresh[k], 1)
+            quantize_a(k - 1, 1)
             if k == 5:
-                ligand_open(0, 0, False)
-                ligand_open(0, 1, False)
-            if k == 6:
-                ligand_close(0, 0)
-                ligand_close(0, 1)
-                ligand(0, 2)
+                quantize_y(1)
+            if k == 2:
+                for t in range(4):
+                    widen_y(0, t)
+            if k == 3:
+                group_y(0, 0)
+                group_y(0, 1)
+            if k == 4:
+                quantize_b(k - 1)
+                group_y(1, 0)
+            relu_near(k, 1)
+            if k == 1:
+                quantize_rows(R1, 0)
+                quantize_rows(R1, 1)
+                rows(R3, 0)
+                rows(R3, 1)
+            quantize_a(k - 1, 0)
+            for t in range(4):
+                stage1(k + 1, t)
+            if k == 4:
+                quantize_y(0)
+            else:
+                quantize_b(k - 1)
+            if k == 5:
                 ligand(0, 3)
-            relu_near(k, 2, 4)
+            if k == 6:
+                for j in (0, 1):
+                    receptor(0, j)
+            group_a(k, 1, "s")
+            if k in turned:
+                for t in range(2 if k == 1 else 0, 4):
+                    rows(turned[k], t)
+            if k == 3:
+                for t in range(4):
+                    widen_y(1, t)
+            if k == 4:
+                ligand(0, 0)
+                group_y(1, 1)
+                ligand(0, 1)
+                ligand(0, 2)
+            if k == 5:
+                for j in (2, 3):
+                    receptor(0, j)
+            if k == 6:
+                for j in (2, 3, 0, 1):
+                    receptor(2, j)
+            relu_near(k, 0)
+
+        k = LAST
+        lig_banks = {}
+
+        def open_ligand(t):
+            lig_banks[t] = s1_bank(t)
+            ligand_passes(lig_banks[t], 1, t, (0, 2))
+
+        def close_ligand(t, on_vector=False):
+            ligand_passes(lig_banks[t], 1, t, (1, 3))
+            finish(lig_banks[t], "l", 1, t, on_vector)
 
         for t in range(4):
-            ligand_open(1, t, True)
-        receptor(2, 0)
-        transpose_z(last, 0)
-        copy_b(last, 0)
-        receptor(2, 1)
-        receptor(2, 2)
-        transpose_z(last, 1)
-        group_a(last, 0, 1, "v")
-        quantize_b(last, 0, 1)
-        group_a(last, 1, 2, "v")
-        quantize_a(last, 0, 1)
-        copy_b(last, 1)
-        group_a(last, 3, 4, "s")
-        for t in range(4):
-            ligand_passes(lig_banks[1, t], 1, t, [2])
-        receptor(2, 3)
-        group_a(last, 2, 3, "v")
-        quantize_a(last, 1, 2)
-        ligand_close(1, 0, True)
-        ligand_close(1, 1)
-        quantize_b(last, 1, 2)
-        receptor(3, 0, True)
-        quantize_a(last, 2, 4)
+            add_prior(k, t)
+        group_a(k - 1, 0, "g")
+        turn_z(k - 1, 0)
+        turn_z(k - 1, 1)
+        quantize_a(k - 1, 1)
+        quantize_a(k - 1, 0)
+        open_ligand(0)
+        open_ligand(1)
+        relu_near(k, 0, 0, 2)
+        relu_near(k, 1, 0, 2)
+        for j in (2, 3, 0, 1):
+            receptor(1, j)
+        quantize_b(k - 1)
+        turn_z(k, 0)
+        relu_near(k, 0, 2, 4)
+        open_ligand(2)
+        open_ligand(3)
+        relu_near(k, 1, 2, 4)
+        group_a(k, 0, "s")
+        quantize_b(k, 0, 1)
+        turn_z(k, 1, True)
+        close_ligand(0)
+        close_ligand(1)
+        group_a(k, 1, "v")
+        quantize_a(k, 0)
+        quantize_b(k, 1, 2)
+        quantize_a(k, 1)
+        receptor(3, 0)
+        close_ligand(2, True)
         receptor(3, 1)
-        ligand_close(1, 2, True)
-        ligand_close(1, 3)
-        receptor(3, 2, True)
-        receptor(3, 3)
+        close_ligand(3, True)
+        receptor(3, 2)
+        receptor(3, 3, True)

@@ -42,8 +42,7 @@ def tile_pair_tensor_messages_s8_kernel(
     with ExitStack() as ctx:
         keep = ctx.enter_context(tc.tile_pool(name="keep", bufs=1))
         work = ctx.enter_context(tc.tile_pool(name="work", bufs=2))
-        s1_pool = ctx.enter_context(tc.psum_pool(name="s1", bufs=1))
-        w_pool = ctx.enter_context(tc.psum_pool(name="w", bufs=4))
+        psum = ctx.enter_context(tc.psum_pool(name="psum", bufs=1))
         ctx.enter_context(tc.manual_schedule())
 
         ident = keep.tile([P, P], F32, name="ident", align_bytes=64)
@@ -59,18 +58,13 @@ def tile_pair_tensor_messages_s8_kernel(
         yc = [keep.tile([P, R], U32, name=f"yc{g}", align_bytes=64) for g in range(2)]
         ys = [keep.tile([P, R], U8, name=f"ys{g}", align_bytes=64) for g in range(2)]
         za_c, za_s, zb_c, zb_s = {}, {}, {}, {}
-        for g, b in ORDER:
-            za_c[g, b] = keep.tile([P, 4, P], U32, name=f"zac{g}{b}", align_bytes=64)
-            za_s[g, b] = keep.tile([P, 4, P], U8, name=f"zas{g}{b}", align_bytes=64)
-            zb_c[g, b] = keep.tile([P, 4, P], U32, name=f"zbc{g}{b}", align_bytes=64)
-            zb_s[g, b] = keep.tile([P, 4, P], U8, name=f"zbs{g}{b}", align_bytes=64)
 
         raws, priors, nears = {}, {}, {}
 
         def load_rows(key, t):
             side, g = key
             view = left_v if side == "l" else right_v
-            raw = work.tile([P, K], BF16, name="raw", tag="raw", bufs=9, align_bytes=64)
+            raw = work.tile([P, K], BF16, name="raw", tag="raw", bufs=8, align_bytes=64)
             nc.sync.dma_start(out=raw[:], in_=view[g, :, t, :])
             raws[key, t] = raw
 
@@ -85,8 +79,17 @@ def tile_pair_tensor_messages_s8_kernel(
             nc.sync.dma_start(out=near_t[:], in_=near_v[g, :, :, W * c : W * (c + 1)])
             nears[g, c] = near_t
 
-        def new_bank(shape):
-            return w_pool.tile(shape, F32, name="bank", tag="bank", bufs=4)
+        ring = [4, 5, 6, 7]
+
+        def bank_tile(n, shape):
+            return psum.tile(shape, F32, name=f"bank{n}", tag=f"bank{n}", bufs=1)
+
+        def new_bank(shape, hold=False):
+            n = ring[0]
+            ring.remove(n)
+            if not hold:
+                ring.append(n)
+            return bank_tile(n, shape)
 
         def copy(on_vector, dst, src):
             if on_vector:
@@ -94,15 +97,23 @@ def tile_pair_tensor_messages_s8_kernel(
             else:
                 nc.scalar.copy(out=dst, in_=src)
 
-        grouped = {}
+        grouped, sorted_rows = {}, {}
+
+        def sort_words(key, t):
+            srt = work.tile([P, 2, 2, P], F32, name="srt", tag="srt", bufs=3, align_bytes=64)
+            words = raws[key, t][:].bitcast(F32).rearrange("p (h x u) -> p h u x", h=2, u=2)
+            nc.vector.tensor_copy(out=srt[:], in_=words)
+            sorted_rows[key, t] = srt
 
         def rows(key, t, on_vector=False):
             side, g = key
-            words = raws[key, t][:].bitcast(F32)
+            words = raws[key, t][:].bitcast(F32).rearrange("p (h x u) -> p h u x", h=2, u=2)
+            if (key, t) in sorted_rows:
+                words = sorted_rows[key, t][:]
             bank = new_bank([P, 2, 2, P])
             for h in range(2):
                 for u in range(2):
-                    nc.tensor.transpose(bank[:, h, u, :], words[:, 256 * h + u : 256 * (h + 1) : 2], ident[:])
+                    nc.tensor.transpose(bank[:, h, u, :], words[:, h, u, :], ident[:])
             if t == 0:
                 grouped[key] = work.tile([P, 8, 2 * P], F32, name="rin", tag="rin", bufs=3, align_bytes=64)
             if side == "l":
@@ -137,7 +148,7 @@ def tile_pair_tensor_messages_s8_kernel(
         s1_banks = {}
 
         def s1_bank(t):
-            return s1_pool.tile([P, W], F32, name="s1b", tag=f"s1b{t}", bufs=1)
+            return bank_tile(t, [P, W])
 
         def stage1(k, t):
             g, b = ORDER[k]
@@ -176,7 +187,7 @@ def tile_pair_tensor_messages_s8_kernel(
             )
 
         def group_a(k, u, engine):
-            zis[k, u] = work.tile([P, 2, P, 4], BF16, name="zi", tag="zi", bufs=4, align_bytes=64)
+            zis[k, u] = work.tile([P, 2, P, 4], BF16, name="zi", tag="zi", bufs=12, align_bytes=64)
             if engine == "g":
                 dst = zis[k, u][:]
                 src = zs[k, u][:].rearrange("p t (q e) -> p e q t", e=2)
@@ -188,6 +199,9 @@ def tile_pair_tensor_messages_s8_kernel(
 
         def quantize_a(k, u):
             g, b = ORDER[k]
+            if (g, b) not in za_c:
+                za_c[g, b] = work.tile([P, 4, P], U32, name="zac", tag="zac", bufs=5, align_bytes=64)
+                za_s[g, b] = work.tile([P, 4, P], U8, name="zas", tag="zas", bufs=5, align_bytes=64)
             quantize(
                 za_c[g, b][:, 2 * u : 2 * u + 2].rearrange("p j q -> p (j q)"),
                 za_s[g, b][:, 2 * u : 2 * u + 2].rearrange("p j q -> p (j q)"),
@@ -206,6 +220,9 @@ def tile_pair_tensor_messages_s8_kernel(
 
         def quantize_b(k, h0=0, h1=2):
             g, b = ORDER[k]
+            if h0 == 0:
+                zb_c[g, b] = work.tile([P, 4, P], U32, name="zbc", tag="zbc", bufs=5, align_bytes=64)
+                zb_s[g, b] = work.tile([P, 4, P], U8, name="zbs", tag="zbs", bufs=5, align_bytes=64)
             quantize(
                 zb_c[g, b][:, 2 * h0 : 2 * h1].rearrange("q t p -> q (t p)"),
                 zb_s[g, b][:, 2 * h0 : 2 * h1].rearrange("q t p -> q (t p)"),
@@ -213,7 +230,7 @@ def tile_pair_tensor_messages_s8_kernel(
             )
 
         def finish(bank, kind, g, t, on_vector=False):
-            o = work.tile([P, R], F32, name="o", tag="o", bufs=8, align_bytes=64)
+            o = work.tile([P, R], F32, name="o", tag="o", bufs=6, align_bytes=64)
             copy(on_vector, o[:], bank[:])
             nc.sync.dma_start(out=out_v[kind][g, :, t, :], in_=o[:])
 
@@ -246,10 +263,20 @@ def tile_pair_tensor_messages_s8_kernel(
                     stop=(b == 3),
                 )
 
-        def ligand(g, t, on_vector=False):
-            bank = new_bank([P, R])
-            ligand_passes(bank, g, t, (0, 2, 1, 3))
+        held = {}
+
+        def open_ligand(g, t, blocks):
+            held[g, t] = ring[0], new_bank([P, R], hold=True)
+            ligand_passes(held[g, t][1], g, t, blocks)
+
+        def more_ligand(g, t, blocks):
+            ligand_passes(held[g, t][1], g, t, blocks)
+
+        def close_ligand(g, t, blocks, on_vector=False):
+            n, bank = held[g, t]
+            ligand_passes(bank, g, t, blocks)
             finish(bank, "l", g, t, on_vector)
+            ring.append(n)
 
         y_codes = keep.tile([P, 2, 4, R], U8, name="y_codes", align_bytes=64)
         y_sc = keep.tile([P, 2, 4], F32, name="y_sc", align_bytes=64)
@@ -261,7 +288,7 @@ def tile_pair_tensor_messages_s8_kernel(
 
         def widen_y(g, t):
             if t == 0:
-                y_plane[g] = work.tile([P, 4, R], BF16, name="y_plane", tag="y_plane", bufs=2, align_bytes=64)
+                y_plane[g] = work.tile([P, 4, R], BF16, name="y_plane", tag="y_plane", bufs=1, align_bytes=64)
             nc.scalar.activation(
                 y_plane[g][:, t, :], y_codes[:, g, t, :].bitcast(FP8), COPY, scale=y_sc[:, g, t : t + 1]
             )
@@ -301,172 +328,208 @@ def tile_pair_tensor_messages_s8_kernel(
         for t in range(1, 4):
             load_rows(L0, t)
         load_prior(0, 0, 2)
-        load_prior(0, 2, 4)
 
-        rows(L0, 0, True)
+        sort_words(L0, 0)
+        sort_words(R0, 0)
+        rows(L0, 0)
+        sort_words(R0, 1)
         rows(R0, 0)
+        sort_words(R0, 2)
         rows(R0, 1)
         quantize_left(0, 0, 1)
+        sort_words(R0, 3)
         rows(R0, 2)
-        load_block(R2)
+        sort_words(L0, 1)
+        rows(R0, 3)
+        load_rows(R2, 0)
+        load_prior(0, 2, 4)
+        for s in range(1, 4):
+            load_rows(R2, s)
         load_near(0, 0)
-        load_prior(1)
         for h in range(2):
             quantize_right(0, h, 0, 2)
-        rows(R0, 3, True)
+        sort_words(L0, 2)
         rows(L0, 1)
         for h in range(2):
-            quantize_right(0, h, 2, 4)
+            quantize_right(0, h, 2, 3)
+        sort_words(L0, 3)
         rows(L0, 2)
-        quantize_left(0, 1, 2)
+        for h in range(2):
+            quantize_right(0, h, 3, 4)
         rows(L0, 3)
         load_block(R1)
-        load_prior(2)
+        load_prior(1)
+        quantize_left(0, 1, 2)
         stage1(0, 0)
-        stage1(0, 1)
+        sort_words(R2, 0)
         quantize_left(0, 2, 3)
+        stage1(0, 1)
         add_prior(0, 0)
-        rows(R2, 0)
+        sort_words(R2, 1)
         quantize_left(0, 3, 4)
-        add_prior(0, 1)
-        rows(R2, 1)
         stage1(0, 2)
-        stage1(0, 3)
+        rows(R2, 0)
+        rows(R2, 1)
+        add_prior(0, 1)
+        sort_words(R2, 2)
+        sort_words(R2, 3)
         rows(R2, 2)
         rows(R2, 3)
         add_prior(0, 2)
-        add_prior(0, 3)
-        load_block(R3)
-        load_near(0, 1)
-        load_prior(3)
+        stage1(0, 3)
         for h in range(2):
             quantize_right(2, h, 0, 2)
+        add_prior(0, 3)
+        load_block(R3)
+        load_y()
+        load_prior(2)
         for h in range(2):
             quantize_right(2, h, 2, 4)
+        rows(R1, 0)
+        rows(R1, 1)
         relu_near(0, 1)
+        stage1(1, 0)
+        stage1(1, 1)
+        rows(R1, 2)
+        rows(R1, 3)
         group_a(0, 1, "s")
-        for t in range(4):
-            stage1(1, t)
         relu_near(0, 0)
 
-        turned = {1: R3, 2: L1}
-        fresh = {2: R3, 3: L1}
-        for k in range(1, LAST):
+        fresh = {1: R1, 2: R3, 3: L1}
+        for k in range(1, 4):
+            stage1(k, 2)
+            stage1(k, 3)
             for t in range(4):
                 add_prior(k, t)
             group_a(k - 1, 0, "g")
-            if k == 1:
-                for s in range(4):
-                    rows(R1, s)
             turn_z(k - 1, 0)
             turn_z(k - 1, 1)
             if k == 1:
-                load_y()
                 load_block(L1)
+                load_near(0, 1)
+                load_prior(3)
+                load_v()
                 load_prior(4)
                 load_near(1, 0)
-                load_v()
-                load_prior(5)
             if k == 2:
-                load_prior(6)
+                load_prior(5)
                 load_near(1, 1)
             if k == 3:
+                load_prior(6)
+            quantize_rows(fresh[k], 0)
+            quantize_rows(fresh[k], 1)
+            if k < 3:
+                rows(fresh[k + 1], 0)
+                rows(fresh[k + 1], 1)
+            else:
+                open_ligand(0, 0, (0, 2))
+                open_ligand(0, 1, (0, 2))
+                group_y(0, 1)
+                widen_y(1, 0)
+                widen_y(1, 1)
+            if k == 2:
+                widen_y(0, 2)
+                widen_y(0, 3)
+            relu_near(k, 1)
+            quantize_b(k - 1)
+            stage1(k + 1, 0)
+            stage1(k + 1, 1)
+            group_a(k, 1, "s")
+            if k < 3:
+                rows(fresh[k + 1], 2)
+                rows(fresh[k + 1], 3)
+            if k == 1:
+                widen_y(0, 0)
+                widen_y(0, 1)
+            if k == 2:
+                group_y(0, 0)
+            if k == 3:
+                widen_y(1, 2)
+                widen_y(1, 3)
+            relu_near(k, 0)
+        stage1(4, 2)
+        stage1(4, 3)
+        more_ligand(0, 0, (1,))
+        more_ligand(0, 1, (1,))
+
+        for k in range(4, LAST):
+            for t in range(4):
+                add_prior(k, t)
+            group_a(k - 1, 0, "g")
+            turn_z(k - 1, 0)
+            turn_z(k - 1, 1)
+            if k == 4:
                 load_prior(7)
-            if k in fresh:
-                quantize_rows(fresh[k], 0)
-                quantize_rows(fresh[k], 1)
-            quantize_a(k - 1, 1)
+                quantize_y(0)
+                group_y(1, 0)
+                group_y(1, 1)
             if k == 5:
                 quantize_y(1)
-            if k == 2:
-                for t in range(4):
-                    widen_y(0, t)
-            if k == 3:
-                group_y(0, 0)
-                group_y(0, 1)
-            if k == 4:
-                quantize_b(k - 1)
-                group_y(1, 0)
+                quantize_a(4, 1)
+                quantize_a(0, 1)
+            if k == 6:
+                quantize_a(5, 1)
+                quantize_a(1, 1)
             relu_near(k, 1)
-            if k == 1:
-                quantize_rows(R1, 0)
-                quantize_rows(R1, 1)
-                rows(R3, 0)
-                rows(R3, 1)
-            quantize_a(k - 1, 0)
             for t in range(4):
                 stage1(k + 1, t)
-            if k == 4:
-                quantize_y(0)
-            else:
-                quantize_b(k - 1)
-            if k == 5:
-                ligand(0, 3)
-            if k == 6:
-                for j in (0, 1):
-                    receptor(0, j)
             group_a(k, 1, "s")
-            if k in turned:
-                for t in range(2 if k == 1 else 0, 4):
-                    rows(turned[k], t)
-            if k == 3:
-                for t in range(4):
-                    widen_y(1, t)
             if k == 4:
-                ligand(0, 0)
-                group_y(1, 1)
-                ligand(0, 1)
-                ligand(0, 2)
-            if k == 5:
-                for j in (2, 3):
-                    receptor(0, j)
-            if k == 6:
+                quantize_b(3)
+                close_ligand(0, 0, (3,))
+                close_ligand(0, 1, (3,))
+                for t in (2, 3):
+                    open_ligand(0, t, (0, 2, 1))
+                    close_ligand(0, t, (3,))
+            else:
+                quantize_a(k - 1, 0)
+                quantize_a(k - 5, 0)
+                quantize_b(k - 1)
                 for j in (2, 3, 0, 1):
-                    receptor(2, j)
+                    receptor(ORDER[k - 1][1], j)
+            if k == 6:
+                open_ligand(1, 0, (0, 2))
+                open_ligand(1, 1, (0, 2))
+                quantize_a(2, 1)
+                quantize_a(6, 1)
             relu_near(k, 0)
 
         k = LAST
-        lig_banks = {}
-
-        def open_ligand(t):
-            lig_banks[t] = s1_bank(t)
-            ligand_passes(lig_banks[t], 1, t, (0, 2))
-
-        def close_ligand(t, on_vector=False):
-            ligand_passes(lig_banks[t], 1, t, (1, 3))
-            finish(lig_banks[t], "l", 1, t, on_vector)
-
         for t in range(4):
             add_prior(k, t)
         group_a(k - 1, 0, "g")
         turn_z(k - 1, 0)
         turn_z(k - 1, 1)
-        quantize_a(k - 1, 1)
+        ring.extend([0, 1, 2, 3])
+        receptor(1, 2)
+        receptor(1, 3)
+        quantize_a(2, 0)
         quantize_a(k - 1, 0)
-        open_ligand(0)
-        open_ligand(1)
-        relu_near(k, 0, 0, 2)
-        relu_near(k, 1, 0, 2)
-        for j in (2, 3, 0, 1):
-            receptor(1, j)
-        quantize_b(k - 1)
-        turn_z(k, 0)
-        relu_near(k, 0, 2, 4)
-        open_ligand(2)
-        open_ligand(3)
-        relu_near(k, 1, 2, 4)
+        open_ligand(1, 2, (0, 2))
+        open_ligand(1, 3, (0, 2))
+        relu_near(k, 0)
         group_a(k, 0, "s")
-        quantize_b(k, 0, 1)
-        turn_z(k, 1, True)
-        close_ligand(0)
-        close_ligand(1)
-        group_a(k, 1, "v")
+        receptor(1, 0)
+        receptor(1, 1)
+        quantize_b(k - 1)
+        relu_near(k, 1, 0, 2)
+        quantize_a(3, 0)
+        turn_z(k, 0)
+        relu_near(k, 1, 2, 4)
+        for t in range(4):
+            more_ligand(1, t, (1,))
         quantize_a(k, 0)
-        quantize_b(k, 1, 2)
-        quantize_a(k, 1)
+        group_a(k, 1, "v")
+        quantize_b(k, 0, 1)
+        turn_z(k, 1)
         receptor(3, 0)
-        close_ligand(2, True)
-        receptor(3, 1)
-        close_ligand(3, True)
+        quantize_a(3, 1)
+        quantize_a(k, 1)
+        close_ligand(1, 0, (3,), True)
+        close_ligand(1, 1, (3,))
+        quantize_b(k, 1, 2)
+        receptor(3, 1, True)
+        close_ligand(1, 2, (3,))
+        close_ligand(1, 3, (3,), True)
         receptor(3, 2)
         receptor(3, 3, True)

@@ -45,6 +45,8 @@ def tile_pair_tensor_messages_s8_kernel(
         psum = ctx.enter_context(tc.psum_pool(name="psum", bufs=1))
         ctx.enter_context(tc.manual_schedule())
 
+        idle = keep.tile([P, W], BF16, name="idle", align_bytes=64)
+        nc.vector.memset(idle[:], 0.0)
         ident = keep.tile([P, P], F32, name="ident", align_bytes=64)
         make_identity(nc, ident[:])
         v_tile = keep.tile([P, 4, 2 * R], U8, name="v_tile", align_bytes=64)
@@ -169,8 +171,14 @@ def tile_pair_tensor_messages_s8_kernel(
 
         def add_prior(k, t):
             if t == 0:
-                sums[k] = work.tile([P, 4, W], F32, name="sum_t", tag="sum_t", bufs=2, align_bytes=64)
-            nc.vector.tensor_tensor(out=sums[k][:, t, :], in0=s1_banks[k, t][:], in1=priors[k][:, t, :], op=ADD)
+                sums[k] = work.tile([P, 2, 4, 2 * P], F32, name="sum_t", tag="sum_t", bufs=2, align_bytes=64)
+            by_parity = "p (q u e) -> p u q e"
+            nc.vector.tensor_tensor(
+                out=sums[k][:, :, t, :].rearrange("p u (q e) -> p u q e", e=2),
+                in0=s1_banks[k, t][:].rearrange(by_parity, u=2, e=2),
+                in1=priors[k][:, t, :].rearrange(by_parity, u=2, e=2),
+                op=ADD,
+            )
 
         def relu_near(k, u, t0=0, t1=4):
             g, b = ORDER[k]
@@ -179,7 +187,7 @@ def tile_pair_tensor_messages_s8_kernel(
             pairs = "p t (q u e) -> p (t q) u e"
             nc.vector.scalar_tensor_tensor(
                 out=zs[k, u][:, t0:t1].rearrange("p t (q e) -> p (t q) e", e=2),
-                in0=sums[k][:, t0:t1].rearrange(pairs, u=2, e=2)[:, :, u, :],
+                in0=sums[k][:, u, t0:t1].rearrange("p t (q e) -> p (t q) e", e=2),
                 scalar=0.0,
                 in1=nears[g, b % 2][:, t0:t1].rearrange(pairs, u=2, e=2)[:, :, u, :],
                 op0=MAX,
@@ -187,25 +195,26 @@ def tile_pair_tensor_messages_s8_kernel(
             )
 
         def group_a(k, u, engine):
-            zis[k, u] = work.tile([P, 2, P, 4], BF16, name="zi", tag="zi", bufs=12, align_bytes=64)
+            if k not in zis:
+                zis[k] = work.tile([P, 2, 2, P, 4], BF16, name="zi", tag="zi", bufs=6, align_bytes=64)
             if engine == "g":
-                dst = zis[k, u][:]
+                dst = zis[k][:, u]
                 src = zs[k, u][:].rearrange("p t (q e) -> p e q t", e=2)
                 nc.gpsimd.tensor_scalar(out=dst, in0=src, scalar1=1.0, scalar2=0.0, op0=MULT, op1=ADD)
             else:
-                dst = zis[k, u][:].rearrange("p e (c i) t -> p c t i e", i=2)
+                dst = zis[k][:, u].rearrange("p e (c i) t -> p c t i e", i=2)
                 src = zs[k, u][:].rearrange("p t (c i e) -> p c t i e", i=2, e=2)
                 copy(engine == "v", dst, src)
 
-        def quantize_a(k, u):
+        def quantize_a(k, u0=0, u1=2):
             g, b = ORDER[k]
             if (g, b) not in za_c:
-                za_c[g, b] = work.tile([P, 4, P], U32, name="zac", tag="zac", bufs=5, align_bytes=64)
-                za_s[g, b] = work.tile([P, 4, P], U8, name="zas", tag="zas", bufs=5, align_bytes=64)
+                za_c[g, b] = work.tile([P, 4, P], U32, name="zac", tag="zac", bufs=7, align_bytes=64)
+                za_s[g, b] = work.tile([P, 4, P], U8, name="zas", tag="zas", bufs=7, align_bytes=64)
             quantize(
-                za_c[g, b][:, 2 * u : 2 * u + 2].rearrange("p j q -> p (j q)"),
-                za_s[g, b][:, 2 * u : 2 * u + 2].rearrange("p j q -> p (j q)"),
-                zis[k, u][:].rearrange("p e q t -> p (e q t)"),
+                za_c[g, b][:, 2 * u0 : 2 * u1].rearrange("p j q -> p (j q)"),
+                za_s[g, b][:, 2 * u0 : 2 * u1].rearrange("p j q -> p (j q)"),
+                zis[k][:, u0:u1].rearrange("p u e q t -> p (u e q t)"),
             )
 
         def turn_z(k, half, on_vector=False):
@@ -323,90 +332,89 @@ def tile_pair_tensor_messages_s8_kernel(
             for t in range(4):
                 load_rows(key, t)
 
+        def warm_up(n, width=W, bank_no=3):
+            bank = bank_tile(bank_no, [P, W])
+            for i in range(n):
+                nc.tensor.matmul(out=bank[:, :width], lhsT=idle[:, :P], rhs=idle[:, :width], start=True, stop=True)
+
         load_rows(L0, 0)
         load_block(R0)
         for t in range(1, 4):
             load_rows(L0, t)
         load_prior(0, 0, 2)
 
+        warm_up(5)
         sort_words(L0, 0)
         sort_words(R0, 0)
         rows(L0, 0)
+        warm_up(1, 320)
         sort_words(R0, 1)
         rows(R0, 0)
+        warm_up(1, 320)
         sort_words(R0, 2)
         rows(R0, 1)
+        warm_up(1, 320)
         quantize_left(0, 0, 1)
         sort_words(R0, 3)
         rows(R0, 2)
+        warm_up(1, 320)
         sort_words(L0, 1)
         rows(R0, 3)
-        load_rows(R2, 0)
+        warm_up(1, 320)
         load_prior(0, 2, 4)
-        for s in range(1, 4):
-            load_rows(R2, s)
         load_near(0, 0)
+        load_block(R2)
         for h in range(2):
             quantize_right(0, h, 0, 2)
         sort_words(L0, 2)
         rows(L0, 1)
+        warm_up(1, 320)
         for h in range(2):
-            quantize_right(0, h, 2, 3)
-        sort_words(L0, 3)
+            quantize_right(0, h, 2, 4)
         rows(L0, 2)
-        for h in range(2):
-            quantize_right(0, h, 3, 4)
         rows(L0, 3)
-        load_block(R1)
-        load_prior(1)
         quantize_left(0, 1, 2)
         stage1(0, 0)
-        sort_words(R2, 0)
-        quantize_left(0, 2, 3)
+        load_prior(1)
+        load_block(R1)
         stage1(0, 1)
+        quantize_left(0, 2, 3)
         add_prior(0, 0)
-        sort_words(R2, 1)
-        quantize_left(0, 3, 4)
         stage1(0, 2)
-        rows(R2, 0)
-        rows(R2, 1)
+        quantize_left(0, 3, 4)
         add_prior(0, 1)
-        sort_words(R2, 2)
-        sort_words(R2, 3)
+        stage1(0, 3)
+        add_prior(0, 2)
+        rows(R2, 0)
+        add_prior(0, 3)
+        rows(R2, 1)
         rows(R2, 2)
         rows(R2, 3)
-        add_prior(0, 2)
-        stage1(0, 3)
+        load_y()
+        load_block(R3)
+        load_prior(2)
+        load_near(0, 1)
+        relu_near(0, 1)
         for h in range(2):
             quantize_right(2, h, 0, 2)
-        add_prior(0, 3)
-        load_block(R3)
-        load_y()
-        load_prior(2)
+        group_a(0, 1, "s")
         for h in range(2):
             quantize_right(2, h, 2, 4)
+        warm_up(2)
         rows(R1, 0)
-        rows(R1, 1)
-        relu_near(0, 1)
-        stage1(1, 0)
-        stage1(1, 1)
-        rows(R1, 2)
-        rows(R1, 3)
-        group_a(0, 1, "s")
+        for t in range(4):
+            stage1(1, t)
         relu_near(0, 0)
 
         fresh = {1: R1, 2: R3, 3: L1}
         for k in range(1, 4):
-            stage1(k, 2)
-            stage1(k, 3)
             for t in range(4):
                 add_prior(k, t)
             group_a(k - 1, 0, "g")
-            turn_z(k - 1, 0)
-            turn_z(k - 1, 1)
+            for t in range(1 if k == 1 else 3, 4):
+                rows(fresh[k], t)
             if k == 1:
                 load_block(L1)
-                load_near(0, 1)
                 load_prior(3)
                 load_v()
                 load_prior(4)
@@ -416,41 +424,47 @@ def tile_pair_tensor_messages_s8_kernel(
                 load_near(1, 1)
             if k == 3:
                 load_prior(6)
-            quantize_rows(fresh[k], 0)
-            quantize_rows(fresh[k], 1)
+            if k > 1:
+                quantize_b(k - 2)
             if k < 3:
+                quantize_a(k - 1)
+            else:
+                quantize_y(0)
+            if k < 3:
+                turn_z(k - 1, 0)
+                turn_z(k - 1, 1)
+                warm_up(2, 512, 3)
                 rows(fresh[k + 1], 0)
                 rows(fresh[k + 1], 1)
             else:
+                turn_z(k - 1, 0)
+                turn_z(k - 1, 1)
                 open_ligand(0, 0, (0, 2))
                 open_ligand(0, 1, (0, 2))
-                group_y(0, 1)
-                widen_y(1, 0)
-                widen_y(1, 1)
-            if k == 2:
-                widen_y(0, 2)
-                widen_y(0, 3)
-            relu_near(k, 1)
-            quantize_b(k - 1)
-            stage1(k + 1, 0)
-            stage1(k + 1, 1)
-            group_a(k, 1, "s")
-            if k < 3:
-                rows(fresh[k + 1], 2)
-                rows(fresh[k + 1], 3)
             if k == 1:
-                widen_y(0, 0)
-                widen_y(0, 1)
+                relu_near(k, 1)
+            quantize_rows(fresh[k], 0)
+            quantize_rows(fresh[k], 1)
+            if k > 1:
+                relu_near(k, 1)
+            for t in range(3):
+                stage1(k + 1, t)
             if k == 2:
                 group_y(0, 0)
+                group_y(0, 1)
+            else:
+                for t in range(4):
+                    widen_y(k // 2, t)
             if k == 3:
-                widen_y(1, 2)
-                widen_y(1, 3)
+                quantize_b(2)
+            if k < 3:
+                rows(fresh[k + 1], 2)
+            group_a(k, 1, "s")
+            stage1(k + 1, 3)
             relu_near(k, 0)
-        stage1(4, 2)
-        stage1(4, 3)
         more_ligand(0, 0, (1,))
         more_ligand(0, 1, (1,))
+        group_y(1, 0)
 
         for k in range(4, LAST):
             for t in range(4):
@@ -460,38 +474,31 @@ def tile_pair_tensor_messages_s8_kernel(
             turn_z(k - 1, 1)
             if k == 4:
                 load_prior(7)
-                quantize_y(0)
-                group_y(1, 0)
+                quantize_a(2)
                 group_y(1, 1)
-            if k == 5:
-                quantize_y(1)
-                quantize_a(4, 1)
-                quantize_a(0, 1)
-            if k == 6:
-                quantize_a(5, 1)
-                quantize_a(1, 1)
+            if k > 4:
+                quantize_a(k - 1)
             relu_near(k, 1)
             for t in range(4):
                 stage1(k + 1, t)
             group_a(k, 1, "s")
             if k == 4:
                 quantize_b(3)
+                quantize_y(1)
                 close_ligand(0, 0, (3,))
                 close_ligand(0, 1, (3,))
                 for t in (2, 3):
                     open_ligand(0, t, (0, 2, 1))
                     close_ligand(0, t, (3,))
             else:
-                quantize_a(k - 1, 0)
-                quantize_a(k - 5, 0)
                 quantize_b(k - 1)
-                for j in (2, 3, 0, 1):
+                for j in range(4):
                     receptor(ORDER[k - 1][1], j)
             if k == 6:
                 open_ligand(1, 0, (0, 2))
                 open_ligand(1, 1, (0, 2))
-                quantize_a(2, 1)
-                quantize_a(6, 1)
+                quantize_a(3)
+                quantize_a(6, 1, 2)
             relu_near(k, 0)
 
         k = LAST
@@ -500,11 +507,11 @@ def tile_pair_tensor_messages_s8_kernel(
         group_a(k - 1, 0, "g")
         turn_z(k - 1, 0)
         turn_z(k - 1, 1)
-        ring.extend([0, 1, 2, 3])
+        ring.clear()
+        ring.extend([0, 1, 2, 3, 4, 5])
         receptor(1, 2)
         receptor(1, 3)
-        quantize_a(2, 0)
-        quantize_a(k - 1, 0)
+        quantize_a(k - 1, 0, 1)
         open_ligand(1, 2, (0, 2))
         open_ligand(1, 3, (0, 2))
         relu_near(k, 0)
@@ -513,23 +520,23 @@ def tile_pair_tensor_messages_s8_kernel(
         receptor(1, 1)
         quantize_b(k - 1)
         relu_near(k, 1, 0, 2)
-        quantize_a(3, 0)
-        turn_z(k, 0)
         relu_near(k, 1, 2, 4)
-        for t in range(4):
-            more_ligand(1, t, (1,))
-        quantize_a(k, 0)
+        more_ligand(1, 0, (1,))
+        more_ligand(1, 1, (1,))
+        turn_z(k, 0)
+        more_ligand(1, 2, (1,))
+        more_ligand(1, 3, (1,))
+        quantize_a(k, 0, 1)
         group_a(k, 1, "v")
         quantize_b(k, 0, 1)
-        turn_z(k, 1)
         receptor(3, 0)
-        quantize_a(3, 1)
-        quantize_a(k, 1)
-        close_ligand(1, 0, (3,), True)
-        close_ligand(1, 1, (3,))
+        receptor(3, 1)
+        quantize_a(k, 1, 2)
+        turn_z(k, 1, True)
+        close_ligand(1, 0, (3,))
+        close_ligand(1, 1, (3,), True)
         quantize_b(k, 1, 2)
-        receptor(3, 1, True)
-        close_ligand(1, 2, (3,))
-        close_ligand(1, 3, (3,), True)
         receptor(3, 2)
         receptor(3, 3, True)
+        close_ligand(1, 2, (3,))
+        close_ligand(1, 3, (3,), True)

@@ -24,6 +24,7 @@ P = 128
 W = 512
 ORDER = [(0, 0), (0, 2), (0, 1), (0, 3), (1, 0), (1, 2), (1, 1), (1, 3)]
 LAST = len(ORDER) - 1
+SINGLE_STORES = (("l", 1), ("r", 3))
 
 
 def tile_pair_tensor_messages_s8_kernel(
@@ -31,7 +32,7 @@ def tile_pair_tensor_messages_s8_kernel(
 ):
     nc = tc.nc
     left_v = left.rearrange("(g p t) d -> g p t d", p=P, t=4)
-    right_v = right.rearrange("(g s q) d -> g q s d", s=4, q=P)
+    right_v = right.rearrange("(g p t) d -> g p t d", p=P, t=4)
     prior_v = prior.rearrange("(g p t) m -> g p t m", p=P, t=4)
     near_v = near.rearrange("(g p t) m -> g p t m", p=P, t=4)
     out_v = {
@@ -63,12 +64,14 @@ def tile_pair_tensor_messages_s8_kernel(
 
         raws, priors, nears = {}, {}, {}
 
-        def load_rows(key, t):
+        def load_rows(key, t0, t1):
             side, g = key
             view = left_v if side == "l" else right_v
-            raw = work.tile([P, K], BF16, name="raw", tag="raw", bufs=8, align_bytes=64)
-            nc.sync.dma_start(out=raw[:], in_=view[g, :, t, :])
-            raws[key, t] = raw
+            n = t1 - t0
+            raw = work.tile([P, n, K], BF16, name="raw", tag=f"raw{n}", bufs=2 * n, align_bytes=64)
+            nc.sync.dma_start(out=raw[:], in_=view[g, :, t0:t1, :])
+            for t in range(t0, t1):
+                raws[key, t] = raw, t - t0
 
         def load_prior(k, t0=0, t1=4):
             g, b = ORDER[k]
@@ -101,28 +104,34 @@ def tile_pair_tensor_messages_s8_kernel(
 
         grouped, sorted_rows = {}, {}
 
-        def sort_words(key, t):
-            srt = work.tile([P, 2, 2, P], F32, name="srt", tag="srt", bufs=3, align_bytes=64)
-            words = raws[key, t][:].bitcast(F32).rearrange("p (h x u) -> p h u x", h=2, u=2)
-            nc.vector.tensor_copy(out=srt[:], in_=words)
-            sorted_rows[key, t] = srt
+        def word_runs(key, n):
+            if key[0] == "l":
+                raw, row = raws[key, n]
+                return raw[:, row, :].bitcast(F32).rearrange("p (a x w) -> p a w x", a=2, w=2)
+            raw = raws[key, 2 * (n // 2)][0]
+            words = raw[:].rearrange("p e d -> p (e d)").bitcast(F32)
+            return words.rearrange("p (a h x w) -> p h a w x", a=2, h=2, w=2)[:, n % 2]
 
-        def rows(key, t, on_vector=False):
-            side, g = key
-            words = raws[key, t][:].bitcast(F32).rearrange("p (h x u) -> p h u x", h=2, u=2)
-            if (key, t) in sorted_rows:
-                words = sorted_rows[key, t][:]
+        def sort_words(key, n):
+            srt = work.tile([P, 2, 2, P], F32, name="srt", tag="srt", bufs=3, align_bytes=64)
+            nc.vector.tensor_copy(out=srt[:], in_=word_runs(key, n))
+            sorted_rows[key, n] = srt
+
+        def rows(key, n, on_vector=False):
+            words = sorted_rows[key, n][:] if (key, n) in sorted_rows else word_runs(key, n)
             bank = new_bank([P, 2, 2, P])
-            for h in range(2):
-                for u in range(2):
-                    nc.tensor.transpose(bank[:, h, u, :], words[:, h, u, :], ident[:])
-            if t == 0:
-                grouped[key] = work.tile([P, 8, 2 * P], F32, name="rin", tag="rin", bufs=3, align_bytes=64)
-            if side == "l":
-                dst = grouped[key][:, 2 * t : 2 * t + 2, :]
+            for a in range(2):
+                for w in range(2):
+                    nc.tensor.transpose(bank[:, a, w, :], words[:, a, w, :], ident[:])
+            if n == 0:
+                grouped[key] = work.tile([P, 4, W], F32, name="rin", tag="rin", bufs=3, align_bytes=64)
+            if key[0] == "l":
+                dst = grouped[key][:, n, :].rearrange("x (a p w) -> x a p w", a=2, w=2)
+                src = bank[:].rearrange("x a w p -> x a p w")
             else:
-                dst = grouped[key][:, t : 8 : 4, :]
-            copy(on_vector, dst.rearrange("x h (p u) -> x h p u", u=2), bank[:].rearrange("x h u p -> x h p u"))
+                dst = grouped[key][:, 2 * (n % 2) + n // 2, :].rearrange("x (p a w) -> x p a w", a=2, w=2)
+                src = bank[:].rearrange("x a w p -> x p a w")
+            copy(on_vector, dst, src)
 
         def quantize(codes, scales, values):
             nc.vector.quantize_mx(out=codes.bitcast(FP8X4), scales=scales, in_=values)
@@ -131,14 +140,14 @@ def tile_pair_tensor_messages_s8_kernel(
             quantize(
                 lc[g][:, t0:t1].rearrange("x t h p -> x (t h p)"),
                 ls[g][:, t0:t1].rearrange("x t h p -> x (t h p)"),
-                grouped["l", g][:, 2 * t0 : 2 * t1].rearrange("x a w -> x (a w)").bitcast(BF16),
+                grouped["l", g][:, t0:t1].rearrange("x a w -> x (a w)").bitcast(BF16),
             )
 
-        def quantize_right(g, h, s0=0, s1=4):
+        def quantize_right(g, h, u0=0, u1=2):
             quantize(
-                rc[g][:, h, P * s0 : P * s1],
-                rs[g][:, h, P * s0 : P * s1],
-                grouped["r", g][:, 4 * h + s0 : 4 * h + s1].rearrange("x a w -> x (a w)").bitcast(BF16),
+                rc[g][:, h, 256 * u0 : 256 * u1],
+                rs[g][:, h, 256 * u0 : 256 * u1],
+                grouped["r", g][:, 2 * h + u0 : 2 * h + u1].rearrange("x a w -> x (a w)").bitcast(BF16),
             )
 
         def quantize_rows(key, half):
@@ -175,7 +184,7 @@ def tile_pair_tensor_messages_s8_kernel(
             by_parity = "p (q u e) -> p u q e"
             nc.vector.tensor_tensor(
                 out=sums[k][:, :, t, :].rearrange("p u (q e) -> p u q e", e=2),
-                in0=s1_banks[k, t][:].rearrange(by_parity, u=2, e=2),
+                in0=s1_banks[k, t][:].rearrange("p (u q e) -> p u q e", u=2, e=2),
                 in1=priors[k][:, t, :].rearrange(by_parity, u=2, e=2),
                 op=ADD,
             )
@@ -209,8 +218,8 @@ def tile_pair_tensor_messages_s8_kernel(
         def quantize_a(k, u0=0, u1=2):
             g, b = ORDER[k]
             if (g, b) not in za_c:
-                za_c[g, b] = work.tile([P, 4, P], U32, name="zac", tag="zac", bufs=7, align_bytes=64)
-                za_s[g, b] = work.tile([P, 4, P], U8, name="zas", tag="zas", bufs=7, align_bytes=64)
+                za_c[g, b] = work.tile([P, 4, P], U32, name="zac", tag="zac", bufs=6, align_bytes=64)
+                za_s[g, b] = work.tile([P, 4, P], U8, name="zas", tag="zas", bufs=6, align_bytes=64)
             quantize(
                 za_c[g, b][:, 2 * u0 : 2 * u1].rearrange("p j q -> p (j q)"),
                 za_s[g, b][:, 2 * u0 : 2 * u1].rearrange("p j q -> p (j q)"),
@@ -238,10 +247,18 @@ def tile_pair_tensor_messages_s8_kernel(
                 lis[k][:, 2 * h0 : 2 * h1].rearrange("q t w -> q (t w)").bitcast(BF16),
             )
 
+        staged = {}
+
         def finish(bank, kind, g, t, on_vector=False):
-            o = work.tile([P, R], F32, name="o", tag="o", bufs=6, align_bytes=64)
-            copy(on_vector, o[:], bank[:])
-            nc.sync.dma_start(out=out_v[kind][g, :, t, :], in_=o[:])
+            pair = kind, g, t // 2
+            second = pair in staged
+            if not second:
+                staged[pair] = work.tile([P, 2, R], F32, name="o", tag="o", bufs=3, align_bytes=64)
+            copy(on_vector, staged[pair][:, t % 2, :], bank[:])
+            if (kind, g) in SINGLE_STORES:
+                nc.sync.dma_start(out=out_v[kind][g, :, t, :], in_=staged[pair][:, t % 2, :])
+            elif second:
+                nc.sync.dma_start(out=out_v[kind][g, :, t - 1 : t + 1, :], in_=staged[pair][:])
 
         def receptor_passes(bank, b, j, groups):
             for g in groups:
@@ -329,48 +346,48 @@ def tile_pair_tensor_messages_s8_kernel(
         L0, L1, R0, R1, R2, R3 = ("l", 0), ("l", 1), ("r", 0), ("r", 1), ("r", 2), ("r", 3)
 
         def load_block(key):
-            for t in range(4):
-                load_rows(key, t)
+            load_rows(key, 0, 2)
+            load_rows(key, 2, 4)
 
         def warm_up(n, width=W, bank_no=3):
             bank = bank_tile(bank_no, [P, W])
             for i in range(n):
                 nc.tensor.matmul(out=bank[:, :width], lhsT=idle[:, :P], rhs=idle[:, :width], start=True, stop=True)
 
-        load_rows(L0, 0)
+        load_rows(L0, 0, 1)
         load_block(R0)
-        for t in range(1, 4):
-            load_rows(L0, t)
+        load_rows(L0, 1, 2)
+        load_rows(L0, 2, 4)
         load_prior(0, 0, 2)
 
         warm_up(5)
         sort_words(L0, 0)
         sort_words(R0, 0)
         rows(L0, 0)
-        warm_up(1, 320)
+        warm_up(1)
         sort_words(R0, 1)
         rows(R0, 0)
-        warm_up(1, 320)
+        warm_up(1)
         sort_words(R0, 2)
         rows(R0, 1)
-        warm_up(1, 320)
+        warm_up(1)
         quantize_left(0, 0, 1)
         sort_words(R0, 3)
         rows(R0, 2)
-        warm_up(1, 320)
+        warm_up(1)
         sort_words(L0, 1)
         rows(R0, 3)
-        warm_up(1, 320)
+        warm_up(1)
         load_prior(0, 2, 4)
-        load_near(0, 0)
         load_block(R2)
+        load_near(0, 0)
         for h in range(2):
-            quantize_right(0, h, 0, 2)
+            quantize_right(0, h, 0, 1)
         sort_words(L0, 2)
         rows(L0, 1)
-        warm_up(1, 320)
+        warm_up(1)
         for h in range(2):
-            quantize_right(0, h, 2, 4)
+            quantize_right(0, h, 1, 2)
         rows(L0, 2)
         rows(L0, 3)
         quantize_left(0, 1, 2)
@@ -394,14 +411,12 @@ def tile_pair_tensor_messages_s8_kernel(
         load_block(R3)
         load_prior(2)
         load_near(0, 1)
+        for u in range(2):
+            for h in range(2):
+                quantize_right(2, h, u, u + 1)
         relu_near(0, 1)
-        for h in range(2):
-            quantize_right(2, h, 0, 2)
         group_a(0, 1, "s")
-        for h in range(2):
-            quantize_right(2, h, 2, 4)
         warm_up(2)
-        rows(R1, 0)
         for t in range(4):
             stage1(1, t)
         relu_near(0, 0)
@@ -411,8 +426,10 @@ def tile_pair_tensor_messages_s8_kernel(
             for t in range(4):
                 add_prior(k, t)
             group_a(k - 1, 0, "g")
-            for t in range(1 if k == 1 else 3, 4):
+            for t in range(0 if k == 1 else 3, 4):
                 rows(fresh[k], t)
+                if t == 1:
+                    warm_up(2, W, 0)
             if k == 1:
                 load_block(L1)
                 load_prior(3)
@@ -464,7 +481,6 @@ def tile_pair_tensor_messages_s8_kernel(
             relu_near(k, 0)
         more_ligand(0, 0, (1,))
         more_ligand(0, 1, (1,))
-        group_y(1, 0)
 
         for k in range(4, LAST):
             for t in range(4):
@@ -474,7 +490,8 @@ def tile_pair_tensor_messages_s8_kernel(
             turn_z(k - 1, 1)
             if k == 4:
                 load_prior(7)
-                quantize_a(2)
+                quantize_b(3)
+                group_y(1, 0)
                 group_y(1, 1)
             if k > 4:
                 quantize_a(k - 1)
@@ -483,7 +500,7 @@ def tile_pair_tensor_messages_s8_kernel(
                 stage1(k + 1, t)
             group_a(k, 1, "s")
             if k == 4:
-                quantize_b(3)
+                quantize_a(2)
                 quantize_y(1)
                 close_ligand(0, 0, (3,))
                 close_ligand(0, 1, (3,))

@@ -123,7 +123,7 @@ def tile_pair_tensor_messages_s8_kernel(
             for a in range(2):
                 for w in range(2):
                     nc.tensor.transpose(bank[:, a, w, :], words[:, a, w, :], ident[:])
-            if n == 0:
+            if key not in grouped:
                 grouped[key] = work.tile([P, 4, W], F32, name="rin", tag="rin", bufs=3, align_bytes=64)
             if key[0] == "l":
                 dst = grouped[key][:, n, :].rearrange("x (a p w) -> x a p w", a=2, w=2)
@@ -362,49 +362,49 @@ def tile_pair_tensor_messages_s8_kernel(
 
         warm_up(5)
         sort_words(L0, 0)
-        sort_words(R0, 0)
         rows(L0, 0)
-        warm_up(1)
+        warm_up(2)
+        sort_words(R0, 0)
         sort_words(R0, 1)
         rows(R0, 0)
-        warm_up(1)
-        sort_words(R0, 2)
         rows(R0, 1)
-        warm_up(1)
+        warm_up(2)
         quantize_left(0, 0, 1)
+        sort_words(R0, 2)
         sort_words(R0, 3)
         rows(R0, 2)
-        warm_up(1)
-        sort_words(L0, 1)
         rows(R0, 3)
-        warm_up(1)
         load_prior(0, 2, 4)
         load_block(R2)
         load_near(0, 0)
+        sort_words(L0, 1)
         for h in range(2):
             quantize_right(0, h, 0, 1)
-        sort_words(L0, 2)
         rows(L0, 1)
-        warm_up(1)
+        warm_up(2)
+        sort_words(L0, 2)
         for h in range(2):
             quantize_right(0, h, 1, 2)
-        rows(L0, 2)
         rows(L0, 3)
+        rows(L0, 2)
         quantize_left(0, 1, 2)
         stage1(0, 0)
         load_prior(1)
         load_block(R1)
         stage1(0, 1)
-        quantize_left(0, 2, 3)
-        add_prior(0, 0)
-        stage1(0, 2)
         quantize_left(0, 3, 4)
-        add_prior(0, 1)
+        add_prior(0, 0)
         stage1(0, 3)
-        add_prior(0, 2)
-        rows(R2, 0)
+        quantize_left(0, 2, 3)
+        add_prior(0, 1)
+        stage1(0, 2)
         add_prior(0, 3)
+        rows(R2, 0)
+        add_prior(0, 2)
         rows(R2, 1)
+        sort_words(R2, 2)
+        sort_words(R2, 3)
+        warm_up(1, W, 0)
         rows(R2, 2)
         rows(R2, 3)
         load_y()
@@ -428,7 +428,7 @@ def tile_pair_tensor_messages_s8_kernel(
             group_a(k - 1, 0, "g")
             for t in range(0 if k == 1 else 3, 4):
                 rows(fresh[k], t)
-                if t == 1:
+                if t == 2:
                     warm_up(2, W, 0)
             if k == 1:
                 load_block(L1)
@@ -441,11 +441,11 @@ def tile_pair_tensor_messages_s8_kernel(
                 load_near(1, 1)
             if k == 3:
                 load_prior(6)
-            if k > 1:
-                quantize_b(k - 2)
-            if k < 3:
-                quantize_a(k - 1)
+            if k == 2:
+                quantize_b(0)
             else:
+                quantize_a(k // 2)
+            if k == 3:
                 quantize_y(0)
             if k < 3:
                 turn_z(k - 1, 0)
@@ -464,6 +464,8 @@ def tile_pair_tensor_messages_s8_kernel(
             quantize_rows(fresh[k], 1)
             if k > 1:
                 relu_near(k, 1)
+            if k == 2:
+                quantize_b(1)
             for t in range(3):
                 stage1(k + 1, t)
             if k == 2:
@@ -493,15 +495,16 @@ def tile_pair_tensor_messages_s8_kernel(
                 quantize_b(3)
                 group_y(1, 0)
                 group_y(1, 1)
-            if k > 4:
+            if k == 5:
+                quantize_y(1)
                 quantize_a(k - 1)
             relu_near(k, 1)
+            if k == 6:
+                quantize_a(k - 1)
             for t in range(4):
                 stage1(k + 1, t)
             group_a(k, 1, "s")
             if k == 4:
-                quantize_a(2)
-                quantize_y(1)
                 close_ligand(0, 0, (3,))
                 close_ligand(0, 1, (3,))
                 for t in (2, 3):
@@ -514,7 +517,7 @@ def tile_pair_tensor_messages_s8_kernel(
             if k == 6:
                 open_ligand(1, 0, (0, 2))
                 open_ligand(1, 1, (0, 2))
-                quantize_a(3)
+                quantize_a(2)
                 quantize_a(6, 1, 2)
             relu_near(k, 0)
 
@@ -543,6 +546,7 @@ def tile_pair_tensor_messages_s8_kernel(
         turn_z(k, 0)
         more_ligand(1, 2, (1,))
         more_ligand(1, 3, (1,))
+        quantize_a(3)
         quantize_a(k, 0, 1)
         group_a(k, 1, "v")
         quantize_b(k, 0, 1)

@@ -205,7 +205,7 @@ def tile_pair_tensor_messages_s8_kernel(
 
         def group_a(k, u, engine):
             if k not in zis:
-                zis[k] = work.tile([P, 2, 2, P, 4], BF16, name="zi", tag="zi", bufs=6, align_bytes=64)
+                zis[k] = work.tile([P, 2, 2, P, 4], BF16, name="zi", tag="zi", bufs=5, align_bytes=64)
             if engine == "g":
                 dst = zis[k][:, u]
                 src = zs[k, u][:].rearrange("p t (q e) -> p e q t", e=2)
@@ -226,8 +226,8 @@ def tile_pair_tensor_messages_s8_kernel(
                 zis[k][:, u0:u1].rearrange("p u e q t -> p (u e q t)"),
             )
 
-        def turn_z(k, half, on_vector=False):
-            bank = new_bank([P, 2, 2, P])
+        def turn_z(k, half, on_vector=False, bank_no=None):
+            bank = new_bank([P, 2, 2, P]) if bank_no is None else bank_tile(bank_no, [P, 2, 2, P])
             for tt in range(2):
                 for u in range(2):
                     nc.tensor.transpose(bank[:, tt, u, :], zs[k, u][:, 2 * half + tt, :].bitcast(F32), ident[:])
@@ -304,19 +304,20 @@ def tile_pair_tensor_messages_s8_kernel(
             finish(bank, "l", g, t, on_vector)
             ring.append(n)
 
-        y_codes = keep.tile([P, 2, 4, R], U8, name="y_codes", align_bytes=64)
+        y_codes = [keep.tile([P, 4, R], U8, name=f"y_codes{g}", align_bytes=64) for g in range(2)]
         y_sc = keep.tile([P, 2, 4], F32, name="y_sc", align_bytes=64)
         y_plane, y_group = {}, {}
 
-        def load_y():
-            nc.sync.dma_start(out=y_sc[:], in_=y_scale.rearrange("(g p t) o -> p g (t o)", p=P, t=4))
-            nc.sync.dma_start(out=y_codes[:], in_=y_bytes.rearrange("(g p t) r -> p g t r", p=P, t=4))
+        def load_y(g):
+            if g == 0:
+                nc.sync.dma_start(out=y_sc[:], in_=y_scale.rearrange("(g p t) o -> p g (t o)", p=P, t=4))
+            nc.sync.dma_start(out=y_codes[g][:], in_=y_bytes.rearrange("(g p t) r -> g p t r", p=P, t=4)[g])
 
         def widen_y(g, t):
             if t == 0:
-                y_plane[g] = work.tile([P, 4, R], BF16, name="y_plane", tag="y_plane", bufs=1, align_bytes=64)
+                y_plane[g] = work.tile([P, 4, R], BF16, name="y_plane", tag="y_plane", bufs=2, align_bytes=64)
             nc.scalar.activation(
-                y_plane[g][:, t, :], y_codes[:, g, t, :].bitcast(FP8), COPY, scale=y_sc[:, g, t : t + 1]
+                y_plane[g][:, t, :], y_codes[g][:, t, :].bitcast(FP8), COPY, scale=y_sc[:, g, t : t + 1]
             )
 
         def group_y(g, half):
@@ -389,6 +390,7 @@ def tile_pair_tensor_messages_s8_kernel(
         rows(L0, 2)
         quantize_left(0, 1, 2)
         stage1(0, 0)
+        load_y(0)
         load_prior(1)
         load_block(R1)
         stage1(0, 1)
@@ -407,13 +409,15 @@ def tile_pair_tensor_messages_s8_kernel(
         warm_up(1, W, 0)
         rows(R2, 2)
         rows(R2, 3)
-        load_y()
         load_block(R3)
+        load_y(1)
         load_prior(2)
         load_near(0, 1)
         for u in range(2):
             for h in range(2):
                 quantize_right(2, h, u, u + 1)
+        for t in range(4):
+            widen_y(0, t)
         relu_near(0, 1)
         group_a(0, 1, "s")
         warm_up(2)
@@ -428,7 +432,7 @@ def tile_pair_tensor_messages_s8_kernel(
             group_a(k - 1, 0, "g")
             for t in range(0 if k == 1 else 3, 4):
                 rows(fresh[k], t)
-                if t == 2:
+                if t == 1:
                     warm_up(2, W, 0)
             if k == 1:
                 load_block(L1)
@@ -441,6 +445,7 @@ def tile_pair_tensor_messages_s8_kernel(
                 load_near(1, 1)
             if k == 3:
                 load_prior(6)
+                group_a(2, 1, "s")
             if k == 2:
                 quantize_b(0)
             else:
@@ -468,17 +473,22 @@ def tile_pair_tensor_messages_s8_kernel(
                 quantize_b(1)
             for t in range(3):
                 stage1(k + 1, t)
-            if k == 2:
+            if k == 1:
                 group_y(0, 0)
+            if k == 2:
                 group_y(0, 1)
-            else:
-                for t in range(4):
-                    widen_y(k // 2, t)
+                widen_y(1, 0)
+                widen_y(1, 1)
+            if k == 3:
+                widen_y(1, 2)
+                widen_y(1, 3)
+                group_y(1, 0)
             if k == 3:
                 quantize_b(2)
             if k < 3:
                 rows(fresh[k + 1], 2)
-            group_a(k, 1, "s")
+            if k != 2:
+                group_a(k, 1, "s")
             stage1(k + 1, 3)
             relu_near(k, 0)
         more_ligand(0, 0, (1,))
@@ -493,7 +503,6 @@ def tile_pair_tensor_messages_s8_kernel(
             if k == 4:
                 load_prior(7)
                 quantize_b(3)
-                group_y(1, 0)
                 group_y(1, 1)
             if k == 5:
                 quantize_y(1)
@@ -503,14 +512,15 @@ def tile_pair_tensor_messages_s8_kernel(
                 quantize_a(k - 1)
             for t in range(4):
                 stage1(k + 1, t)
-            group_a(k, 1, "s")
             if k == 4:
                 close_ligand(0, 0, (3,))
                 close_ligand(0, 1, (3,))
+                group_a(k, 1, "s")
                 for t in (2, 3):
                     open_ligand(0, t, (0, 2, 1))
                     close_ligand(0, t, (3,))
             else:
+                group_a(k, 1, "s")
                 quantize_b(k - 1)
                 for j in range(4):
                     receptor(ORDER[k - 1][1], j)

@@ -24,7 +24,6 @@ P = 128
 W = 512
 ORDER = [(0, 0), (0, 2), (0, 1), (0, 3), (1, 0), (1, 2), (1, 1), (1, 3)]
 LAST = len(ORDER) - 1
-SINGLE_STORES = (("l", 1), ("r", 3))
 
 
 def tile_pair_tensor_messages_s8_kernel(
@@ -84,17 +83,8 @@ def tile_pair_tensor_messages_s8_kernel(
             nc.sync.dma_start(out=near_t[:], in_=near_v[g, :, :, W * c : W * (c + 1)])
             nears[g, c] = near_t
 
-        ring = [4, 5, 6, 7]
-
         def bank_tile(n, shape):
             return psum.tile(shape, F32, name=f"bank{n}", tag=f"bank{n}", bufs=1)
-
-        def new_bank(shape, hold=False):
-            n = ring[0]
-            ring.remove(n)
-            if not hold:
-                ring.append(n)
-            return bank_tile(n, shape)
 
         def copy(on_vector, dst, src):
             if on_vector:
@@ -112,19 +102,33 @@ def tile_pair_tensor_messages_s8_kernel(
             words = raw[:].rearrange("p e d -> p (e d)").bitcast(F32)
             return words.rearrange("p (a h x w) -> p h a w x", a=2, h=2, w=2)[:, n % 2]
 
-        def sort_words(key, n):
-            srt = work.tile([P, 2, 2, P], F32, name="srt", tag="srt", bufs=3, align_bytes=64)
-            nc.vector.tensor_copy(out=srt[:], in_=word_runs(key, n))
-            sorted_rows[key, n] = srt
+        def sort_words(key, n0, n1, engine):
+            srt = work.tile([P, n1 - n0, 2, 2, P], U32, name="srt", tag="srt", bufs=2, align_bytes=64)
+            for n in range(n0, n1):
+                sorted_rows[key, n] = srt[:, n - n0].bitcast(F32)
+            raw, row = raws[key, n0]
+            words = raw[:, row : row + n1 - n0].rearrange("p e d -> p (e d)").bitcast(U32)
+            if key[0] == "l":
+                src = words.rearrange("p (a x w) -> p a w x", x=P, w=2)
+                engine.tensor_copy(out=srt[:].rearrange("p n a w x -> p (n a) w x"), in_=src)
+            else:
+                src = words.rearrange("p (a h x w) -> p a h w x", a=2, h=2, w=2)
+                engine.tensor_copy(out=srt[:].rearrange("p h a w x -> p a h w x"), in_=src)
 
-        def rows(key, n, on_vector=False):
-            words = sorted_rows[key, n][:] if (key, n) in sorted_rows else word_runs(key, n)
-            bank = new_bank([P, 2, 2, P])
+        turned = {}
+
+        def turn_rows(key, n, bank_no):
+            words = sorted_rows[key, n] if (key, n) in sorted_rows else word_runs(key, n)
+            bank = bank_tile(bank_no, [P, 2, 2, P])
             for a in range(2):
                 for w in range(2):
                     nc.tensor.transpose(bank[:, a, w, :], words[:, a, w, :], ident[:])
+            turned[key, n] = bank
+
+        def empty_rows(key, n, on_vector=False):
+            bank = turned[key, n]
             if key not in grouped:
-                grouped[key] = work.tile([P, 4, W], F32, name="rin", tag="rin", bufs=3, align_bytes=64)
+                grouped[key] = work.tile([P, 4, W], F32, name="rin", tag="rin", bufs=2, align_bytes=64)
             if key[0] == "l":
                 dst = grouped[key][:, n, :].rearrange("x (a p w) -> x a p w", a=2, w=2)
                 src = bank[:].rearrange("x a w p -> x a p w")
@@ -132,6 +136,10 @@ def tile_pair_tensor_messages_s8_kernel(
                 dst = grouped[key][:, 2 * (n % 2) + n // 2, :].rearrange("x (p a w) -> x p a w", a=2, w=2)
                 src = bank[:].rearrange("x a w p -> x p a w")
             copy(on_vector, dst, src)
+
+        def rows(key, n, bank_no, on_vector=False):
+            turn_rows(key, n, bank_no)
+            empty_rows(key, n, on_vector)
 
         def quantize(codes, scales, values):
             nc.vector.quantize_mx(out=codes.bitcast(FP8X4), scales=scales, in_=values)
@@ -158,12 +166,9 @@ def tile_pair_tensor_messages_s8_kernel(
 
         s1_banks = {}
 
-        def s1_bank(t):
-            return bank_tile(t, [P, W])
-
-        def stage1(k, t):
+        def stage1(k, t, bank_no=None):
             g, b = ORDER[k]
-            bank = s1_bank(t)
+            bank = bank_tile(t if bank_no is None else bank_no, [P, W])
             for h in range(2):
                 nc.tensor.matmul_mx(
                     out=bank[:],
@@ -179,7 +184,7 @@ def tile_pair_tensor_messages_s8_kernel(
         sums, zs, zis, lis = {}, {}, {}, {}
 
         def add_prior(k, t):
-            if t == 0:
+            if k not in sums:
                 sums[k] = work.tile([P, 2, 4, 2 * P], F32, name="sum_t", tag="sum_t", bufs=2, align_bytes=64)
             by_parity = "p (q u e) -> p u q e"
             nc.vector.tensor_tensor(
@@ -191,8 +196,8 @@ def tile_pair_tensor_messages_s8_kernel(
 
         def relu_near(k, u, t0=0, t1=4):
             g, b = ORDER[k]
-            if t0 == 0:
-                zs[k, u] = work.tile([P, 4, 2 * P], BF16, name="z", tag="z", bufs=4, align_bytes=64)
+            if (k, u) not in zs:
+                zs[k, u] = work.tile([P, 4, 2 * P], BF16, name="z", tag="z", bufs=6, align_bytes=64)
             pairs = "p t (q u e) -> p (t q) u e"
             nc.vector.scalar_tensor_tensor(
                 out=zs[k, u][:, t0:t1].rearrange("p t (q e) -> p (t q) e", e=2),
@@ -226,15 +231,18 @@ def tile_pair_tensor_messages_s8_kernel(
                 zis[k][:, u0:u1].rearrange("p u e q t -> p (u e q t)"),
             )
 
-        def turn_z(k, half, on_vector=False, bank_no=None):
-            bank = new_bank([P, 2, 2, P]) if bank_no is None else bank_tile(bank_no, [P, 2, 2, P])
+        def turn_z(k, half, bank_no):
+            bank = bank_tile(bank_no, [P, 2, 2, P])
             for tt in range(2):
                 for u in range(2):
                     nc.tensor.transpose(bank[:, tt, u, :], zs[k, u][:, 2 * half + tt, :].bitcast(F32), ident[:])
+            turned[k, half] = bank
+
+        def empty_z(k, half, on_vector=False):
             if half == 0:
                 lis[k] = work.tile([P, 4, 2 * P], F32, name="li", tag="li", bufs=2, align_bytes=64)
             dst = lis[k][:, 2 * half : 2 * half + 2].rearrange("q t (p u) -> q t p u", u=2)
-            copy(on_vector, dst, bank[:].rearrange("q t u p -> q t p u"))
+            copy(on_vector, dst, turned[k, half][:].rearrange("q t u p -> q t p u"))
 
         def quantize_b(k, h0=0, h1=2):
             g, b = ORDER[k]
@@ -247,23 +255,25 @@ def tile_pair_tensor_messages_s8_kernel(
                 lis[k][:, 2 * h0 : 2 * h1].rearrange("q t w -> q (t w)").bitcast(BF16),
             )
 
-        staged = {}
+        staged, sum_banks = {}, {}
 
-        def finish(bank, kind, g, t, on_vector=False):
+        def finish(kind, g, t, on_vector=False, alone=False):
             pair = kind, g, t // 2
             second = pair in staged
             if not second:
-                staged[pair] = work.tile([P, 2, R], F32, name="o", tag="o", bufs=3, align_bytes=64)
-            copy(on_vector, staged[pair][:, t % 2, :], bank[:])
-            if (kind, g) in SINGLE_STORES:
+                staged[pair] = work.tile([P, 2, R], F32, name="o", tag="o", bufs=4, align_bytes=64)
+            copy(on_vector, staged[pair][:, t % 2, :], sum_banks[kind, g, t][:])
+            if alone:
                 nc.sync.dma_start(out=out_v[kind][g, :, t, :], in_=staged[pair][:, t % 2, :])
             elif second:
                 nc.sync.dma_start(out=out_v[kind][g, :, t - 1 : t + 1, :], in_=staged[pair][:])
 
-        def receptor_passes(bank, b, j, groups):
+        def receptor(b, j, groups, bank_no=None):
+            if bank_no is not None:
+                sum_banks["r", b, j] = bank_tile(bank_no, [P, R])
             for g in groups:
                 nc.tensor.matmul_mx(
-                    out=bank[:],
+                    out=sum_banks["r", b, j][:],
                     lhsT=za_c[g, b][:, j, :].bitcast(FP8X4),
                     lhsT_scale=za_s[g, b][:, j, :],
                     rhs=yc[g][:].bitcast(FP8X4),
@@ -272,37 +282,19 @@ def tile_pair_tensor_messages_s8_kernel(
                     stop=(g == 1),
                 )
 
-        def receptor(b, j, on_vector=False):
-            bank = new_bank([P, R])
-            receptor_passes(bank, b, j, (0, 1))
-            finish(bank, "r", b, j, on_vector)
-
-        def ligand_passes(bank, g, t, blocks):
+        def ligand(g, t, blocks, bank_no=None, last=3):
+            if bank_no is not None:
+                sum_banks["l", g, t] = bank_tile(bank_no, [P, R])
             for b in blocks:
                 nc.tensor.matmul_mx(
-                    out=bank[:],
+                    out=sum_banks["l", g, t][:],
                     lhsT=zb_c[g, b][:, t, :].bitcast(FP8X4),
                     lhsT_scale=zb_s[g, b][:, t, :],
                     rhs=v_tile[:, b, :].bitcast(FP4X4),
                     rhs_scale=vs_tile[:, b, :],
                     start=(b == 0),
-                    stop=(b == 3),
+                    stop=(b == last),
                 )
-
-        held = {}
-
-        def open_ligand(g, t, blocks):
-            held[g, t] = ring[0], new_bank([P, R], hold=True)
-            ligand_passes(held[g, t][1], g, t, blocks)
-
-        def more_ligand(g, t, blocks):
-            ligand_passes(held[g, t][1], g, t, blocks)
-
-        def close_ligand(g, t, blocks, on_vector=False):
-            n, bank = held[g, t]
-            ligand_passes(bank, g, t, blocks)
-            finish(bank, "l", g, t, on_vector)
-            ring.append(n)
 
         y_codes = [keep.tile([P, 4, R], U8, name=f"y_codes{g}", align_bytes=64) for g in range(2)]
         y_sc = keep.tile([P, 2, 4], F32, name="y_sc", align_bytes=64)
@@ -315,14 +307,14 @@ def tile_pair_tensor_messages_s8_kernel(
 
         def widen_y(g, t):
             if t == 0:
-                y_plane[g] = work.tile([P, 4, R], BF16, name="y_plane", tag="y_plane", bufs=2, align_bytes=64)
+                y_plane[g] = work.tile([P, 4, R], BF16, name="y_plane", tag="y_plane", bufs=1, align_bytes=64)
             nc.scalar.activation(
                 y_plane[g][:, t, :], y_codes[g][:, t, :].bitcast(FP8), COPY, scale=y_sc[:, g, t : t + 1]
             )
 
         def group_y(g, half):
             if half == 0:
-                y_group[g] = work.tile([P, R, 4], BF16, name="y_group", tag="y_group", bufs=1, align_bytes=64)
+                y_group[g] = work.tile([P, R, 4], BF16, name="y_group", tag="y_group", bufs=2, align_bytes=64)
             cols = slice(256 * half, 256 * (half + 1))
             nc.scalar.copy(
                 out=y_group[g][:, cols].rearrange("p (c i) t -> p c t i", i=4),
@@ -360,214 +352,264 @@ def tile_pair_tensor_messages_s8_kernel(
         load_rows(L0, 1, 2)
         load_rows(L0, 2, 4)
         load_prior(0, 0, 2)
-
-        warm_up(5)
-        sort_words(L0, 0)
-        rows(L0, 0)
-        warm_up(2)
-        sort_words(R0, 0)
-        sort_words(R0, 1)
-        rows(R0, 0)
-        rows(R0, 1)
-        warm_up(2)
-        quantize_left(0, 0, 1)
-        sort_words(R0, 2)
-        sort_words(R0, 3)
-        rows(R0, 2)
-        rows(R0, 3)
         load_prior(0, 2, 4)
         load_block(R2)
+
+        warm_up(5)
+        sort_words(L0, 0, 1, nc.vector)
+        rows(L0, 0, 4)
+        warm_up(2)
+        sort_words(R0, 0, 2, nc.vector)
+        rows(R0, 0, 5)
+        rows(R0, 1, 6)
+        warm_up(2)
         load_near(0, 0)
-        sort_words(L0, 1)
+        load_rows(R1, 0, 2)
+        quantize_left(0, 0, 1)
+        sort_words(R0, 2, 4, nc.vector)
+        rows(R0, 2, 7)
+        rows(R0, 3, 4)
+        load_rows(R1, 2, 4)
+        load_prior(1)
+        sort_words(L0, 1, 2, nc.vector)
         for h in range(2):
             quantize_right(0, h, 0, 1)
-        rows(L0, 1)
+        rows(L0, 1, 5)
         warm_up(2)
-        sort_words(L0, 2)
         for h in range(2):
             quantize_right(0, h, 1, 2)
-        rows(L0, 3)
-        rows(L0, 2)
+        rows(L0, 2, 6)
+        rows(L0, 3, 7)
         quantize_left(0, 1, 2)
         stage1(0, 0)
-        load_y(0)
-        load_prior(1)
-        load_block(R1)
         stage1(0, 1)
-        quantize_left(0, 3, 4)
-        add_prior(0, 0)
-        stage1(0, 3)
         quantize_left(0, 2, 3)
-        add_prior(0, 1)
+        add_prior(0, 0)
+        quantize_left(0, 3, 4)
         stage1(0, 2)
-        add_prior(0, 3)
-        rows(R2, 0)
-        add_prior(0, 2)
-        rows(R2, 1)
-        sort_words(R2, 2)
-        sort_words(R2, 3)
+        stage1(0, 3)
+        rows(R2, 0, 4)
+        rows(R2, 1, 5)
+        sort_words(R2, 2, 4, nc.gpsimd)
+        for t in range(1, 4):
+            add_prior(0, t)
         warm_up(1, W, 0)
-        rows(R2, 2)
-        rows(R2, 3)
+        rows(R2, 2, 6)
+        rows(R2, 3, 7)
+        load_y(0)
         load_block(R3)
-        load_y(1)
         load_prior(2)
         load_near(0, 1)
-        for u in range(2):
-            for h in range(2):
-                quantize_right(2, h, u, u + 1)
-        for t in range(4):
-            widen_y(0, t)
         relu_near(0, 1)
-        group_a(0, 1, "s")
-        warm_up(2)
+        for h in range(2):
+            quantize_right(2, h, 0, 1)
+        warm_up(1, W, 0)
+        rows(R1, 0, 4)
+        rows(R1, 1, 5)
+        for h in range(2):
+            quantize_right(2, h, 1, 2)
+        warm_up(1, W, 0)
         for t in range(4):
             stage1(1, t)
+        group_a(0, 1, "s")
+        widen_y(0, 0)
+        widen_y(0, 1)
+        rows(R1, 2, 6)
+        rows(R1, 3, 7)
         relu_near(0, 0)
 
-        fresh = {1: R1, 2: R3, 3: L1}
-        for k in range(1, 4):
+        for k, ready, fresh in ((1, R1, R3), (2, R3, L1)):
             for t in range(4):
                 add_prior(k, t)
             group_a(k - 1, 0, "g")
-            for t in range(0 if k == 1 else 3, 4):
-                rows(fresh[k], t)
-                if t == 1:
-                    warm_up(2, W, 0)
+            turn_z(k - 1, 0, 4)
+            turn_z(k - 1, 1, 5)
+            empty_z(k - 1, 0)
+            empty_z(k - 1, 1)
+            warm_up(2, W, 0)
+            rows(fresh, 0, 6)
+            rows(fresh, 1, 7)
+            relu_near(k, 1, 0, 2)
+            relu_near(k, 1, 2, 4)
+            quantize_rows(ready, 0)
+            quantize_rows(ready, 1)
             if k == 1:
                 load_block(L1)
                 load_prior(3)
                 load_v()
+                load_y(1)
                 load_prior(4)
                 load_near(1, 0)
-            if k == 2:
+                widen_y(0, 2)
+                widen_y(0, 3)
+                group_y(0, 0)
+            else:
                 load_prior(5)
                 load_near(1, 1)
-            if k == 3:
-                load_prior(6)
-                group_a(2, 1, "s")
-            if k == 2:
-                quantize_b(0)
-            else:
-                quantize_a(k // 2)
-            if k == 3:
-                quantize_y(0)
-            if k < 3:
-                turn_z(k - 1, 0)
-                turn_z(k - 1, 1)
-                warm_up(2, 512, 3)
-                rows(fresh[k + 1], 0)
-                rows(fresh[k + 1], 1)
-            else:
-                turn_z(k - 1, 0)
-                turn_z(k - 1, 1)
-                open_ligand(0, 0, (0, 2))
-                open_ligand(0, 1, (0, 2))
-            if k == 1:
-                relu_near(k, 1)
-            quantize_rows(fresh[k], 0)
-            quantize_rows(fresh[k], 1)
-            if k > 1:
-                relu_near(k, 1)
-            if k == 2:
-                quantize_b(1)
-            for t in range(3):
-                stage1(k + 1, t)
-            if k == 1:
-                group_y(0, 0)
-            if k == 2:
+                group_a(1, 1, "s")
                 group_y(0, 1)
-                widen_y(1, 0)
-                widen_y(1, 1)
-            if k == 3:
-                widen_y(1, 2)
-                widen_y(1, 3)
-                group_y(1, 0)
-            if k == 3:
-                quantize_b(2)
-            if k < 3:
-                rows(fresh[k + 1], 2)
-            if k != 2:
-                group_a(k, 1, "s")
-            stage1(k + 1, 3)
-            relu_near(k, 0)
-        more_ligand(0, 0, (1,))
-        more_ligand(0, 1, (1,))
-
-        for k in range(4, LAST):
-            for t in range(4):
-                add_prior(k, t)
-            group_a(k - 1, 0, "g")
-            turn_z(k - 1, 0)
-            turn_z(k - 1, 1)
-            if k == 4:
-                load_prior(7)
-                quantize_b(3)
-                group_y(1, 1)
-            if k == 5:
-                quantize_y(1)
-                quantize_a(k - 1)
-            relu_near(k, 1)
-            if k == 6:
-                quantize_a(k - 1)
             for t in range(4):
                 stage1(k + 1, t)
-            if k == 4:
-                close_ligand(0, 0, (3,))
-                close_ligand(0, 1, (3,))
-                group_a(k, 1, "s")
-                for t in (2, 3):
-                    open_ligand(0, t, (0, 2, 1))
-                    close_ligand(0, t, (3,))
-            else:
-                group_a(k, 1, "s")
-                quantize_b(k - 1)
-                for j in range(4):
-                    receptor(ORDER[k - 1][1], j)
-            if k == 6:
-                open_ligand(1, 0, (0, 2))
-                open_ligand(1, 1, (0, 2))
-                quantize_a(2)
-                quantize_a(6, 1, 2)
+            rows(fresh, 2, 6)
+            rows(fresh, 3, 7)
+            quantize_b(k - 1)
             relu_near(k, 0)
+
+        for t in range(4):
+            add_prior(3, t)
+        group_a(2, 0, "g")
+        turn_z(2, 0, 4)
+        turn_z(2, 1, 5)
+        empty_z(2, 0)
+        empty_z(2, 1)
+        load_prior(6)
+        for t in range(2):
+            ligand(0, t, (0, 2), 6 + t)
+        group_a(2, 1, "s")
+        for t in range(4):
+            widen_y(1, t)
+        quantize_rows(L1, 0)
+        relu_near(3, 1)
+        quantize_rows(L1, 1)
+        quantize_b(2)
+        for t in range(4):
+            stage1(4, t)
+        for t in range(2):
+            ligand(0, t, (1,))
+        relu_near(3, 0)
+
+        for t in range(4):
+            add_prior(4, t)
+        group_a(3, 0, "g")
+        turn_z(3, 0, 4)
+        turn_z(3, 1, 5)
+        empty_z(3, 0)
+        empty_z(3, 1)
+        group_y(1, 0)
+        group_y(1, 1)
+        load_prior(7)
+        for t in range(4):
+            stage1(5, t)
+        quantize_y(0)
+        quantize_b(3)
+        relu_near(4, 1)
+        for t in range(2):
+            ligand(0, t, (3,))
+        for t in range(2, 4):
+            ligand(0, t, (0, 2, 1, 3), 2 + t)
+        finish("l", 0, 0)
+        finish("l", 0, 1)
+        group_a(4, 1, "s")
+        finish("l", 0, 2)
+        finish("l", 0, 3)
+        quantize_a(0)
+        relu_near(4, 0)
+
+        for t in range(4):
+            add_prior(5, t)
+        group_a(4, 0, "g")
+        turn_z(4, 0, 6)
+        turn_z(4, 1, 7)
+        empty_z(4, 0)
+        empty_z(4, 1)
+        group_a(3, 1, "s")
+        for t in range(4):
+            stage1(6, t)
+        quantize_y(1)
+        quantize_a(4)
+        relu_near(5, 1)
+        quantize_b(4)
+        for j in range(4):
+            receptor(0, j, (0, 1), (4, 5, 6, 7)[j])
+        finish("r", 0, 0)
+        finish("r", 0, 1)
+        finish("r", 0, 2)
+        finish("r", 0, 3)
+        group_a(5, 1, "s")
+        for t in range(2):
+            ligand(1, t, (0,), 4 + t)
+        quantize_a(1)
+        relu_near(5, 0)
+
+        for t in range(4):
+            add_prior(6, t)
+        group_a(5, 0, "g")
+        turn_z(5, 0, 6)
+        turn_z(5, 1, 7)
+        empty_z(5, 0)
+        empty_z(5, 1)
+        relu_near(6, 1, 0, 2)
+        relu_near(6, 1, 2, 4)
+        group_a(6, 1, "s")
+        for t in range(4):
+            stage1(7, t)
+        quantize_a(5)
+        quantize_b(5)
+        receptor(2, 0, (0, 1), 6)
+        receptor(2, 1, (0, 1), 7)
+        finish("r", 2, 0)
+        finish("r", 2, 1)
+        for t in range(2):
+            ligand(1, t, (2,))
+        receptor(2, 2, (0, 1), 6)
+        receptor(2, 3, (0, 1), 7)
+        finish("r", 2, 2)
+        finish("r", 2, 3)
+        quantize_a(2)
+        quantize_a(6, 1, 2)
+        relu_near(6, 0)
 
         k = LAST
         for t in range(4):
             add_prior(k, t)
-        group_a(k - 1, 0, "g")
-        turn_z(k - 1, 0)
-        turn_z(k - 1, 1)
-        ring.clear()
-        ring.extend([0, 1, 2, 3, 4, 5])
-        receptor(1, 2)
-        receptor(1, 3)
-        quantize_a(k - 1, 0, 1)
-        open_ligand(1, 2, (0, 2))
-        open_ligand(1, 3, (0, 2))
+        group_a(6, 0, "g")
+        receptor(1, 2, (0, 1), 0)
+        receptor(1, 3, (0, 1), 1)
+        turn_z(6, 0, 6)
+        turn_z(6, 1, 7)
+        finish("r", 1, 2)
+        finish("r", 1, 3)
+        empty_z(6, 0)
+        empty_z(6, 1)
+        quantize_a(6, 0, 1)
+        ligand(1, 2, (0, 2), 2)
+        ligand(1, 3, (0, 2), 3)
         relu_near(k, 0)
+        receptor(1, 0, (0, 1), 0)
+        receptor(1, 1, (0, 1), 1)
         group_a(k, 0, "s")
-        receptor(1, 0)
-        receptor(1, 1)
-        quantize_b(k - 1)
+        finish("r", 1, 0)
+        finish("r", 1, 1)
         relu_near(k, 1, 0, 2)
+        quantize_b(6)
         relu_near(k, 1, 2, 4)
-        more_ligand(1, 0, (1,))
-        more_ligand(1, 1, (1,))
-        turn_z(k, 0)
-        more_ligand(1, 2, (1,))
-        more_ligand(1, 3, (1,))
+        turn_z(k, 0, 6)
+        ligand(1, 0, (1,))
+        ligand(1, 1, (1,))
         quantize_a(3)
+        empty_z(k, 0)
         quantize_a(k, 0, 1)
+        turn_z(k, 1, 7)
+        receptor(3, 0, (0, 1), 0)
+        receptor(3, 1, (0, 1), 1)
         group_a(k, 1, "v")
+        empty_z(k, 1)
         quantize_b(k, 0, 1)
-        receptor(3, 0)
-        receptor(3, 1)
+        finish("r", 3, 0, False, True)
+        finish("r", 3, 1, False, True)
+        ligand(1, 0, (3,))
+        ligand(1, 1, (3,))
         quantize_a(k, 1, 2)
-        turn_z(k, 1, True)
-        close_ligand(1, 0, (3,))
-        close_ligand(1, 1, (3,), True)
         quantize_b(k, 1, 2)
-        receptor(3, 2)
-        receptor(3, 3, True)
-        close_ligand(1, 2, (3,))
-        close_ligand(1, 3, (3,), True)
+        ligand(1, 2, (1,))
+        ligand(1, 3, (1,))
+        finish("l", 1, 0, True, True)
+        finish("l", 1, 1, False, True)
+        ligand(1, 2, (3,))
+        ligand(1, 3, (3,))
+        receptor(3, 2, (0, 1), 6)
+        receptor(3, 3, (0, 1), 7)
+        finish("l", 1, 2, True, True)
+        finish("l", 1, 3, False, True)
+        finish("r", 3, 2, True, True)
+        finish("r", 3, 3, False, True)

@@ -103,7 +103,7 @@ def tile_pair_tensor_messages_s8_kernel(
             return words.rearrange("p (a h x w) -> p h a w x", a=2, h=2, w=2)[:, n % 2]
 
         def sort_words(key, n0, n1, engine):
-            srt = work.tile([P, n1 - n0, 2, 2, P], U32, name="srt", tag="srt", bufs=2, align_bytes=64)
+            srt = work.tile([P, n1 - n0, 2, 2, P], U32, name="srt", tag="srt", bufs=1, align_bytes=64)
             for n in range(n0, n1):
                 sorted_rows[key, n] = srt[:, n - n0].bitcast(F32)
             raw, row = raws[key, n0]
@@ -197,7 +197,7 @@ def tile_pair_tensor_messages_s8_kernel(
         def relu_near(k, u, t0=0, t1=4):
             g, b = ORDER[k]
             if (k, u) not in zs:
-                zs[k, u] = work.tile([P, 4, 2 * P], BF16, name="z", tag="z", bufs=6, align_bytes=64)
+                zs[k, u] = work.tile([P, 4, 2 * P], BF16, name="z", tag="z", bufs=8, align_bytes=64)
             pairs = "p t (q u e) -> p (t q) u e"
             nc.vector.scalar_tensor_tensor(
                 out=zs[k, u][:, t0:t1].rearrange("p t (q e) -> p (t q) e", e=2),
@@ -223,8 +223,8 @@ def tile_pair_tensor_messages_s8_kernel(
         def quantize_a(k, u0=0, u1=2):
             g, b = ORDER[k]
             if (g, b) not in za_c:
-                za_c[g, b] = work.tile([P, 4, P], U32, name="zac", tag="zac", bufs=6, align_bytes=64)
-                za_s[g, b] = work.tile([P, 4, P], U8, name="zas", tag="zas", bufs=6, align_bytes=64)
+                za_c[g, b] = work.tile([P, 4, P], U32, name="zac", tag="zac", bufs=5, align_bytes=64)
+                za_s[g, b] = work.tile([P, 4, P], U8, name="zas", tag="zas", bufs=5, align_bytes=64)
             quantize(
                 za_c[g, b][:, 2 * u0 : 2 * u1].rearrange("p j q -> p (j q)"),
                 za_s[g, b][:, 2 * u0 : 2 * u1].rearrange("p j q -> p (j q)"),
@@ -353,33 +353,30 @@ def tile_pair_tensor_messages_s8_kernel(
         load_rows(L0, 2, 4)
         load_prior(0, 0, 2)
         load_prior(0, 2, 4)
-        load_block(R2)
+        load_rows(R2, 0, 2)
 
         warm_up(5)
-        sort_words(L0, 0, 1, nc.vector)
         rows(L0, 0, 4)
         warm_up(2)
-        sort_words(R0, 0, 2, nc.vector)
         rows(R0, 0, 5)
-        rows(R0, 1, 6)
-        warm_up(2)
+        rows(R0, 1, 6, True)
+        load_rows(R2, 2, 4)
         load_near(0, 0)
-        load_rows(R1, 0, 2)
+        warm_up(1)
         quantize_left(0, 0, 1)
-        sort_words(R0, 2, 4, nc.vector)
         rows(R0, 2, 7)
-        rows(R0, 3, 4)
-        load_rows(R1, 2, 4)
+        quantize_right(0, 0, 0, 1)
+        quantize_right(0, 1, 0, 1)
+        rows(R0, 3, 4, True)
+        load_rows(R1, 0, 2)
         load_prior(1)
-        sort_words(L0, 1, 2, nc.vector)
-        for h in range(2):
-            quantize_right(0, h, 0, 1)
+        warm_up(1)
         rows(L0, 1, 5)
-        warm_up(2)
         for h in range(2):
             quantize_right(0, h, 1, 2)
         rows(L0, 2, 6)
         rows(L0, 3, 7)
+        load_rows(R1, 2, 4)
         quantize_left(0, 1, 2)
         stage1(0, 0)
         stage1(0, 1)
@@ -390,32 +387,30 @@ def tile_pair_tensor_messages_s8_kernel(
         stage1(0, 3)
         rows(R2, 0, 4)
         rows(R2, 1, 5)
-        sort_words(R2, 2, 4, nc.gpsimd)
         for t in range(1, 4):
             add_prior(0, t)
+        sort_words(R2, 2, 4, nc.vector)
         warm_up(1, W, 0)
         rows(R2, 2, 6)
         rows(R2, 3, 7)
-        load_y(0)
-        load_block(R3)
+        load_rows(R3, 0, 2)
         load_prior(2)
-        load_near(0, 1)
+        load_y(0)
+        quantize_right(2, 0, 0, 1)
         relu_near(0, 1)
-        for h in range(2):
-            quantize_right(2, h, 0, 1)
-        warm_up(1, W, 0)
+        quantize_right(2, 1, 0, 1)
+        warm_up(2, W, 0)
         rows(R1, 0, 4)
         rows(R1, 1, 5)
         for h in range(2):
             quantize_right(2, h, 1, 2)
-        warm_up(1, W, 0)
         for t in range(4):
             stage1(1, t)
         group_a(0, 1, "s")
-        widen_y(0, 0)
-        widen_y(0, 1)
         rows(R1, 2, 6)
         rows(R1, 3, 7)
+        load_rows(R3, 2, 4)
+        load_near(0, 1)
         relu_near(0, 0)
 
         for k, ready, fresh in ((1, R1, R3), (2, R3, L1)):
@@ -426,7 +421,7 @@ def tile_pair_tensor_messages_s8_kernel(
             turn_z(k - 1, 1, 5)
             empty_z(k - 1, 0)
             empty_z(k - 1, 1)
-            warm_up(2, W, 0)
+            warm_up(1, W, 0)
             rows(fresh, 0, 6)
             rows(fresh, 1, 7)
             relu_near(k, 1, 0, 2)
@@ -434,20 +429,21 @@ def tile_pair_tensor_messages_s8_kernel(
             quantize_rows(ready, 0)
             quantize_rows(ready, 1)
             if k == 1:
-                load_block(L1)
+                load_rows(L1, 0, 2)
                 load_prior(3)
-                load_v()
+                load_rows(L1, 2, 4)
                 load_y(1)
+                load_v()
                 load_prior(4)
                 load_near(1, 0)
-                widen_y(0, 2)
-                widen_y(0, 3)
-                group_y(0, 0)
+                for t in range(4):
+                    widen_y(0, t)
             else:
                 load_prior(5)
                 load_near(1, 1)
                 group_a(1, 1, "s")
-                group_y(0, 1)
+                group_y(0, 0)
+                warm_up(1, W, 0)
             for t in range(4):
                 stage1(k + 1, t)
             rows(fresh, 2, 6)
@@ -465,7 +461,7 @@ def tile_pair_tensor_messages_s8_kernel(
         load_prior(6)
         for t in range(2):
             ligand(0, t, (0, 2), 6 + t)
-        group_a(2, 1, "s")
+        group_y(0, 1)
         for t in range(4):
             widen_y(1, t)
         quantize_rows(L1, 0)
@@ -512,7 +508,7 @@ def tile_pair_tensor_messages_s8_kernel(
         turn_z(4, 1, 7)
         empty_z(4, 0)
         empty_z(4, 1)
-        group_a(3, 1, "s")
+        group_a(2, 1, "s")
         for t in range(4):
             stage1(6, t)
         quantize_y(1)
@@ -538,6 +534,7 @@ def tile_pair_tensor_messages_s8_kernel(
         turn_z(5, 1, 7)
         empty_z(5, 0)
         empty_z(5, 1)
+        group_a(3, 1, "s")
         relu_near(6, 1, 0, 2)
         relu_near(6, 1, 2, 4)
         group_a(6, 1, "s")

@@ -78,10 +78,10 @@ def tile_pair_tensor_messages_s8_kernel(
                 priors[k] = work.tile([P, 4, W], BF16, name="prior_t", tag="prior_t", bufs=5, align_bytes=64)
             nc.sync.dma_start(out=priors[k][:, t0:t1, :], in_=prior_v[g, :, t0:t1, W * b : W * (b + 1)])
 
-        def load_near(g, c):
-            near_t = keep.tile([P, 4, W], BF16, name=f"near{g}{c}", align_bytes=64)
-            nc.sync.dma_start(out=near_t[:], in_=near_v[g, :, :, W * c : W * (c + 1)])
-            nears[g, c] = near_t
+        def load_near(g, c, t0=0, t1=4):
+            if t0 == 0:
+                nears[g, c] = keep.tile([P, 4, W], BF16, name=f"near{g}{c}", align_bytes=64)
+            nc.sync.dma_start(out=nears[g, c][:, t0:t1, :], in_=near_v[g, :, t0:t1, W * c : W * (c + 1)])
 
         def bank_tile(n, shape):
             return psum.tile(shape, F32, name=f"bank{n}", tag=f"bank{n}", bufs=1)
@@ -92,7 +92,7 @@ def tile_pair_tensor_messages_s8_kernel(
             else:
                 nc.scalar.copy(out=dst, in_=src)
 
-        grouped, sorted_rows = {}, {}
+        grouped = {}
 
         def word_runs(key, n):
             if key[0] == "l":
@@ -102,23 +102,10 @@ def tile_pair_tensor_messages_s8_kernel(
             words = raw[:].rearrange("p e d -> p (e d)").bitcast(F32)
             return words.rearrange("p (a h x w) -> p h a w x", a=2, h=2, w=2)[:, n % 2]
 
-        def sort_words(key, n0, n1, engine):
-            srt = work.tile([P, n1 - n0, 2, 2, P], U32, name="srt", tag="srt", bufs=1, align_bytes=64)
-            for n in range(n0, n1):
-                sorted_rows[key, n] = srt[:, n - n0].bitcast(F32)
-            raw, row = raws[key, n0]
-            words = raw[:, row : row + n1 - n0].rearrange("p e d -> p (e d)").bitcast(U32)
-            if key[0] == "l":
-                src = words.rearrange("p (a x w) -> p a w x", x=P, w=2)
-                engine.tensor_copy(out=srt[:].rearrange("p n a w x -> p (n a) w x"), in_=src)
-            else:
-                src = words.rearrange("p (a h x w) -> p a h w x", a=2, h=2, w=2)
-                engine.tensor_copy(out=srt[:].rearrange("p h a w x -> p a h w x"), in_=src)
-
         turned = {}
 
         def turn_rows(key, n, bank_no):
-            words = sorted_rows[key, n] if (key, n) in sorted_rows else word_runs(key, n)
+            words = word_runs(key, n)
             bank = bank_tile(bank_no, [P, 2, 2, P])
             for a in range(2):
                 for w in range(2):
@@ -360,8 +347,8 @@ def tile_pair_tensor_messages_s8_kernel(
         warm_up(2)
         rows(R0, 0, 5)
         rows(R0, 1, 6, True)
+        load_near(0, 0, 0, 2)
         load_rows(R2, 2, 4)
-        load_near(0, 0)
         warm_up(1)
         quantize_left(0, 0, 1)
         rows(R0, 2, 7)
@@ -369,7 +356,9 @@ def tile_pair_tensor_messages_s8_kernel(
         quantize_right(0, 1, 0, 1)
         rows(R0, 3, 4, True)
         load_rows(R1, 0, 2)
-        load_prior(1)
+        load_near(0, 0, 2, 4)
+        load_prior(1, 0, 2)
+        load_prior(1, 2, 4)
         warm_up(1)
         rows(L0, 1, 5)
         for h in range(2):
@@ -389,29 +378,30 @@ def tile_pair_tensor_messages_s8_kernel(
         rows(R2, 1, 5)
         for t in range(1, 4):
             add_prior(0, t)
-        sort_words(R2, 2, 4, nc.vector)
         warm_up(1, W, 0)
         rows(R2, 2, 6)
         rows(R2, 3, 7)
         load_rows(R3, 0, 2)
         load_prior(2)
         load_y(0)
-        quantize_right(2, 0, 0, 1)
-        relu_near(0, 1)
-        quantize_right(2, 1, 0, 1)
-        warm_up(2, W, 0)
+        relu_near(0, 1, 0, 2)
+        relu_near(0, 0, 0, 2)
+        for h in range(2):
+            quantize_right(2, h, 0, 1)
+        warm_up(1, W, 0)
         rows(R1, 0, 4)
         rows(R1, 1, 5)
         for h in range(2):
             quantize_right(2, h, 1, 2)
+        relu_near(0, 1, 2, 4)
         for t in range(4):
             stage1(1, t)
         group_a(0, 1, "s")
-        rows(R1, 2, 6)
-        rows(R1, 3, 7)
+        for n in (2, 3):
+            rows(R1, n, 4 + n)
         load_rows(R3, 2, 4)
         load_near(0, 1)
-        relu_near(0, 0)
+        relu_near(0, 0, 2, 4)
 
         for k, ready, fresh in ((1, R1, R3), (2, R3, L1)):
             for t in range(4):
@@ -432,8 +422,8 @@ def tile_pair_tensor_messages_s8_kernel(
                 load_rows(L1, 0, 2)
                 load_prior(3)
                 load_rows(L1, 2, 4)
-                load_y(1)
                 load_v()
+                load_y(1)
                 load_prior(4)
                 load_near(1, 0)
                 for t in range(4):
@@ -578,35 +568,34 @@ def tile_pair_tensor_messages_s8_kernel(
         finish("r", 1, 0)
         finish("r", 1, 1)
         relu_near(k, 1, 0, 2)
-        quantize_b(6)
+        quantize_a(3, 0, 1)
         relu_near(k, 1, 2, 4)
-        turn_z(k, 0, 6)
-        ligand(1, 0, (1,))
-        ligand(1, 1, (1,))
-        quantize_a(3)
-        empty_z(k, 0)
         quantize_a(k, 0, 1)
+        turn_z(k, 0, 6)
         turn_z(k, 1, 7)
+        quantize_b(6)
+        empty_z(k, 0)
+        empty_z(k, 1)
         receptor(3, 0, (0, 1), 0)
         receptor(3, 1, (0, 1), 1)
         group_a(k, 1, "v")
-        empty_z(k, 1)
         quantize_b(k, 0, 1)
         finish("r", 3, 0, False, True)
         finish("r", 3, 1, False, True)
-        ligand(1, 0, (3,))
-        ligand(1, 1, (3,))
-        quantize_a(k, 1, 2)
+        for t in range(2):
+            ligand(1, t, (1,))
+        for t in range(2):
+            ligand(1, t, (3,))
         quantize_b(k, 1, 2)
-        ligand(1, 2, (1,))
-        ligand(1, 3, (1,))
-        finish("l", 1, 0, True, True)
-        finish("l", 1, 1, False, True)
-        ligand(1, 2, (3,))
-        ligand(1, 3, (3,))
+        quantize_a(3, 1, 2)
+        quantize_a(k, 1, 2)
+        finish("l", 1, 0, True)
+        finish("l", 1, 1)
+        for t in range(2, 4):
+            ligand(1, t, (1, 3))
         receptor(3, 2, (0, 1), 6)
         receptor(3, 3, (0, 1), 7)
-        finish("l", 1, 2, True, True)
-        finish("l", 1, 3, False, True)
+        finish("l", 1, 2, True)
+        finish("l", 1, 3)
         finish("r", 3, 2, True, True)
         finish("r", 3, 3, False, True)

@@ -49,6 +49,8 @@ def tile_pair_tensor_messages_s8_kernel(
         nc.vector.memset(idle[:], 0.0)
         ident = keep.tile([P, P], F32, name="ident", align_bytes=64)
         make_identity(nc, ident[:])
+        ident_bf = keep.tile([P, P], BF16, name="ident_bf", align_bytes=64)
+        make_identity(nc, ident_bf[:])
         v_tile = keep.tile([P, 4, 2 * R], U8, name="v_tile", align_bytes=64)
         vs_tile = keep.tile([P, 4, R], U8, name="vs_tile", align_bytes=64)
         nc.gpsimd.memset(vs_tile[:].rearrange("p g n -> p (g n)").bitcast(I32), 0)
@@ -83,8 +85,8 @@ def tile_pair_tensor_messages_s8_kernel(
                 nears[g, c] = keep.tile([P, 4, W], BF16, name=f"near{g}{c}", align_bytes=64)
             nc.sync.dma_start(out=nears[g, c][:, t0:t1, :], in_=near_v[g, :, t0:t1, W * c : W * (c + 1)])
 
-        def bank_tile(n, shape):
-            return psum.tile(shape, F32, name=f"bank{n}", tag=f"bank{n}", bufs=1)
+        def bank_tile(n, shape, dtype=F32):
+            return psum.tile(shape, dtype, name=f"bank{n}", tag=f"bank{n}", bufs=1)
 
         def copy(on_vector, dst, src):
             if on_vector:
@@ -168,7 +170,48 @@ def tile_pair_tensor_messages_s8_kernel(
                 )
             s1_banks[k, t] = bank
 
-        sums, zs, zis, lis = {}, {}, {}, {}
+        sums, zs, zis, lis, flipped = {}, {}, {}, {}, {}
+
+        def stage1_flipped(k, t):
+            g, b = ORDER[k]
+            bank = bank_tile(t, [P, 4, P])
+            for c in range(4):
+                cols = slice(P * c, P * (c + 1))
+                for h in range(2):
+                    nc.tensor.matmul_mx(
+                        out=bank[:, c, :],
+                        lhsT=rc[b][:, h, cols].bitcast(FP8X4),
+                        lhsT_scale=rs[b][:, h, cols],
+                        rhs=lc[g][:, t, h, :].bitcast(FP8X4),
+                        rhs_scale=ls[g][:, t, h, :],
+                        start=(h == 0),
+                        stop=(h == 1),
+                    )
+            s1_banks[k, t] = bank
+
+        def empty_flipped(k, t):
+            flipped[k] = work.tile([P, 4, P], F32, name="flipped", tag="flipped", bufs=1, align_bytes=64)
+            nc.scalar.copy(out=flipped[k][:], in_=s1_banks[k, t][:])
+
+        def sum_on_tensor(k, t):
+            bank = bank_tile(t, [P, W])
+            nc.tensor.matmul(
+                out=bank[:].rearrange("p (u q e) -> p q u e", u=2, e=2),
+                lhsT=ident_bf[:],
+                rhs=priors[k][:, t, :].rearrange("p (q u e) -> p q u e", u=2, e=2),
+                start=True,
+                stop=False,
+            )
+            for c in range(4):
+                nc.tensor.matmul(
+                    out=bank[:, P * c : P * (c + 1)],
+                    lhsT=flipped[k][:, c, :],
+                    rhs=ident[:],
+                    is_transpose=True,
+                    start=False,
+                    stop=(c == 3),
+                )
+            s1_banks[k, t] = bank
 
         def add_prior(k, t):
             if k not in sums:
@@ -181,14 +224,18 @@ def tile_pair_tensor_messages_s8_kernel(
                 op=ADD,
             )
 
-        def relu_near(k, u, t0=0, t1=4):
+        def relu_near(k, u, t0=0, t1=4, from_bank=False):
             g, b = ORDER[k]
             if (k, u) not in zs:
-                zs[k, u] = work.tile([P, 4, 2 * P], BF16, name="z", tag="z", bufs=8, align_bytes=64)
+                zs[k, u] = work.tile([P, 4, 2 * P], BF16, name="z", tag="z", bufs=9, align_bytes=64)
             pairs = "p t (q u e) -> p (t q) u e"
             nc.vector.scalar_tensor_tensor(
                 out=zs[k, u][:, t0:t1].rearrange("p t (q e) -> p (t q) e", e=2),
-                in0=sums[k][:, u, t0:t1].rearrange("p t (q e) -> p (t q) e", e=2),
+                in0=(
+                    s1_banks[k, t0][:].rearrange("p (u q e) -> p u q e", u=2, e=2)[:, u]
+                    if from_bank
+                    else sums[k][:, u, t0:t1].rearrange("p t (q e) -> p (t q) e", e=2)
+                ),
                 scalar=0.0,
                 in1=nears[g, b % 2][:, t0:t1].rearrange(pairs, u=2, e=2)[:, :, u, :],
                 op0=MAX,
@@ -308,6 +355,27 @@ def tile_pair_tensor_messages_s8_kernel(
                 in_=y_plane[g][:, :, cols].rearrange("p t (c i) -> p c t i", i=4),
             )
 
+        def weave_y(g, half, bank_no):
+            if half == 0:
+                y_group[g] = work.tile([P, R, 4], BF16, name="y_group", tag="y_group", bufs=2, align_bytes=64)
+            bank = bank_tile(bank_no, [P, 2, P, 4], BF16)
+            for i in range(2):
+                cols = slice(256 * half + P * i, 256 * half + P * (i + 1))
+                nc.tensor.matmul(
+                    out=bank[:, i],
+                    lhsT=ident_bf[:],
+                    rhs=y_plane[g][:, :, cols].rearrange("p t r -> p r t"),
+                    start=True,
+                    stop=True,
+                )
+            turned["y", g, half] = bank
+
+        def empty_y(g, half):
+            nc.scalar.copy(
+                out=y_group[g][:, 256 * half : 256 * (half + 1)].rearrange("p r t -> p (r t)"),
+                in_=turned["y", g, half][:].rearrange("p i r t -> p (i r t)"),
+            )
+
         def quantize_y(g):
             quantize(yc[g][:], ys[g][:], y_group[g][:].rearrange("p r t -> p (r t)"))
 
@@ -411,7 +479,11 @@ def tile_pair_tensor_messages_s8_kernel(
             turn_z(k - 1, 1, 5)
             empty_z(k - 1, 0)
             empty_z(k - 1, 1)
-            warm_up(1, W, 0)
+            if k == 1:
+                warm_up(1, W, 0)
+            else:
+                weave_y(0, 0, 0)
+                empty_y(0, 0)
             rows(fresh, 0, 6)
             rows(fresh, 1, 7)
             relu_near(k, 1, 0, 2)
@@ -431,9 +503,9 @@ def tile_pair_tensor_messages_s8_kernel(
             else:
                 load_prior(5)
                 load_near(1, 1)
+                weave_y(0, 1, 4)
+                empty_y(0, 1)
                 group_a(1, 1, "s")
-                group_y(0, 0)
-                warm_up(1, W, 0)
             for t in range(4):
                 stage1(k + 1, t)
             rows(fresh, 2, 6)
@@ -451,7 +523,7 @@ def tile_pair_tensor_messages_s8_kernel(
         load_prior(6)
         for t in range(2):
             ligand(0, t, (0, 2), 6 + t)
-        group_y(0, 1)
+        group_a(2, 1, "s")
         for t in range(4):
             widen_y(1, t)
         quantize_rows(L1, 0)
@@ -474,8 +546,10 @@ def tile_pair_tensor_messages_s8_kernel(
         group_y(1, 0)
         group_y(1, 1)
         load_prior(7)
-        for t in range(4):
+        for t in range(3):
             stage1(5, t)
+        stage1_flipped(5, 3)
+        empty_flipped(5, 3)
         quantize_y(0)
         quantize_b(3)
         relu_near(4, 1)
@@ -483,6 +557,7 @@ def tile_pair_tensor_messages_s8_kernel(
             ligand(0, t, (3,))
         for t in range(2, 4):
             ligand(0, t, (0, 2, 1, 3), 2 + t)
+        sum_on_tensor(5, 3)
         finish("l", 0, 0)
         finish("l", 0, 1)
         group_a(4, 1, "s")
@@ -491,19 +566,23 @@ def tile_pair_tensor_messages_s8_kernel(
         quantize_a(0)
         relu_near(4, 0)
 
-        for t in range(4):
+        for t in range(3):
             add_prior(5, t)
+        for u in (1, 0):
+            relu_near(5, u, 3, 4, True)
         group_a(4, 0, "g")
         turn_z(4, 0, 6)
         turn_z(4, 1, 7)
         empty_z(4, 0)
         empty_z(4, 1)
-        group_a(2, 1, "s")
-        for t in range(4):
+        group_a(3, 1, "s")
+        for t in range(3):
             stage1(6, t)
+        stage1_flipped(6, 3)
+        empty_flipped(6, 3)
         quantize_y(1)
         quantize_a(4)
-        relu_near(5, 1)
+        relu_near(5, 1, 0, 3)
         quantize_b(4)
         for j in range(4):
             receptor(0, j, (0, 1), (4, 5, 6, 7)[j])
@@ -514,19 +593,20 @@ def tile_pair_tensor_messages_s8_kernel(
         group_a(5, 1, "s")
         for t in range(2):
             ligand(1, t, (0,), 4 + t)
+        sum_on_tensor(6, 3)
         quantize_a(1)
-        relu_near(5, 0)
+        relu_near(5, 0, 0, 3)
 
-        for t in range(4):
+        for t in range(3):
             add_prior(6, t)
+        for u in (1, 0):
+            relu_near(6, u, 3, 4, True)
         group_a(5, 0, "g")
         turn_z(5, 0, 6)
         turn_z(5, 1, 7)
         empty_z(5, 0)
         empty_z(5, 1)
-        group_a(3, 1, "s")
-        relu_near(6, 1, 0, 2)
-        relu_near(6, 1, 2, 4)
+        relu_near(6, 1, 0, 3)
         group_a(6, 1, "s")
         for t in range(4):
             stage1(7, t)
@@ -544,7 +624,7 @@ def tile_pair_tensor_messages_s8_kernel(
         finish("r", 2, 3)
         quantize_a(2)
         quantize_a(6, 1, 2)
-        relu_near(6, 0)
+        relu_near(6, 0, 0, 3)
 
         k = LAST
         for t in range(4):

@@ -291,16 +291,16 @@ def tile_pair_tensor_messages_s8_kernel(
 
         staged, sum_banks = {}, {}
 
-        def finish(kind, g, t, on_vector=False, alone=False):
+        def finish(kind, g, t, on_vector=False, alone=False, queue=nc.sync):
             pair = kind, g, t // 2
             second = pair in staged
             if not second:
                 staged[pair] = work.tile([P, 2, R], F32, name="o", tag="o", bufs=4, align_bytes=64)
             copy(on_vector, staged[pair][:, t % 2, :], sum_banks[kind, g, t][:])
             if alone:
-                nc.sync.dma_start(out=out_v[kind][g, :, t, :], in_=staged[pair][:, t % 2, :])
+                queue.dma_start(out=out_v[kind][g, :, t, :], in_=staged[pair][:, t % 2, :])
             elif second:
-                nc.sync.dma_start(out=out_v[kind][g, :, t - 1 : t + 1, :], in_=staged[pair][:])
+                queue.dma_start(out=out_v[kind][g, :, t - 1 : t + 1, :], in_=staged[pair][:])
 
         def receptor(b, j, groups, bank_no=None):
             if bank_no is not None:
@@ -670,12 +670,12 @@ def tile_pair_tensor_messages_s8_kernel(
         quantize_a(3, 1, 2)
         quantize_a(k, 1, 2)
         finish("l", 1, 0, True)
-        finish("l", 1, 1)
+        finish("l", 1, 1, False, False, nc.scalar)
         for t in range(2, 4):
             ligand(1, t, (1, 3))
         receptor(3, 2, (0, 1), 6)
         receptor(3, 3, (0, 1), 7)
         finish("l", 1, 2, True)
-        finish("l", 1, 3)
+        finish("l", 1, 3, False, False, nc.scalar)
         finish("r", 3, 2, True, True)
-        finish("r", 3, 3, False, True)
+        finish("r", 3, 3, False, True, nc.scalar)

@@ -410,14 +410,12 @@ def tile_pair_tensor_messages_s8_kernel(
         load_prior(0, 2, 4)
         load_rows(R2, 0, 2)
 
-        warm_up(5)
         rows(L0, 0, 4)
         warm_up(2)
         rows(R0, 0, 5)
         rows(R0, 1, 6, True)
         load_near(0, 0, 0, 2)
         load_rows(R2, 2, 4)
-        warm_up(1)
         quantize_left(0, 0, 1)
         rows(R0, 2, 7)
         quantize_right(0, 0, 0, 1)

@@ -45,7 +45,7 @@ def tile_pair_tensor_messages_s8_kernel(
         psum = ctx.enter_context(tc.psum_pool(name="psum", bufs=1))
         ctx.enter_context(tc.manual_schedule())
 
-        idle = keep.tile([P, W], BF16, name="idle", align_bytes=64)
+        idle = keep.tile([P, W], F32, name="idle", align_bytes=64)
         nc.vector.memset(idle[:], 0.0)
         ident = keep.tile([P, P], F32, name="ident", align_bytes=64)
         make_identity(nc, ident[:])
@@ -397,68 +397,63 @@ def tile_pair_tensor_messages_s8_kernel(
             load_rows(key, 0, 2)
             load_rows(key, 2, 4)
 
-        def warm_up(n, width=W, bank_no=3):
+        def warm_up(width, bank_no=3):
             bank = bank_tile(bank_no, [P, W])
-            for i in range(n):
-                nc.tensor.matmul(out=bank[:, :width], lhsT=idle[:, :P], rhs=idle[:, :width], start=True, stop=True)
+            nc.tensor.matmul(out=bank[:, :width], lhsT=idle[:, :P], rhs=idle[:, :width], start=True, stop=True)
 
         load_rows(L0, 0, 1)
         load_block(R0)
         load_rows(L0, 1, 2)
         load_rows(L0, 2, 4)
         load_prior(0, 0, 2)
-        load_prior(0, 2, 4)
         load_rows(R2, 0, 2)
+        load_prior(0, 2, 4)
 
+        warm_up(512)
         rows(L0, 0, 4)
-        warm_up(2)
+        warm_up(256)
         rows(R0, 0, 5)
-        rows(R0, 1, 6, True)
-        load_near(0, 0, 0, 2)
+        rows(R0, 1, 6)
         load_rows(R2, 2, 4)
+        load_near(0, 0, 0, 2)
         quantize_left(0, 0, 1)
+        warm_up(128)
         rows(R0, 2, 7)
-        quantize_right(0, 0, 0, 1)
-        quantize_right(0, 1, 0, 1)
-        rows(R0, 3, 4, True)
+        turn_rows(R0, 3, 4)
         load_rows(R1, 0, 2)
         load_near(0, 0, 2, 4)
         load_prior(1, 0, 2)
         load_prior(1, 2, 4)
-        warm_up(1)
+        quantize_right(0, 0, 0, 1)
+        quantize_right(0, 1, 0, 1)
+        empty_rows(R0, 3, True)
         rows(L0, 1, 5)
+        warm_up(128)
         for h in range(2):
             quantize_right(0, h, 1, 2)
         rows(L0, 2, 6)
         rows(L0, 3, 7)
         load_rows(R1, 2, 4)
-        quantize_left(0, 1, 2)
-        stage1(0, 0)
-        stage1(0, 1)
-        quantize_left(0, 2, 3)
-        add_prior(0, 0)
-        quantize_left(0, 3, 4)
-        stage1(0, 2)
-        stage1(0, 3)
-        rows(R2, 0, 4)
-        rows(R2, 1, 5)
         for t in range(1, 4):
-            add_prior(0, t)
-        warm_up(1, W, 0)
-        rows(R2, 2, 6)
-        rows(R2, 3, 7)
+            quantize_left(0, t, t + 1)
+        for t in range(4):
+            stage1(0, t)
+        for n in range(4):
+            rows(R2, n, 4 + n)
         load_rows(R3, 0, 2)
         load_prior(2)
         load_y(0)
+        for t in range(4):
+            add_prior(0, t)
         relu_near(0, 1, 0, 2)
+        quantize_right(2, 0, 0, 1)
+        quantize_right(2, 1, 0, 1)
         relu_near(0, 0, 0, 2)
         for h in range(2):
-            quantize_right(2, h, 0, 1)
-        warm_up(1, W, 0)
+            quantize_right(2, h, 1, 2)
+        warm_up(128, 0)
         rows(R1, 0, 4)
         rows(R1, 1, 5)
-        for h in range(2):
-            quantize_right(2, h, 1, 2)
         relu_near(0, 1, 2, 4)
         for t in range(4):
             stage1(1, t)
@@ -478,7 +473,7 @@ def tile_pair_tensor_messages_s8_kernel(
             empty_z(k - 1, 0)
             empty_z(k - 1, 1)
             if k == 1:
-                warm_up(1, W, 0)
+                warm_up(128, 0)
             else:
                 weave_y(0, 0, 0)
                 empty_y(0, 0)

@@ -31,7 +31,7 @@ def tile_pair_tensor_messages_s8_kernel(
 ):
     nc = tc.nc
     left_v = left.rearrange("(g p t) d -> g p t d", p=P, t=4)
-    right_v = right.rearrange("(g p t) d -> g p t d", p=P, t=4)
+    right_v = right.rearrange("(g a p e) d -> g a p e d", a=2, p=P, e=2)
     prior_v = prior.rearrange("(g p t) m -> g p t m", p=P, t=4)
     near_v = near.rearrange("(g p t) m -> g p t m", p=P, t=4)
     out_v = {
@@ -67,10 +67,10 @@ def tile_pair_tensor_messages_s8_kernel(
 
         def load_rows(key, t0, t1):
             side, g = key
-            view = left_v if side == "l" else right_v
             n = t1 - t0
+            view = left_v[g, :, t0:t1, :] if side == "l" else right_v[g, t0 // 2]
             raw = work.tile([P, n, K], BF16, name="raw", tag=f"raw{n}", bufs=2 * n, align_bytes=64)
-            nc.sync.dma_start(out=raw[:], in_=view[g, :, t0:t1, :])
+            nc.sync.dma_start(out=raw[:], in_=view)
             for t in range(t0, t1):
                 raws[key, t] = raw, t - t0
 
@@ -196,9 +196,9 @@ def tile_pair_tensor_messages_s8_kernel(
         def sum_on_tensor(k, t):
             bank = bank_tile(t, [P, W])
             nc.tensor.matmul(
-                out=bank[:].rearrange("p (u q e) -> p q u e", u=2, e=2),
+                out=bank[:],
                 lhsT=ident_bf[:],
-                rhs=priors[k][:, t, :].rearrange("p (q u e) -> p q u e", u=2, e=2),
+                rhs=priors[k][:, t, :],
                 start=True,
                 stop=False,
             )
@@ -219,7 +219,7 @@ def tile_pair_tensor_messages_s8_kernel(
             by_parity = "p (q u e) -> p u q e"
             nc.vector.tensor_tensor(
                 out=sums[k][:, :, t, :].rearrange("p u (q e) -> p u q e", e=2),
-                in0=s1_banks[k, t][:].rearrange("p (u q e) -> p u q e", u=2, e=2),
+                in0=s1_banks[k, t][:].rearrange(by_parity, u=2, e=2),
                 in1=priors[k][:, t, :].rearrange(by_parity, u=2, e=2),
                 op=ADD,
             )
@@ -232,7 +232,7 @@ def tile_pair_tensor_messages_s8_kernel(
             nc.vector.scalar_tensor_tensor(
                 out=zs[k, u][:, t0:t1].rearrange("p t (q e) -> p (t q) e", e=2),
                 in0=(
-                    s1_banks[k, t0][:].rearrange("p (u q e) -> p u q e", u=2, e=2)[:, u]
+                    s1_banks[k, t0][:].rearrange("p (q u e) -> p u q e", u=2, e=2)[:, u]
                     if from_bank
                     else sums[k][:, u, t0:t1].rearrange("p t (q e) -> p (t q) e", e=2)
                 ),

from contextlib import ExitStack

import concourse.mybir as mybir
from concourse.masks import make_identity

I, J, C, K, R = 1024, 1024, 2, 1024, 512
M = C * J
FLOPS = 2 * I * M * K + 2 * I * M * R + 2 * I * M * R

F32 = mybir.dt.float32
BF16 = mybir.dt.bfloat16
I32 = mybir.dt.int32
U32 = mybir.dt.uint32
U8 = mybir.dt.uint8
FP8 = mybir.dt.float8_e4m3fn
FP8X4 = mybir.dt.float8_e4m3fn_x4
FP4X4 = mybir.dt.float4_e2m1fn_x4
ADD = mybir.AluOpType.add
MAX = mybir.AluOpType.max
MULT = mybir.AluOpType.mult
COPY = mybir.ActivationFunctionType.Copy

P = 128
W = 512
ORDER = [(0, 0), (0, 2), (0, 1), (0, 3), (1, 0), (1, 2), (1, 1), (1, 3)]
LAST = len(ORDER) - 1


def tile_pair_tensor_messages_s8_kernel(
    tc, left, right, prior, near, v_words, v_scales, y_bytes, y_scale, to_ligand, to_receptor
):
    nc = tc.nc
    left_v = left.rearrange("(g p t) d -> g p t d", p=P, t=4)
    right_v = right.rearrange("(g a p e) d -> g a p e d", a=2, p=P, e=2)
    prior_v = prior.rearrange("(g p t) m -> g p t m", p=P, t=4)
    near_v = near.rearrange("(g p t) m -> g p t m", p=P, t=4)
    out_v = {
        "l": to_ligand.rearrange("(g p t) r -> g p t r", p=P, t=4),
        "r": to_receptor.rearrange("(g p t) r -> g p t r", p=P, t=4),
    }

    with ExitStack() as ctx:
        keep = ctx.enter_context(tc.tile_pool(name="keep", bufs=1))
        work = ctx.enter_context(tc.tile_pool(name="work", bufs=2))
        psum = ctx.enter_context(tc.psum_pool(name="psum", bufs=1))
        ctx.enter_context(tc.manual_schedule())

        idle = keep.tile([P, W], F32, name="idle", align_bytes=64)
        nc.vector.memset(idle[:], 0.0)
        ident = keep.tile([P, P], F32, name="ident", align_bytes=64)
        make_identity(nc, ident[:])
        ident_bf = keep.tile([P, P], BF16, name="ident_bf", align_bytes=64)
        make_identity(nc, ident_bf[:])
        v_tile = keep.tile([P, 4, 2 * R], U8, name="v_tile", align_bytes=64)
        vs_tile = keep.tile([P, 4, R], U8, name="vs_tile", align_bytes=64)
        nc.gpsimd.memset(vs_tile[:].rearrange("p g n -> p (g n)").bitcast(I32), 0)

        lc = [keep.tile([P, 4, 2, P], U32, name=f"lc{g}", align_bytes=64) for g in range(2)]
        ls = [keep.tile([P, 4, 2, P], U8, name=f"ls{g}", align_bytes=64) for g in range(2)]
        rc = [keep.tile([P, 2, W], U32, name=f"rc{g}", align_bytes=64) for g in range(4)]
        rs = [keep.tile([P, 2, W], U8, name=f"rs{g}", align_bytes=64) for g in range(4)]
        yc = [keep.tile([P, R], U32, name=f"yc{g}", align_bytes=64) for g in range(2)]
        ys = [keep.tile([P, R], U8, name=f"ys{g}", align_bytes=64) for g in range(2)]
        za_c, za_s, zb_c, zb_s = {}, {}, {}, {}

        raws, priors, nears = {}, {}, {}

        def load_rows(key, t0, t1):
            side, g = key
            n = t1 - t0
            view = left_v[g, :, t0:t1, :] if side == "l" else right_v[g, t0 // 2]
            raw = work.tile([P, n, K], BF16, name="raw", tag=f"raw{n}", bufs=2 * n, align_bytes=64)
            nc.sync.dma_start(out=raw[:], in_=view)
            for t in range(t0, t1):
                raws[key, t] = raw, t - t0

        def load_prior(k, t0=0, t1=4):
            g, b = ORDER[k]
            if t0 == 0:
                priors[k] = work.tile([P, 4, W], BF16, name="prior_t", tag="prior_t", bufs=5, align_bytes=64)
            nc.sync.dma_start(out=priors[k][:, t0:t1, :], in_=prior_v[g, :, t0:t1, W * b : W * (b + 1)])

        def load_near(g, c, t0=0, t1=4):
            if t0 == 0:
                nears[g, c] = keep.tile([P, 4, W], BF16, name=f"near{g}{c}", align_bytes=64)
            nc.sync.dma_start(out=nears[g, c][:, t0:t1, :], in_=near_v[g, :, t0:t1, W * c : W * (c + 1)])

        def bank_tile(n, shape, dtype=F32):
            return psum.tile(shape, dtype, name=f"bank{n}", tag=f"bank{n}", bufs=1)

        def copy(on_vector, dst, src):
            if on_vector:
                nc.vector.tensor_copy(out=dst, in_=src)
            else:
                nc.scalar.copy(out=dst, in_=src)

        grouped = {}

        def word_runs(key, n):
            if key[0] == "l":
                raw, row = raws[key, n]
                return raw[:, row, :].bitcast(F32).rearrange("p (a x w) -> p a w x", a=2, w=2)
            raw = raws[key, 2 * (n // 2)][0]
            words = raw[:].rearrange("p e d -> p (e d)").bitcast(F32)
            return words.rearrange("p (a h x w) -> p h a w x", a=2, h=2, w=2)[:, n % 2]

        turned = {}

        def turn_rows(key, n, bank_no):
            words = word_runs(key, n)
            bank = bank_tile(bank_no, [P, 2, 2, P])
            for a in range(2):
                for w in range(2):
                    nc.tensor.transpose(bank[:, a, w, :], words[:, a, w, :], ident[:])
            turned[key, n] = bank

        def empty_rows(key, n, on_vector=False):
            bank = turned[key, n]
            if key not in grouped:
                grouped[key] = work.tile([P, 4, W], F32, name="rin", tag="rin", bufs=2, align_bytes=64)
            if key[0] == "l":
                dst = grouped[key][:, n, :].rearrange("x (a p w) -> x a p w", a=2, w=2)
                src = bank[:].rearrange("x a w p -> x a p w")
            else:
                dst = grouped[key][:, 2 * (n % 2) + n // 2, :].rearrange("x (p a w) -> x p a w", a=2, w=2)
                src = bank[:].rearrange("x a w p -> x p a w")
            copy(on_vector, dst, src)

        def rows(key, n, bank_no, on_vector=False):
            turn_rows(key, n, bank_no)
            empty_rows(key, n, on_vector)

        def quantize(codes, scales, values):
            nc.vector.quantize_mx(out=codes.bitcast(FP8X4), scales=scales, in_=values)

        def quantize_left(g, t0, t1):
            quantize(
                lc[g][:, t0:t1].rearrange("x t h p -> x (t h p)"),
                ls[g][:, t0:t1].rearrange("x t h p -> x (t h p)"),
                grouped["l", g][:, t0:t1].rearrange("x a w -> x (a w)").bitcast(BF16),
            )

        def quantize_right(g, h, u0=0, u1=2):
            quantize(
                rc[g][:, h, 256 * u0 : 256 * u1],
                rs[g][:, h, 256 * u0 : 256 * u1],
                grouped["r", g][:, 2 * h + u0 : 2 * h + u1].rearrange("x a w -> x (a w)").bitcast(BF16),
            )

        def quantize_rows(key, half):
            if key[0] == "l":
                quantize_left(key[1], 2 * half, 2 * half + 2)
            else:
                quantize_right(key[1], half)

        s1_banks = {}

        def stage1(k, t, bank_no=None):
            g, b = ORDER[k]
            bank = bank_tile(t if bank_no is None else bank_no, [P, W])
            for h in range(2):
                nc.tensor.matmul_mx(
                    out=bank[:],
                    lhsT=lc[g][:, t, h, :].bitcast(FP8X4),
                    lhsT_scale=ls[g][:, t, h, :],
                    rhs=rc[b][:, h, :].bitcast(FP8X4),
                    rhs_scale=rs[b][:, h, :],
                    start=(h == 0),
                    stop=(h == 1),
                )
            s1_banks[k, t] = bank

        sums, zs, zis, lis, flipped = {}, {}, {}, {}, {}

        def stage1_flipped(k, t):
            g, b = ORDER[k]
            bank = bank_tile(t, [P, 4, P])
            for c in range(4):
                cols = slice(P * c, P * (c + 1))
                for h in range(2):
                    nc.tensor.matmul_mx(
                        out=bank[:, c, :],
                        lhsT=rc[b][:, h, cols].bitcast(FP8X4),
                        lhsT_scale=rs[b][:, h, cols],
                        rhs=lc[g][:, t, h, :].bitcast(FP8X4),
                        rhs_scale=ls[g][:, t, h, :],
                        start=(h == 0),
                        stop=(h == 1),
                    )
            s1_banks[k, t] = bank

        def empty_flipped(k, t):
            flipped[k] = work.tile([P, 4, P], F32, name="flipped", tag="flipped", bufs=1, align_bytes=64)
            nc.scalar.copy(out=flipped[k][:], in_=s1_banks[k, t][:])

        def sum_on_tensor(k, t):
            bank = bank_tile(t, [P, W])
            nc.tensor.matmul(
                out=bank[:],
                lhsT=ident_bf[:],
                rhs=priors[k][:, t, :],
                start=True,
                stop=False,
            )
            for c in range(4):
                nc.tensor.matmul(
                    out=bank[:, P * c : P * (c + 1)],
                    lhsT=flipped[k][:, c, :],
                    rhs=ident[:],
                    is_transpose=True,
                    start=False,
                    stop=(c == 3),
                )
            s1_banks[k, t] = bank

        def add_prior(k, t):
            if k not in sums:
                sums[k] = work.tile([P, 2, 4, 2 * P], F32, name="sum_t", tag="sum_t", bufs=2, align_bytes=64)
            by_parity = "p (q u e) -> p u q e"
            nc.vector.tensor_tensor(
                out=sums[k][:, :, t, :].rearrange("p u (q e) -> p u q e", e=2),
                in0=s1_banks[k, t][:].rearrange(by_parity, u=2, e=2),
                in1=priors[k][:, t, :].rearrange(by_parity, u=2, e=2),
                op=ADD,
            )

        def relu_near(k, u, t0=0, t1=4, from_bank=False):
            g, b = ORDER[k]
            if (k, u) not in zs:
                zs[k, u] = work.tile([P, 4, 2 * P], BF16, name="z", tag="z", bufs=9, align_bytes=64)
            pairs = "p t (q u e) -> p (t q) u e"
            nc.vector.scalar_tensor_tensor(
                out=zs[k, u][:, t0:t1].rearrange("p t (q e) -> p (t q) e", e=2),
                in0=(
                    s1_banks[k, t0][:].rearrange("p (q u e) -> p u q e", u=2, e=2)[:, u]
                    if from_bank
                    else sums[k][:, u, t0:t1].rearrange("p t (q e) -> p (t q) e", e=2)
                ),
                scalar=0.0,
                in1=nears[g, b % 2][:, t0:t1].rearrange(pairs, u=2, e=2)[:, :, u, :],
                op0=MAX,
                op1=MULT,
            )

        def group_a(k, u, engine):
            if k not in zis:
                zis[k] = work.tile([P, 2, 2, P, 4], BF16, name="zi", tag="zi", bufs=5, align_bytes=64)
            if engine == "g":
                dst = zis[k][:, u]
                src = zs[k, u][:].rearrange("p t (q e) -> p e q t", e=2)
                nc.gpsimd.tensor_scalar(out=dst, in0=src, scalar1=1.0, scalar2=0.0, op0=MULT, op1=ADD)
            else:
                dst = zis[k][:, u].rearrange("p e (c i) t -> p c t i e", i=2)
                src = zs[k, u][:].rearrange("p t (c i e) -> p c t i e", i=2, e=2)
                copy(engine == "v", dst, src)

        def quantize_a(k, u0=0, u1=2):
            g, b = ORDER[k]
            if (g, b) not in za_c:
                za_c[g, b] = work.tile([P, 4, P], U32, name="zac", tag="zac", bufs=5, align_bytes=64)
                za_s[g, b] = work.tile([P, 4, P], U8, name="zas", tag="zas", bufs=5, align_bytes=64)
            quantize(
                za_c[g, b][:, 2 * u0 : 2 * u1].rearrange("p j q -> p (j q)"),
                za_s[g, b][:, 2 * u0 : 2 * u1].rearrange("p j q -> p (j q)"),
                zis[k][:, u0:u1].rearrange("p u e q t -> p (u e q t)"),
            )

        def turn_z(k, half, bank_no):
            bank = bank_tile(bank_no, [P, 2, 2, P])
            for tt in range(2):
                for u in range(2):
                    nc.tensor.transpose(bank[:, tt, u, :], zs[k, u][:, 2 * half + tt, :].bitcast(F32), ident[:])
            turned[k, half] = bank

        def empty_z(k, half, on_vector=False):
            if half == 0:
                lis[k] = work.tile([P, 4, 2 * P], F32, name="li", tag="li", bufs=2, align_bytes=64)
            dst = lis[k][:, 2 * half : 2 * half + 2].rearrange("q t (p u) -> q t p u", u=2)
            copy(on_vector, dst, turned[k, half][:].rearrange("q t u p -> q t p u"))

        def quantize_b(k, h0=0, h1=2):
            g, b = ORDER[k]
            if h0 == 0:
                zb_c[g, b] = work.tile([P, 4, P], U32, name="zbc", tag="zbc", bufs=5, align_bytes=64)
                zb_s[g, b] = work.tile([P, 4, P], U8, name="zbs", tag="zbs", bufs=5, align_bytes=64)
            quantize(
                zb_c[g, b][:, 2 * h0 : 2 * h1].rearrange("q t p -> q (t p)"),
                zb_s[g, b][:, 2 * h0 : 2 * h1].rearrange("q t p -> q (t p)"),
                lis[k][:, 2 * h0 : 2 * h1].rearrange("q t w -> q (t w)").bitcast(BF16),
            )

        staged, sum_banks = {}, {}

        def finish(kind, g, t, on_vector=False, alone=False, queue=nc.sync):
            pair = kind, g, t // 2
            second = pair in staged
            if not second:
                staged[pair] = work.tile([P, 2, R], F32, name="o", tag="o", bufs=4, align_bytes=64)
            copy(on_vector, staged[pair][:, t % 2, :], sum_banks[kind, g, t][:])
            if alone:
                queue.dma_start(out=out_v[kind][g, :, t, :], in_=staged[pair][:, t % 2, :])
            elif second:
                queue.dma_start(out=out_v[kind][g, :, t - 1 : t + 1, :], in_=staged[pair][:])

        def receptor(b, j, groups, bank_no=None):
            if bank_no is not None:
                sum_banks["r", b, j] = bank_tile(bank_no, [P, R])
            for g in groups:
                nc.tensor.matmul_mx(
                    out=sum_banks["r", b, j][:],
                    lhsT=za_c[g, b][:, j, :].bitcast(FP8X4),
                    lhsT_scale=za_s[g, b][:, j, :],
                    rhs=yc[g][:].bitcast(FP8X4),
                    rhs_scale=ys[g][:],
                    start=(g == 0),
                    stop=(g == 1),
                )

        def ligand(g, t, blocks, bank_no=None, last=3):
            if bank_no is not None:
                sum_banks["l", g, t] = bank_tile(bank_no, [P, R])
            for b in blocks:
                nc.tensor.matmul_mx(
                    out=sum_banks["l", g, t][:],
                    lhsT=zb_c[g, b][:, t, :].bitcast(FP8X4),
                    lhsT_scale=zb_s[g, b][:, t, :],
                    rhs=v_tile[:, b, :].bitcast(FP4X4),
                    rhs_scale=vs_tile[:, b, :],
                    start=(b == 0),
                    stop=(b == last),
                )

        y_codes = [keep.tile([P, 4, R], U8, name=f"y_codes{g}", align_bytes=64) for g in range(2)]
        y_sc = keep.tile([P, 2, 4], F32, name="y_sc", align_bytes=64)
        y_plane, y_group = {}, {}

        def load_y(g):
            if g == 0:
                nc.sync.dma_start(out=y_sc[:], in_=y_scale.rearrange("(g p t) o -> p g (t o)", p=P, t=4))
            nc.sync.dma_start(out=y_codes[g][:], in_=y_bytes.rearrange("(g p t) r -> g p t r", p=P, t=4)[g])

        def widen_y(g, t):
            if t == 0:
                y_plane[g] = work.tile([P, 4, R], BF16, name="y_plane", tag="y_plane", bufs=1, align_bytes=64)
            nc.scalar.activation(
                y_plane[g][:, t, :], y_codes[g][:, t, :].bitcast(FP8), COPY, scale=y_sc[:, g, t : t + 1]
            )

        def group_y(g, half):
            if half == 0:
                y_group[g] = work.tile([P, R, 4], BF16, name="y_group", tag="y_group", bufs=2, align_bytes=64)
            cols = slice(256 * half, 256 * (half + 1))
            nc.scalar.copy(
                out=y_group[g][:, cols].rearrange("p (c i) t -> p c t i", i=4),
                in_=y_plane[g][:, :, cols].rearrange("p t (c i) -> p c t i", i=4),
            )

        def weave_y(g, half, bank_no):
            if half == 0:
                y_group[g] = work.tile([P, R, 4], BF16, name="y_group", tag="y_group", bufs=2, align_bytes=64)
            bank = bank_tile(bank_no, [P, 2, P, 4], BF16)
            for i in range(2):
                cols = slice(256 * half + P * i, 256 * half + P * (i + 1))
                nc.tensor.matmul(
                    out=bank[:, i],
                    lhsT=ident_bf[:],
                    rhs=y_plane[g][:, :, cols].rearrange("p t r -> p r t"),
                    start=True,
                    stop=True,
                )
            turned["y", g, half] = bank

        def empty_y(g, half):
            nc.scalar.copy(
                out=y_group[g][:, 256 * half : 256 * (half + 1)].rearrange("p r t -> p (r t)"),
                in_=turned["y", g, half][:].rearrange("p i r t -> p (i r t)"),
            )

        def quantize_y(g):
            quantize(yc[g][:], ys[g][:], y_group[g][:].rearrange("p r t -> p (r t)"))

        def load_v():
            nc.sync.dma_start(
                out=v_tile[:].rearrange("p g n -> p (g n)").bitcast(I32).rearrange("p (g n) -> p g n", g=4),
                in_=v_words.bitcast(I32).rearrange("g p n -> p g n"),
            )
            vs_words = vs_tile[:].rearrange("p g n -> p (g n)").bitcast(I32).rearrange("p (g n) -> p g n", g=4)
            for quad in range(4):
                nc.sync.dma_start(
                    out=vs_words[32 * quad : 32 * quad + 4],
                    in_=v_scales.bitcast(I32)[:, 4 * quad : 4 * quad + 4, :].rearrange("g q n -> q g n"),
                )

        L0, L1, R0, R1, R2, R3 = ("l", 0), ("l", 1), ("r", 0), ("r", 1), ("r", 2), ("r", 3)

        def load_block(key):
            load_rows(key, 0, 2)
            load_rows(key, 2, 4)

        def warm_up(width, bank_no=3):
            bank = bank_tile(bank_no, [P, W])
            nc.tensor.matmul(out=bank[:, :width], lhsT=idle[:, :P], rhs=idle[:, :width], start=True, stop=True)

        load_rows(L0, 0, 1)
        load_block(R0)
        load_rows(L0, 1, 2)
        load_rows(L0, 2, 4)
        load_prior(0, 0, 2)
        load_rows(R2, 0, 2)
        load_prior(0, 2, 4)

        warm_up(512)
        rows(L0, 0, 4)
        warm_up(256)
        rows(R0, 0, 5)
        rows(R0, 1, 6)
        load_rows(R2, 2, 4)
        load_near(0, 0, 0, 2)
        quantize_left(0, 0, 1)
        warm_up(128)
        rows(R0, 2, 7)
        turn_rows(R0, 3, 4)
        load_rows(R1, 0, 2)
        load_near(0, 0, 2, 4)
        load_prior(1, 0, 2)
        load_prior(1, 2, 4)
        quantize_right(0, 0, 0, 1)
        quantize_right(0, 1, 0, 1)
        empty_rows(R0, 3, True)
        rows(L0, 1, 5)
        warm_up(128)
        for h in range(2):
            quantize_right(0, h, 1, 2)
        rows(L0, 2, 6)
        rows(L0, 3, 7)
        load_rows(R1, 2, 4)
        for t in range(1, 4):
            quantize_left(0, t, t + 1)
        for t in range(4):
            stage1(0, t)
        for n in range(4):
            rows(R2, n, 4 + n)
        load_rows(R3, 0, 2)
        load_prior(2)
        load_y(0)
        for t in range(4):
            add_prior(0, t)
        relu_near(0, 1, 0, 2)
        quantize_right(2, 0, 0, 1)
        quantize_right(2, 1, 0, 1)
        relu_near(0, 0, 0, 2)
        for h in range(2):
            quantize_right(2, h, 1, 2)
        warm_up(128, 0)
        rows(R1, 0, 4)
        rows(R1, 1, 5)
        relu_near(0, 1, 2, 4)
        for t in range(4):
            stage1(1, t)
        group_a(0, 1, "s")
        for n in (2, 3):
            rows(R1, n, 4 + n)
        load_rows(R3, 2, 4)
        load_near(0, 1)
        relu_near(0, 0, 2, 4)

        for k, ready, fresh in ((1, R1, R3), (2, R3, L1)):
            for t in range(4):
                add_prior(k, t)
            group_a(k - 1, 0, "g")
            turn_z(k - 1, 0, 4)
            turn_z(k - 1, 1, 5)
            empty_z(k - 1, 0)
            empty_z(k - 1, 1)
            if k == 1:
                warm_up(128, 0)
            else:
                weave_y(0, 0, 0)
                empty_y(0, 0)
            rows(fresh, 0, 6)
            rows(fresh, 1, 7)
            relu_near(k, 1, 0, 2)
            relu_near(k, 1, 2, 4)
            quantize_rows(ready, 0)
            quantize_rows(ready, 1)
            if k == 1:
                load_rows(L1, 0, 2)
                load_prior(3)
                load_rows(L1, 2, 4)
                load_v()
                load_y(1)
                load_prior(4)
                load_near(1, 0)
                for t in range(4):
                    widen_y(0, t)
            else:
                load_prior(5)
                load_near(1, 1)
                weave_y(0, 1, 4)
                empty_y(0, 1)
                group_a(1, 1, "s")
            for t in range(4):
                stage1(k + 1, t)
            rows(fresh, 2, 6)
            rows(fresh, 3, 7)
            quantize_b(k - 1)
            relu_near(k, 0)

        for t in range(4):
            add_prior(3, t)
        group_a(2, 0, "g")
        turn_z(2, 0, 4)
        turn_z(2, 1, 5)
        empty_z(2, 0)
        empty_z(2, 1)
        load_prior(6)
        for t in range(2):
            ligand(0, t, (0, 2), 6 + t)
        group_a(2, 1, "s")
        for t in range(4):
            widen_y(1, t)
        quantize_rows(L1, 0)
        relu_near(3, 1)
        quantize_rows(L1, 1)
        quantize_b(2)
        for t in range(4):
            stage1(4, t)
        for t in range(2):
            ligand(0, t, (1,))
        relu_near(3, 0)

        for t in range(4):
            add_prior(4, t)
        group_a(3, 0, "g")
        turn_z(3, 0, 4)
        turn_z(3, 1, 5)
        empty_z(3, 0)
        empty_z(3, 1)
        group_y(1, 0)
        group_y(1, 1)
        load_prior(7)
        for t in range(3):
            stage1(5, t)
        stage1_flipped(5, 3)
        empty_flipped(5, 3)
        quantize_y(0)
        quantize_b(3)
        relu_near(4, 1)
        for t in range(2):
            ligand(0, t, (3,))
        for t in range(2, 4):
            ligand(0, t, (0, 2, 1, 3), 2 + t)
        sum_on_tensor(5, 3)
        finish("l", 0, 0)
        finish("l", 0, 1)
        group_a(4, 1, "s")
        finish("l", 0, 2)
        finish("l", 0, 3)
        quantize_a(0)
        relu_near(4, 0)

        for t in range(3):
            add_prior(5, t)
        for u in (1, 0):
            relu_near(5, u, 3, 4, True)
        group_a(4, 0, "g")
        turn_z(4, 0, 6)
        turn_z(4, 1, 7)
        empty_z(4, 0)
        empty_z(4, 1)
        group_a(3, 1, "s")
        for t in range(3):
            stage1(6, t)
        stage1_flipped(6, 3)
        empty_flipped(6, 3)
        quantize_y(1)
        quantize_a(4)
        relu_near(5, 1, 0, 3)
        quantize_b(4)
        for j in range(4):
            receptor(0, j, (0, 1), (4, 5, 6, 7)[j])
        finish("r", 0, 0)
        finish("r", 0, 1)
        finish("r", 0, 2)
        finish("r", 0, 3)
        group_a(5, 1, "s")
        for t in range(2):
            ligand(1, t, (0,), 4 + t)
        sum_on_tensor(6, 3)
        quantize_a(1)
        relu_near(5, 0, 0, 3)

        for t in range(3):
            add_prior(6, t)
        for u in (1, 0):
            relu_near(6, u, 3, 4, True)
        group_a(5, 0, "g")
        turn_z(5, 0, 6)
        turn_z(5, 1, 7)
        empty_z(5, 0)
        empty_z(5, 1)
        relu_near(6, 1, 0, 3)
        group_a(6, 1, "s")
        for t in range(4):
            stage1(7, t)
        quantize_a(5)
        quantize_b(5)
        receptor(2, 0, (0, 1), 6)
        receptor(2, 1, (0, 1), 7)
        finish("r", 2, 0)
        finish("r", 2, 1)
        for t in range(2):
            ligand(1, t, (2,))
        receptor(2, 2, (0, 1), 6)
        receptor(2, 3, (0, 1), 7)
        finish("r", 2, 2)
        finish("r", 2, 3)
        quantize_a(2)
        quantize_a(6, 1, 2)
        relu_near(6, 0, 0, 3)

        k = LAST
        for t in range(4):
            add_prior(k, t)
        group_a(6, 0, "g")
        receptor(1, 2, (0, 1), 0)
        receptor(1, 3, (0, 1), 1)
        turn_z(6, 0, 6)
        turn_z(6, 1, 7)
        finish("r", 1, 2)
        finish("r", 1, 3)
        empty_z(6, 0)
        empty_z(6, 1)
        quantize_a(6, 0, 1)
        ligand(1, 2, (0, 2), 2)
        ligand(1, 3, (0, 2), 3)
        relu_near(k, 0)
        receptor(1, 0, (0, 1), 0)
        receptor(1, 1, (0, 1), 1)
        group_a(k, 0, "s")
        finish("r", 1, 0)
        finish("r", 1, 1)
        relu_near(k, 1, 0, 2)
        quantize_a(3, 0, 1)
        relu_near(k, 1, 2, 4)
        quantize_a(k, 0, 1)
        turn_z(k, 0, 6)
        turn_z(k, 1, 7)
        quantize_b(6)
        empty_z(k, 0)
        empty_z(k, 1)
        receptor(3, 0, (0, 1), 0)
        receptor(3, 1, (0, 1), 1)
        group_a(k, 1, "v")
        quantize_b(k, 0, 1)
        finish("r", 3, 0, False, True)
        finish("r", 3, 1, False, True)
        for t in range(2):
            ligand(1, t, (1,))
        for t in range(2):
            ligand(1, t, (3,))
        quantize_b(k, 1, 2)
        quantize_a(3, 1, 2)
        quantize_a(k, 1, 2)
        finish("l", 1, 0, True)
        finish("l", 1, 1, False, False, nc.scalar)
        for t in range(2, 4):
            ligand(1, t, (1, 3))
        receptor(3, 2, (0, 1), 6)
        receptor(3, 3, (0, 1), 7)
        finish("l", 1, 2, True)
        finish("l", 1, 3, False, False, nc.scalar)
        finish("r", 3, 2, True, True)
        finish("r", 3, 3, False, True, nc.scalar)
